import numpy as np, ml_dtypes
CORES = [16,17,18,19,32,33,34,35]
N = 8
import mx_ref
BF = ml_dtypes.bfloat16
def entries(a):
    return np.ascontiguousarray(a.T).reshape(-1)
def table(e):
    return np.ascontiguousarray(np.reshape(e, (-1, 16)).T).astype(np.int32)
def cols(t, e):
    v = np.concatenate([t.reshape(128, -1, 4), np.zeros((128, 1, 4), BF)], axis=1)
    return np.ascontiguousarray(v[:, e]).reshape(128, -1)
def f(rng, *shape):
    return mx_ref.flush((rng.standard_normal(shape, dtype=np.float32) * np.exp2(rng.integers(-2, 3, shape[:-1] + (1,)))).astype(BF))
def wide(rng, *shape, cols=0):
    v = rng.standard_normal(shape, dtype=np.float32) * np.exp2(rng.integers(-12, 13, shape)).astype(np.float32)
    if cols: v *= np.repeat(np.exp2(rng.integers(-cols, cols + 1, shape[:-2] + (1, shape[-1] // 4))) * (rng.random(shape[:-2] + (1, shape[-1] // 4)) > 0.0625), 4, axis=-1).astype(np.float32)
    return mx_ref.flush(v.astype(BF))
P, V, R, O, CAP, ALL = 256, 64, 4, 2, 14, 48
HOME = np.concatenate([np.repeat(np.arange(N), P), np.repeat(np.arange(N), V)])
def flat(a):
    return np.concatenate([entries(e) for e in a])
def game(alt, f1, f2):
    first, second = np.concatenate([np.arange(N * P), f1]), np.concatenate([alt, f2])
    stands = np.where(alt >= 0, np.arange(N * P), -1)
    k, leave, to, out = N * P + np.arange(N * V), np.repeat(np.arange(N), V), f1, []
    for t in range(R):
        was = stands[to]
        stands = np.array(stands); stands[to] = k
        out.append((k, leave, to, stands))
        k, at = was[was >= 0], to[was >= 0]
        leave, to = at // P, np.where(first[k] == at, second[k], first[k])
    return out
def draw(rng, lo, hi, aim):
    stands = np.full((N, P), -1)
    for r in range(N):
        p = rng.permutation(P)[:rng.integers(lo, hi + 1)]
        stands[r, p] = r * P + p
    if aim == "long":
        r = int(rng.integers(0, N)); stands[r] = r * P + np.arange(P)
    if aim == "short": stands[int(rng.integers(0, N))] = -1
    stands = stands.reshape(-1); start = stands >= 0
    first, second = np.concatenate([np.arange(N * P), np.full(N * V, -1)]), np.full(N * P + N * V, -1)
    came, total = np.zeros((N * P + N * V, N), bool), np.zeros((N, N), int)
    k, leave, at = N * P + np.arange(N * V), np.repeat(np.arange(N), V), np.full(N * V, -1)
    goal, last = int(rng.integers(0, N)), None
    mark, late = (goal + 1) % N, 0
    for t in range(R):
        used, free, to = np.zeros((N, N), int), np.ones(N * P, bool), np.full(len(k), -1)
        if aim == "long": mask = stands >= 0
        elif aim == "short" and t > 0: mask = stands < 0
        elif aim == "home" and t == 2: mask = np.isin(np.arange(N * P), last)
        elif aim == "peak": mask = np.arange(N * P) // P == goal
        else: mask = np.ones(N * P, bool)
        known = second[k] >= 0
        o = rng.permutation(len(k))
        if aim == "peak": o = np.concatenate([o[HOME[k[o]] == mark], o[HOME[k[o]] != mark]])
        for i in np.concatenate([o[known[o]], o[~known[o]]]):
            j, q, h = k[i], leave[i], HOME[k[i]]
            good = free & np.repeat((used[q] < CAP) & (came[j] | (total[h] < ALL) | (np.arange(N) == h)), P)
            if at[i] >= 0: good[at[i]] = False
            if known[i]:
                x = second[j] if first[j] == at[i] else first[j]
                if not good[x]: return None
            else:
                if (good & mask).any(): good = good & mask
                if not good.any(): return None
                x = rng.choice(np.flatnonzero(good))
                if t == 0: first[j] = x
                else: second[j] = x
            r = x // P
            to[i] = x; free[x] = False; used[q, r] += 1
            if r != h and not came[j, r]: total[h, r] += 1
            came[j, r] = True
        if aim == "long" and len(k) < N * V: return None
        if aim == "short" and ((t == 1 and len(k) == 0) or (t > 1 and len(k) > 0)): return None
        if aim == "home" and t == R - 1 and (to == k).sum() < N * V // 4: return None
        if aim == "peak" and t < 2 and (used[:, goal] < CAP).any(): return None
        if aim == "peak" and t >= 2: late = max(late, int(used[np.arange(N) != goal, goal].max()))
        was = stands[to]; stands[to] = k; last = to
        k, at = was[was >= 0], to[was >= 0]
        leave = at // P
    if aim == "peak" and (late < CAP - 4 or total[mark, goal] < ALL - 1): return None
    j = np.flatnonzero((second < 0) & np.concatenate([start, np.ones(N * V, bool)]))
    x = rng.integers(0, N * P - 1, len(j)); second[j] = x + (x >= first[j])
    return {"alt": np.stack([table(e) for e in second[:N * P].reshape(N, P)]), "f1": np.stack([table(e) for e in first[N * P:].reshape(N, V)]), "f2": np.stack([table(e) for e in second[N * P:].reshape(N, V)])}
def lists(rng, lo, hi, aim=None):
    for i in range(50):
        d = draw(rng, lo, hi, aim)
        if d is not None: return d
    raise RuntimeError("no draw in 50 tries")
def setup_inputs(rng):
    return {"c": f(rng, N, 128, 4 * P), "v": f(rng, N, 128, 4 * V), "w": f(rng, N, 128, 512 * R * O), **lists(rng, P // 2, 7 * P // 8)}
def setup_inputs_long(rng):
    return {**setup_inputs(rng), **lists(rng, 15 * P // 16, 31 * P // 32, "long")}
def setup_inputs_short(rng):
    return {**setup_inputs(rng), **lists(rng, P // 2, P // 2, "short")}
def setup_inputs_home(rng):
    return {**setup_inputs(rng), **lists(rng, 3 * P // 4, 3 * P // 4, "home")}
def setup_inputs_peak(rng):
    return {**setup_inputs(rng), **lists(rng, 7 * P // 8, 7 * P // 8, "peak")}
def setup_inputs_spread(rng):
    d = setup_inputs(rng); d["c"] = wide(rng, N, 128, 4 * P, cols=6); d["v"] = wide(rng, N, 128, 4 * V, cols=6); return d
def check_inputs(d):
    b = []
    alt, f1, f2 = flat(d["alt"]), flat(d["f1"]), flat(d["f2"])
    if alt.min() < -1 or alt.max() >= N * P or (alt == np.arange(N * P)).any(): b.append("alt")
    if f1.min() < 0 or f1.max() >= N * P: b.append("f1")
    if f2.min() < 0 or f2.max() >= N * P or (f1 == f2).any(): b.append("f2")
    if b: return b
    came = np.zeros((N * P + N * V, N), bool)
    for k, leave, to, stands in game(alt, f1, f2):
        if len(set(to.tolist())) != len(to): return b + ["two columns go to one place in one round"]
        n = np.zeros((N, N), int); np.add.at(n, (leave, to // P), 1)
        if n.max() > CAP: b.append("more than CAP columns from one rank to one rank in one round")
        came[k, to // P] = True
    for q in range(N):
        for r in range(N):
            if q != r and came[HOME == q, r].sum() > ALL: b.append("more than ALL columns of one rank come to another one")
    return b
def reference(c, v, w, alt, f1, f2):
    every = np.concatenate([c[r] for r in range(N)] + [v[r] for r in range(N)], axis=1)
    y = np.zeros((N, 128, R * O * P), np.float32)
    for t, (k, leave, to, stands) in enumerate(game(flat(alt), flat(f1), flat(f2))):
        for r in range(N):
            q = mx_ref.quantize(cols(every, stands[P * r:P * r + P]))
            for i in range(O * t, O * t + O):
                y[r][:, P * i:P * i + P] = mx_ref.matmul(mx_ref.quantize(w[r][:, 512 * i:512 * i + 512]), q)
    return {"y": y}

@@ -1,0 +1,471 @@
+from concourse.bass import DstId, RemoteDMATransfer
+from concourse.mybir import dt, AluOpType as A, ActivationFunctionType as F
+
+N, P, V, R, O = 8, 256, 64, 4, 2
+CH = N * V
+NP = N * P
+AD = 8
+IDS = P + V
+NO = NP + CH + 8
+S0 = 512
+Z = 32
+E0, E1 = 16, 48
+OWN = Z + IDS
+W1 = OWN + (N - 1) * E0
+WW = W1 + (N - 1) * E1
+IT = P + V
+K0, K1 = 64, 200
+C0, C1 = 7, 21
+W = {"0": 1, "1": 3}
+CC = {"0": C0, "1": C1}
+KK = {"0": K0, "1": K1}
+
+SCRATCH = {"lists": ("dram", [8, 128, 4], "float32"), "hbd": ("dram", [128, 4], "int32"), "idd": ("dram", [64, 4], "float32"),
+           "acc": ("psum", [128, 4096], "float32")}
+POOL = {}
+
+
+def _sb(dtype, **cols):
+    for k in cols:
+        SCRATCH[k] = ("sbuf", [128, cols[k]], dtype)
+        POOL[k] = (k, 0, cols[k])
+
+
+def _pool(buf, dtype, **cols):
+    a = 0
+    for k in cols:
+        POOL[k] = (buf, a, cols[k])
+        a += cols[k]
+    SCRATCH[buf] = ("sbuf", [128, a], dtype)
+
+
+_sb("int32", src=4, shh=4, pi=1, row1=V, hb1=V, row0=IT, dd=32, gli=20)
+_sb("float32", sv=4, k4=4, idc=4, idf=4, jm=16, gm0=CH, gm1=CH, gm2=CH, tr=CH, f1f=32, v1=CH, v2=CH, xt=3 * NP, yt=NP, a0=IT,
+    x1s=P, x2s=P, x3s=P, ei=IT, gg=IT, pf=IT, qq=IT, tq=IT, ts=IT, val=160, val0=32, vp0=32, vm0=32, pl0=208,
+    pl1=560, la0=C0, lb0=C0, ma0=C0, mb0=C0, la1=C1, lb1=C1, ma1=C1, mb1=C1, slot=S0 + NO + 8, sl0=(N - 1) * E0,
+    sl1=(N - 1) * E1, idw=64, gs=4 * P, gsc=4 * P, ys=2048, dcol=1, b16=1, b48=1)
+_sb("uint16", of1=32, ofq=32, ofz=32, ofw=32, gl=20, ofp=10, ofp0=2, pk0u=C0, pk1u=C1, mt0u=C0, mt1u=C1, meta0=C0, meta1=C1, idu=64,
+    so=64)
+_sb("bfloat16", cv=4 * OWN, wt=4096, ones=IT, k32=IT, md=IT, md1=V, mask=CH, keep=CH)
+_sb("float8_e4m3fn_x4", wq=1024, qo=OWN, sn0=112, sn1=336, fw=WW, pk0=P, pk1=P, pk2=P, pk3=P)
+_sb("uint8", wqs=1024, qos=OWN, sn0s=112, sn1s=336, fws=WW, ps0=P, ps1=P, ps2=P, ps3=P)
+_pool("tf", "float32", sa=4, sb=4, sc=4, s1=4, s2=4, em=4, pmf=1, px0=C0, px1=C1, mt0=C0, mt1=C1)
+_pool("ti", "int32", sy=4, pm=1, lo=10, hi=10, l2=10, sm2=10, mx2=10)
+SEMAPHORES = ["vv", "aa", "pp", "gq", "lsent", "aL", "aM0", "aC0", "aS0", "aM1", "aC1", "aS1", "dsrc", "drow", "dhb", "dhd", "did",
+              "demp", "dcv", "dw0", "dw1", "dfw", "down", "dfan", "df1", "dv1", "dpl0", "dpl1", "dpm0", "dpm1", "di0", "di1", "di2",
+              "di3", "dy"]
+
+
+def rank_program(g, core, T, topo):
+    me = T.rank_of(core)
+    if me is None:
+        return
+    cores = T.cores
+    others = [d for d in range(N) if d != me]
+    OB = P * me
+    VB = NP + V * me
+    q = {"v": g.vector, "a": g.scalar, "p": g.tensor, "g": g, "y": g.sync}
+    csem = {"v": "vv", "a": "aa", "p": "pp", "g": "gq"}
+    cnt = {"v": 0, "a": 0, "p": 0, "g": 0}
+    known, wr, rd, pre = {}, {}, {}, {}
+
+    def b(name, r0=0, r1=128, c0=0, c1=None):
+        buf, a, w = POOL[name]
+        return T[buf][r0:r1, a + c0:a + (w if c1 is None else c1)]
+
+    def need(e, toks):
+        best = {}
+        for s, n in toks:
+            best[s] = max(best.get(s, 0), n)
+        for s in sorted(best):
+            if known.get((e, s), 0) < best[s]:
+                q[e].wait_ge(T.sem[s], best[s])
+                known[(e, s)] = best[s]
+
+    def op(e, fn, reads, writes, *args, **kw):
+        toks = []
+        for k in reads:
+            toks += wr.get(k, [])
+        for k in writes:
+            toks += wr.get(k, []) + rd.get(k, [])
+        need(e, toks)
+        cnt[e] += 1
+        fn(*args, **kw).then_inc(T.sem[csem[e]], 1)
+        tok = (csem[e], cnt[e])
+        for k in reads:
+            rd.setdefault(k, []).append(tok)
+        for k in writes:
+            wr[k], rd[k] = [tok], []
+
+    def dma(e, sem, total, reads, writes, out, in_):
+        tok, toks = (sem, total), []
+        for k in writes:
+            if wr.get(k) != [tok]:
+                pre[(sem, k)] = wr.get(k, []) + rd.get(k, [])
+                wr[k], rd[k] = [tok], []
+            toks += pre[(sem, k)]
+        for k in reads:
+            toks += wr.get(k, [])
+        need(e, toks)
+        q[e].dma_start(out, in_).then_inc(T.sem[sem], 16)
+        for k in reads:
+            rd.setdefault(k, []).append(tok)
+
+    def copy(reads, writes, out, in_, e="v", plus=None):
+        if e == "v":
+            op("v", g.vector.tensor_copy, reads, writes, out, in_)
+        elif plus is None:
+            op("a", g.scalar.activation, reads, writes, out, in_, F.Copy)
+        else:
+            op("a", g.scalar.activation, reads, writes, out, in_, F.Identity, bias=float(plus))
+
+    def tsc(reads, writes, out, in0, s1, op0, s2=None, op1=None):
+        if op1 is None:
+            op("v", g.vector.tensor_scalar, reads, writes, out, in0, s1, None, op0)
+        else:
+            op("v", g.vector.tensor_scalar, reads, writes, out, in0, s1, s2, op0, op1)
+
+    def tt(reads, writes, out, in0, in1, o):
+        op("v", g.vector.tensor_tensor, reads, writes, out, in0, in1, o)
+
+    def tb(out, in0, in1, o):
+        tt([in0, in1], [out], b(out), b(in0), b(in1), o)
+
+    def sb(out, in0, s1, op0, s2=None, op1=None):
+        tsc([in0], [out], b(out), b(in0), s1, op0, s2, op1)
+
+    def scan(reads, writes, out, d0, d1, initial):
+        op("v", g.vector.tensor_tensor_scan, reads, writes, out, d0, d1, initial, A.mult, A.add)
+
+    def fill(key, ap, c):
+        op("v", g.vector.memset, [], [key], ap, c)
+
+    def iota(key, out, pattern, base, mult, f=True):
+        kw = {"allow_small_or_imprecise_dtypes": True} if f else {}
+        op("g", g.iota, [], [key], out, pattern, base, mult, **kw)
+
+    def engines(a, c):
+        off = [k for k in cores if k != a and topo.chip(k) != topo.chip(a)]
+        on = [k for k in cores if k != a and topo.chip(k) == topo.chip(a)]
+        far = topo.engines(a, off[0])
+        if c in off:
+            n, k = len(far) // len(off), off.index(c)
+            return far[n * k:n * k + n]
+        near = [x for x in topo.engines(a, c) if x not in far]
+        k = on.index(c)
+        return near[2 * k:2 * k + 2]
+
+    sent = [0]
+
+    def spread(sem, piece):
+        ts = []
+        for d in others:
+            src, dst = piece(d)
+            rid, pid = topo.addr(cores[d])[0:2]
+            m = 0
+            for x in engines(core, cores[d]):
+                m |= 1 << x
+                sent[0] += 1
+            ts.append(RemoteDMATransfer(dst_ids=[DstId(rid=rid, pnc=pid)], dma_engine_mask=m, remote_sem=T.sem[sem], src=src, dst=dst))
+        g.remote_dma_fused(ts, local_sem=T.sem.lsent)
+
+    def arrive(sem, key):
+        wr[key] = [(sem, sum(len(engines(cores[s], core)) for s in others))]
+
+    def at(s, d):
+        return s if s < d else s - 1
+
+    def load_w(e, h):
+        dma(e, "dw%d" % h, 16, [], ["wt%d" % h], T.wt[:, 2048 * h:2048 * h + 2048], T.w[:, 2048 * h:2048 * h + 2048])
+
+    def pack(h):
+        w = slice(512 * h, 512 * h + 512)
+        op("v", g.vector.quantize_mx, ["wt%d" % h], ["wq%d" % h], T.wq[:, w], T.wqs[:, w], T.wt[:, 2048 * h:2048 * h + 2048])
+
+    dma("y", "dsrc", 224, [], ["src"], T.src[0:64, :], T.alt[:, :])
+    for c in range(4):
+        dma("a", "dsrc", 224, [], ["src"], T.src[64:80, c:c + 1], T.f1[4 * c:4 * c + 4, :])
+    dma("y", "dsrc", 224, [], ["src"], T.src[96:112, :], T.f2[:, :])
+    for c in range(4):
+        x = c + 1 - 2 * (c % 2)
+        dma("a", "dsrc", 224, [], ["src"], T.src[80:96, c:c + 1], T.f1[4 * x:4 * x + 4, :])
+        dma("y", "dsrc", 224, [], ["src"], T.src[112 + 4 * c:116 + 4 * c, :], T.f2[4 * x:4 * x + 4, :])
+    for p in range(N):
+        dma("ya"[p % 2], "drow", 16 * N, [], ["row1"], T.row1[p:p + 1, :], T.f1[:, :])
+    dma("y", "dcv", 32, [], ["cv.c"], T.cv[:, 4 * Z:4 * (Z + P)], T.c[:, :])
+    dma("y", "dcv", 32, [], ["cv.c"], T.cv[:, 4 * (Z + P):4 * OWN], T.v[:, :])
+
+    def begin(nm, e, k):
+        iota(nm, b(nm), [[1, 1]], 16 * k - 1 - e, e)
+        iota(nm, b(nm, 0, me + 1), [[1, 1]], 16 * k - 1, e)
+
+    iota("k4", b("k4"), [[1, 4]], NP + OB, 4)
+    iota("dd", b("dd"), [[16, 32]], 0, 1, False)
+    iota("yt", T.yt[:, 0:256], [[1, 256]], 0, 0)
+    iota("idc", b("idc"), [[1, 4]], OB, 4)
+    fill("pl0", b("pl0", 0, 32, K0, K0 + 16 * C0), 0.0)
+    iota("pl0", b("pl0", 0, 16, K0, K0 + 16 * C0), [[1, 16], [0, N - 1]], E0 * me, 0)
+    iota("dcol", b("dcol"), [[1, 1]], 0, 1)
+    iota("dcol", b("dcol", 0, me + 1), [[1, 1]], 99, 0)
+    if me:
+        iota("dcol", b("dcol", 0, me), [[1, 1]], 0, 1)
+    begin("b16", E0, K0)
+    iota("vp0", b("vp0"), [[8, 2], [1, 4], [16, 4]], Z + P, 0)
+    iota("vm0", b("vm0"), [[32, 2], [1, 16]], S0 + VB, 0)
+    fill("ones", b("ones"), 1.0)
+    fill("k32", b("k32"), 1.0)
+    fill("k32", T.k32[:, 0:IT:32], 0.0)
+    fill("md", T.md[0:32, :], 0.0)
+    fill("md1", T.md1[0:32, :], 0.0)
+    fill("val0", b("val0"), 0.0)
+    fill("slot.z", T.slot[:, S0 + NO:S0 + NO + 8], 0.0)
+    fill("cv.z", T.cv[:, 0:4 * Z], 0.0)
+    fill("keep", T.keep[:, 0:16], 1.0)
+    fill("keep", T.keep[:, 0:1], 0.0)
+    for nm in ("of1", "ofq", "ofz", "ofw"):
+        copy(["dd"], [nm], b(nm), b("dd"))
+    copy(["dd"], ["ofp0"], b("ofp0"), T.dd[:, 0:2])
+    copy(["dd"], ["ofp"], b("ofp"), T.dd[:, 0:10])
+
+    sb("sy", "src", 4, A.arith_shift_right)
+    sb("shh", "src", 8, A.arith_shift_right, 4095, A.bitwise_and)
+    sb("sa", "src", 16.0, A.mult)
+    sb("sb", "sy", -255.0, A.mult)
+    sb("sc", "shh", 240.0, A.mult)
+    tb("s1", "sa", "sb", A.add)
+    tb("s2", "s1", "sc", A.add)
+    tb("sv", "s2", "k4", A.min)
+    need("g", wr["sv"])
+    spread("aL", lambda d: (b("sv"), T.lists[me]))
+    tsc(["src"], ["em"], b("em"), b("src"), 0.0, A.is_lt, float(NO), A.mult)
+    tb("idf", "em", "idc", A.max)
+    dma("y", "dhd", 16, ["shh"], ["hbd"], T.hbd[:, :], b("shh"))
+    dma("y", "down", 16, ["sv"], ["lown"], T.lists[me], b("sv"))
+    dma("y", "did", 16, ["idf"], ["idd"], T.idd[:, :], T.idf[0:64, :])
+    for p in range(N):
+        dma("y", "dhb", 32 * N, ["hbd"], ["row0"], T.row0[p:p + 1, 0:P], T.hbd[0:64, :])
+        dma("y", "dhb", 32 * N, ["hbd"], ["row0"], T.row0[p:p + 1, P:IT], T.hbd[96:112, :])
+
+    for n in (256, 512, 1024):
+        copy(["yt"], ["yt"], T.yt[:, n:2 * n], T.yt[:, 0:n], "a", n)
+    copy(["yt"], ["xt"], T.xt[:, 0:NP], T.yt[:, :], "a")
+    wr["xf"] = wr["xt"]
+    copy(["yt"], ["v1"], b("v1"), T.yt[:, 0:CH], "a", NP)
+
+    iota("jm", b("jm"), [[1, 16]], 0, 0)
+    iota("pi", b("pi"), [[1, 1]], 0, 1, False)
+    iota("gli", b("gli"), [[16, 20]], 0, 1, False)
+    iota("gli", b("gli", 0, 16), [[16, 20]], OB, 1, False)
+    begin("b48", E1, K1)
+    for k, rm, rw in ((1, 128, 24), (0, 16, 8)):
+        iota("val.c", b("val", 0, rm, 0, 128), [[32, 8], [1, 16]], S0 + OB + 16 * k, 0)
+        iota("val.c", b("val", 0, rw, 0, 128), [[2, 8], [16, 16]], Z + k, 0)
+        iota("val.v", b("val", 0, rm, 128, 160), [[32, 2], [1, 16]], S0 + VB + 16 * k, 0)
+        iota("val.v", b("val", 0, rw, 128, 160), [[8, 2], [1, 4], [16, 4]], Z + P + 4 * k, 0)
+
+    def compact(n, marks, key, base, width, of, val, vkeys, pl):
+        k = n // 32
+
+        def s(name, w=k):
+            return b(name, 0, 32, 0, w)
+        scan(["ones", base, key], ["pf"], s("pf", n), s("ones", n), marks, b(base, 0, 32))
+        tt(["pf", key], ["qq"], s("qq", n), s("pf", n), marks, A.mult)
+        op("v", g.vector.transpose, ["qq"], ["tq"], s("tq", n), s("qq", n))
+        scan(["tq", "k32"], ["ts"], s("ts", n), s("k32", n), s("tq", n), 0.0)
+        u = T.ts[0:32, 31:n:32]
+        tsc(["ts"], ["hi"], s("hi"), u, 1.0 / 16, A.mult, -0.46875, A.add)
+        tsc(["ts"], ["lo"], s("lo"), u, float(width), A.mult)
+        tsc(["hi"], ["l2"], s("l2"), s("hi"), 1.0 - 16.0 * width, A.mult)
+        tt(["l2", "lo"], ["sm2"], s("sm2"), s("l2"), s("lo"), A.add)
+        tt(["sm2", "dd"], ["mx2"], s("mx2"), s("sm2"), s("dd"), A.max)
+        copy(["mx2"], [of], s(of), s("mx2"))
+        copy([of] + vkeys, [pl], T[pl][:, :].indirect(T[of][:, 0:k]), T[val][:, :])
+
+    def wrap(k):
+        c, a = CC[k], KK[k]
+        both = [("dpm", 8, ("ma", "mb")), ("dpl", 0, ("la", "lb"))]
+        for sem, r, nms in both if k == "1" else both[::-1]:
+            for i, nm in enumerate(nms):
+                dma("y", sem + k, 32, ["pl" + k], [nm + k], b(nm + k), T["pl" + k][16 * i + r:16 * i + r + 8, a:a + 16 * c])
+
+    for r1, nm, plus in ((32, "vm0", 16), (24, "vp0", 4), (16, "vm0", 0), (8, "vp0", 0)):
+        tsc([nm], ["val0"], b("val0", 0, r1), b(nm, 0, r1), float(plus), A.add)
+    fill("pl0", b("pl0", 0, 8, K0, K0 + 16 * C0), 0.0)
+    tsc(["row1"], ["hb1"], T.hb1[0:N, :], T.row1[0:N, :], 8, A.arith_shift_right)
+    tsc(["hb1", "dcol"], ["md1"], T.md1[0:N, :], T.hb1[0:N, :], b("dcol", 0, N), A.is_equal)
+    compact(V, T.md1[0:32, :], "md1", "b16", C0, "ofp0", "val0", ["val0"], "pl0")
+    wrap("0")
+    for p in range(N):
+        dma("y", "demp", 16 * N, ["idd", "xf"], ["xo"], T.xt[p:p + 1, OB:OB + P], T.idd[:, :])
+    op("v", g.vector.quantize_mx, ["cv.z", "cv.c"], ["qo.own"], T.qo[:, 0:OWN], T.qos[:, 0:OWN], T.cv[:, :])
+    copy(["gli"], ["gl"], T.gl[:, 0:16], T.gli[:, 0:16])
+    sb("pm", "pi", 15, A.bitwise_and)
+    copy(["pm"], ["pmf"], b("pmf"), b("pm"))
+    tsc(["jm", "pmf"], ["mask"], T.mask[:, 0:16], b("jm"), b("pmf"), A.is_equal)
+    tsc(["row0", "dcol"], ["md"], T.md[0:N, :], T.row0[0:N, :], b("dcol", 0, N), A.is_equal)
+
+    arrive("aL", "lfar")
+    for r in range(N):
+        dma("y", "df1", 128, ["lfar", "lown"], ["f1f"], T.f1f[0:32, 4 * r:4 * r + 4], T.lists[r, 64:96, :])
+    for h in range(2):
+        p = 16 * h + AD
+        dma("a", "dfan", 32, ["lfar", "lown"], ["xt"], T.xt[p:p + 1, 0:NP], T.lists[:, 0:64, :])
+    for h in range(2):
+        p = 16 * h + AD
+        dma("a", "dv1", 32, ["lfar", "lown"], ["v1"], T.v1[p:p + 1, :], T.lists[:, 96 + 16 * h:112 + 16 * h, :])
+    load_w("y", 0)
+    load_w("y", 1)
+    dma("y", "dfw", 32, ["qo.own"], ["fw.own"], T.fw[:, 0:OWN].bitcast(dt.uint8), T.qo[:, 0:OWN].bitcast(dt.uint8))
+    dma("y", "dfw", 32, ["qo.own"], ["fw.own"], T.fws[:, 0:OWN], T.qos[:, 0:OWN])
+    copy(["yt"], ["x1"], T.xt[:, NP:2 * NP], T.yt[:, :], "a", 2 * NP)
+
+    def look(table, keys, of, ok, gm, gk, n):
+        tt(keys + [ok, "mask"], [gk], gm, table.indirect(of), T.mask[:, 0:n], A.mult)
+
+    X = ["xt", "x1", "x2"]
+
+    def step(t, of, gm):
+        copy(X[0:t + 1] + ["xo", of], [gm], b(gm), T.xt[:, 0:NP * (t + 1)].indirect(b(of)))
+
+    def turn(gm, of):
+        op("v", g.vector.transpose, [gm], ["tr"], T.tr[0:32, :], T[gm][0:32, :])
+        copy(["tr"], [of], b(of, 0, 32), T.tr[0:32, AD:CH:16])
+
+    def put(t, of, val):
+        copy([of, val], X[0:t + 1], T.xt[:, 0:NP * (t + 1)].indirect(b(of)), b(val))
+
+    def picks(k):
+        la, lb, ma, mb, pku, dst, px, mt = [x + k for x in ("la", "lb", "ma", "mb", "pk", "sn", "px", "mt")]
+        pku, dss, mtu = pku + "u", dst + "s", mt + "u"
+
+        def slots_of():
+            tb(mt, ma, mb, A.max)
+            copy([mt], [mtu], b(mtu), b(mt))
+        if k == "1":
+            slots_of()
+        tb(px, la, lb, A.max)
+        copy([px], [pku], b(pku), b(px))
+        copy(["qo.own", pku], [dst], b(dst).bitcast(dt.uint32), b("qo").bitcast(dt.uint32).indirect(b(pku)))
+        copy(["qo.own", pku], [dss], b(dss), b("qos").indirect(b(pku)), "a")
+        if k == "0":
+            slots_of()
+
+    def send(k, first, e):
+        mtu, meta, dst, dss, w = "mt" + k + "u", "meta" + k, "sn" + k, "sn" + k + "s", W[k]
+        need("g", wr[mtu])
+        spread("aM" + k, lambda d: (T[mtu][:, w * at(d, me):w * at(d, me) + w], T[meta][:, w * at(me, d):w * at(me, d) + w]))
+        need("g", wr[dst])
+        spread("aC" + k, lambda d: (T[dst][:, e * at(d, me):e * at(d, me) + e].bitcast(dt.uint8),
+                                    T.fw[:, first + e * at(me, d):first + e * at(me, d) + e].bitcast(dt.uint8)))
+        need("g", wr[dss])
+        spread("aS" + k, lambda d: (T[dss][:, e * at(d, me):e * at(d, me) + e],
+                                    T.fws[:, first + e * at(me, d):first + e * at(me, d) + e]))
+        arrive("aM" + k, meta)
+        arrive("aC" + k, "fw" + k)
+        arrive("aS" + k, "fws" + k)
+
+    picks("0")
+    copy(["f1f"], ["of1"], b("of1", 0, 32), b("f1f", 0, 32))
+    copy(["yt", "of1"], ["v2"], b("v2"), b("yt").indirect(b("of1")), "a")
+    step(0, "of1", "gm0")
+    need("g", wr["of1"])
+    send("0", OWN, E0)
+    iota("a0", b("a0", 0, 128, 0, P), [[1, P]], OB, 0)
+    iota("a0.v", b("a0", 0, 128, P, IT), [[1, V]], VB, 0)
+    iota("pl1", b("pl1", 0, 32, K1, K1 + 16 * C1), [[0, 16 * C1]], 0, 0)
+    iota("pl1", b("pl1", 0, 16, K1, K1 + 16 * C1), [[1, 16], [0, N - 1], [16, 3]], E1 * me, 0)
+    iota("pl1", b("pl1", 0, 8, K1, K1 + 16 * C1), [[0, 16 * C1]], 0, 0)
+    iota("slot.own", b("slot", 0, 128, S0 + OB, S0 + OB + P), [[1, 16], [16, 16]], Z, 0)
+    iota("slot.own", b("slot", 0, 128, S0 + VB, S0 + VB + V), [[1, 16], [16, 4]], Z + P, 0)
+    iota("sl0", b("sl0"), [[1, (N - 1) * E0]], OWN, 0)
+    iota("sl1", b("sl1"), [[1, (N - 1) * E1]], W1, 0)
+
+    OX = T.xt[0:16, OB:OB + P]
+    put(0, "of1", "v1")
+    copy(["xt"], ["x1s"], T.x1s[0:16, :], OX, "a")
+    copy(["yt"], ["x2"], T.xt[:, 2 * NP:3 * NP], T.yt[:, :], "a", 2 * NP)
+    turn("gm0", "ofq")
+    step(1, "ofq", "gm1")
+    put(1, "ofq", "v2")
+    copy(["xt"], ["x2s"], T.x2s[0:16, :], OX, "a")
+    turn("gm1", "ofz")
+    step(2, "ofz", "gm2")
+    copy(["of1"], ["gl.v"], T.gl[:, 16:20], T.of1[:, 4 * me:4 * me + 4])
+    put(2, "ofz", "gm1")
+
+    tt(["xt", "gl", "gl.v", "a0", "a0.v"], ["ei"], b("ei"), T.xt[:, 0:NP].indirect(b("gl")), b("a0"), A.not_equal)
+    tt(["ei", "md"], ["gg"], T.gg[0:32, :], T.ei[0:32, :], T.md[0:32, :], A.mult)
+    compact(IT, T.gg[0:32, :], "gg", "b48", C1, "ofp", "val", ["val.c", "val.v"], "pl1")
+    for t, nm in enumerate(("x1s", "x2s")):
+        dma("y", "di%d" % t, 16, [nm], ["idw%d" % t], T.idw[:, 16 * t:16 * t + 16], T[nm][0:8, :])
+    wrap("1")
+    copy(["xt"], ["x3s"], T.x3s[0:16, :], OX, "a")
+    dma("y", "di2", 16, ["x3s"], ["idw2"], T.idw[:, 32:48], T.x3s[0:8, :])
+    for nm in ("mask", "keep"):
+        n = 16
+        while n < CH:
+            copy([nm], [nm], T[nm][:, n:2 * n], T[nm][:, 0:n], "a")
+            n *= 2
+
+    def fill_slots(k):
+        copy(["meta" + k, "sl" + k], ["slot", "slot.own", "slot.z"],
+             b("slot").indirect(T["meta" + k][:, 0:W[k] * (N - 1)]), b("sl" + k))
+
+    def slots(keys, c0, c1):
+        tsc(keys, ["idu%d" % t for t in range(c0, c1, 16)], T.idu[:, c0:c1], T.idw[:, c0:c1], float(S0), A.add)
+
+    def stand(c0, c1):
+        gk, w, n = "gs%d" % c0, slice(16 * c0, 16 * c1), 16 * (c1 - c0)
+        look(b("slot"), ["slot", "slot.own", "slot.z"], T.idu[:, c0:c1], "idu%d" % c0, T.gs[:, w], gk, n)
+        scan([gk, "keep"], [gk + "c"], T.gsc[:, w], T.keep[:, 0:n], T.gs[:, w], 0.0)
+        op("v", g.vector.tensor_copy, [gk + "c"], ["so%d" % t for t in range(c0 // 16, c1 // 16)], T.so[:, c0:c1],
+           T.gsc[:, 16 * c0 + 15:16 * c1:16])
+
+    def place(t):
+        copy(["fw.own", "so%d" % t] + ["fw%d" % k for k in range(min(t, 1) + 1)], ["pk%d" % t], b("pk%d" % t).bitcast(dt.uint32),
+             T.fw[:, 0:WW if t else W1].bitcast(dt.uint32).indirect(T.so[:, 16 * t:16 * t + 16]))
+
+    def products(t):
+        pk, ps = "pk%d" % t, "ps%d" % t
+        copy(["fw.own", "so%d" % t] + ["fws%d" % k for k in range(min(t, 1) + 1)], [ps], b(ps),
+             T.fws[:, 0:WW if t else W1].indirect(T.so[:, 16 * t:16 * t + 16]), "a")
+        for i in range(O * t, O * t + O):
+            w = slice(128 * i, 128 * i + 128)
+            op("p", g.tensor.matmul_mx, ["wq%d" % (i // 4), pk, ps], ["acc%d" % i], T.acc[:, 512 * i:512 * i + P],
+               T.wq[:, w], T.wqs[:, w], b(pk), b(ps), True, True)
+
+    def out(t, es):
+        for o in range(O):
+            i = O * t + o
+            w = slice(P * i, P * i + P)
+            copy(["acc%d" % i], ["ys%d" % i], T.ys[:, w], T.acc[:, 512 * i:512 * i + P], es[o])
+            dma("y", "dy", 16 * R * O, ["ys%d" % i], ["y%d" % i], T.y[:, w], T.ys[:, w])
+
+    turn("gm2", "ofw")
+    put(2, "ofw", "gm2")
+    picks("1")
+    send("1", W1, E1)
+    dma("y", "di3", 16, ["xt"], ["idw3"], T.idw[:, 48:64], T.xt[0:8, OB:OB + P])
+    slots(["idw0", "idw1", "idw2"], 0, 48)
+    fill_slots("0")
+    stand(0, 16)
+    place(0)
+    pack(0)
+    products(0)
+    out(0, "aa")
+    fill_slots("1")
+    slots(["idw3"], 48, 64)
+    stand(16, 48)
+    place(1)
+    products(1)
+    place(2)
+    pack(1)
+    products(2)
+    out(1, "aa")
+    stand(48, 64)
+    place(3)
+    products(3)
+    out(2, "va")
+    out(3, "va")
+    need("y", [("dy", 16 * R * O)])
+    need("g", [("lsent", sent[0])])

@@ -1,27 +1,23 @@
 from concourse.bass import DstId, RemoteDMATransfer
-from concourse.mybir import dt, AluOpType as A, ActivationFunctionType as F
+from concourse.mybir import dt, AluOpType as A, ActivationFunctionType as F, AxisListType as AX
 
 N, P, V, R, O = 8, 256, 64, 4, 2
 CH = N * V
 NP = N * P
-AD = 8
-IDS = P + V
-NO = NP + CH + 8
-S0 = 512
-Z = 32
-E0, E1 = 16, 48
-OWN = Z + IDS
-W1 = OWN + (N - 1) * E0
-WW = W1 + (N - 1) * E1
+AD, AY = 15, 14
+E = 48
 IT = P + V
-K0, K1 = 64, 200
-C0, C1 = 7, 21
-W = {"0": 1, "1": 3}
-CC = {"0": C0, "1": C1}
-KK = {"0": K0, "1": K1}
+NI = IT + V + E
+SI = IT + E
+NO = N * SI
+ZC = NI - 8
+TAG = 4096
+LC = 25
+MC = 26
+WW = NI + (N - 1) * E
+BIG = 1.0e9
 
-SCRATCH = {"lists": ("dram", [8, 128, 4], "float32"), "hbd": ("dram", [128, 4], "int32"), "idd": ("dram", [64, 4], "float32"),
-           "acc": ("psum", [128, 4096], "float32")}
+SCRATCH = {"lists": ("dram", [8, 128, 4], "float32"), "acc": ("psum", [128, 4096], "float32")}
 POOL = {}
 
 
@@ -39,21 +35,18 @@ def _pool(buf, dtype, **cols):
     SCRATCH[buf] = ("sbuf", [128, a], dtype)
 
 
-_sb("int32", src=4, shh=4, pi=1, row1=V, hb1=V, row0=IT, dd=32, gli=20)
-_sb("float32", sv=4, k4=4, idc=4, idf=4, jm=16, gm0=CH, gm1=CH, gm2=CH, tr=CH, f1f=32, v1=CH, v2=CH, xt=3 * NP, yt=NP, a0=IT,
-    x1s=P, x2s=P, x3s=P, ei=IT, gg=IT, pf=IT, qq=IT, tq=IT, ts=IT, val=160, val0=32, vp0=32, vm0=32, pl0=208,
-    pl1=560, la0=C0, lb0=C0, ma0=C0, mb0=C0, la1=C1, lb1=C1, ma1=C1, mb1=C1, slot=S0 + NO + 8, sl0=(N - 1) * E0,
-    sl1=(N - 1) * E1, idw=64, gs=4 * P, gsc=4 * P, ys=2048, dcol=1, b16=1, b48=1)
-_sb("uint16", of1=32, ofq=32, ofz=32, ofw=32, gl=20, ofp=10, ofp0=2, pk0u=C0, pk1u=C1, mt0u=C0, mt1u=C1, meta0=C0, meta1=C1, idu=64,
-    so=64)
-_sb("bfloat16", cv=4 * OWN, wt=4096, ones=IT, k32=IT, md=IT, md1=V, mask=CH, keep=CH)
-_sb("float8_e4m3fn_x4", wq=1024, qo=OWN, sn0=112, sn1=336, fw=WW, pk0=P, pk1=P, pk2=P, pk3=P)
-_sb("uint8", wqs=1024, qos=OWN, sn0s=112, sn1s=336, fws=WW, ps0=P, ps1=P, ps2=P, ps3=P)
-_pool("tf", "float32", sa=4, sb=4, sc=4, s1=4, s2=4, em=4, pmf=1, px0=C0, px1=C1, mt0=C0, mt1=C1)
-_pool("ti", "int32", sy=4, pm=1, lo=10, hi=10, l2=10, sm2=10, mx2=10)
-SEMAPHORES = ["vv", "aa", "pp", "gq", "lsent", "aL", "aM0", "aC0", "aS0", "aM1", "aC1", "aS1", "dsrc", "drow", "dhb", "dhd", "did",
-              "demp", "dcv", "dw0", "dw1", "dfw", "down", "dfan", "df1", "dv1", "dpl0", "dpl1", "dpm0", "dpm1", "di0", "di1", "di2",
-              "di3", "dy"]
+_sb("int32", src=28, ale=8, pi=1, dd=32, gli=16)
+_sb("float32", sv=8, k4=8, jm=16, g0=CH, g1=CH, g2=CH, tr=CH, f1f=32, v1=CH, xt=2 * NP, yt=NP, xs=3 * P, th=IT, thr=48, kk=64, kt=64,
+    cnt=32, ct=32, fl=2 * MC, slot=NO + 8, sl=(N - 1) * E, idw=8, gs=P, gt=P, ys=2048)
+_sb("uint16", of1=32, ofq=32, ofz=32, ofw=32, gl=20, ow=24, pm=2 * MC, meta=3 * (N - 1), idu=16, sf=16, so=64)
+_sb("bfloat16", cv=4 * NI, wt=4096, ones=NI, mk=NI, pf=NI, ja=NI, jv=NI)
+_sb("float8_e4m3fn_x4", wq=1024, qo=NI, sn=16 * LC, fw=WW, pk0=P, pk1=P, pk2=P, pk3=P)
+_sb("uint8", wqs=1024, qos=NI, sns=16 * LC, fws=WW, ps0=P, ps1=P, ps2=P, ps3=P)
+_pool("tf", "float32", s1=8, s2=8, s3=8, m14=1, bc1=1, bc2=1, bc4=1, tag=1, bi=1, bi2=1, thc=1, ne=16, uu=4, emw=8, tm=MC, i2=MC,
+      m2=32, d2=32, t3=32)
+_pool("ti", "int32", b1=8, b2=8, b3=8, p15=1, p3=1, rk=24, eq=4, e15=4, r2=4, idi=8, idj=8)
+SEMAPHORES = ["vv", "aa", "pp", "gq", "lsent", "aL", "aM", "aC", "aS", "dsrc", "dcod", "dale", "dcv", "dw0", "dw1", "dfw", "down",
+              "dfan", "dfay", "df1", "dv1", "di", "dy"]
 
 
 def rank_program(g, core, T, topo):
@@ -63,7 +56,6 @@ def rank_program(g, core, T, topo):
     cores = T.cores
     others = [d for d in range(N) if d != me]
     OB = P * me
-    VB = NP + V * me
     q = {"v": g.vector, "a": g.scalar, "p": g.tensor, "g": g, "y": g.sync}
     csem = {"v": "vv", "a": "aa", "p": "pp", "g": "gq"}
     cnt = {"v": 0, "a": 0, "p": 0, "g": 0}
@@ -112,12 +104,14 @@ def rank_program(g, core, T, topo):
             rd.setdefault(k, []).append(tok)
 
     def copy(reads, writes, out, in_, e="v", plus=None):
-        if e == "v":
+        if e == "v" and plus is None:
             op("v", g.vector.tensor_copy, reads, writes, out, in_)
+        elif e == "v":
+            op("v", g.vector.tensor_scalar, reads, writes, out, in_, plus, None, A.add)
         elif plus is None:
             op("a", g.scalar.activation, reads, writes, out, in_, F.Copy)
         else:
-            op("a", g.scalar.activation, reads, writes, out, in_, F.Identity, bias=float(plus))
+            op("a", g.scalar.activation, reads, writes, out, in_, F.Identity, bias=plus)
 
     def tsc(reads, writes, out, in0, s1, op0, s2=None, op1=None):
         if op1 is None:
@@ -134,8 +128,8 @@ def rank_program(g, core, T, topo):
     def sb(out, in0, s1, op0, s2=None, op1=None):
         tsc([in0], [out], b(out), b(in0), s1, op0, s2, op1)
 
-    def scan(reads, writes, out, d0, d1, initial):
-        op("v", g.vector.tensor_tensor_scan, reads, writes, out, d0, d1, initial, A.mult, A.add)
+    def flip(reads, writes, out, in_):
+        op("v", g.vector.transpose, reads, writes, out, in_)
 
     def fill(key, ap, c):
         op("v", g.vector.memset, [], [key], ap, c)
@@ -175,6 +169,9 @@ def rank_program(g, core, T, topo):
     def at(s, d):
         return s if s < d else s - 1
 
+    def lc(k):
+        return 3 * k + (4 if k >= 4 else 0)
+
     def load_w(e, h):
         dma(e, "dw%d" % h, 16, [], ["wt%d" % h], T.wt[:, 2048 * h:2048 * h + 2048], T.w[:, 2048 * h:2048 * h + 2048])
 
@@ -182,290 +179,253 @@ def rank_program(g, core, T, topo):
         w = slice(512 * h, 512 * h + 512)
         op("v", g.vector.quantize_mx, ["wt%d" % h], ["wq%d" % h], T.wq[:, w], T.wqs[:, w], T.wt[:, 2048 * h:2048 * h + 2048])
 
-    dma("y", "dsrc", 224, [], ["src"], T.src[0:64, :], T.alt[:, :])
+    quads = [(32 * a, 32 * a + 32) for a in range(4)]
+
+    ns = 16 * 17
+    for h in range(2):
+        dma("y", "dsrc", ns, [], ["src"], T.src[32 * h:32 * h + 32, 0:4], T.alt[:, 8 * h:8 * h + 8])
     for c in range(4):
-        dma("a", "dsrc", 224, [], ["src"], T.src[64:80, c:c + 1], T.f1[4 * c:4 * c + 4, :])
-    dma("y", "dsrc", 224, [], ["src"], T.src[96:112, :], T.f2[:, :])
+        dma("a", "dsrc", ns, [], ["src"], T.src[64:80, c:c + 1], T.f1[4 * c:4 * c + 4, :])
+    dma("y", "dsrc", ns, [], ["src"], T.src[96:112, 0:4], T.f2[:, :])
     for c in range(4):
         x = c + 1 - 2 * (c % 2)
-        dma("a", "dsrc", 224, [], ["src"], T.src[80:96, c:c + 1], T.f1[4 * x:4 * x + 4, :])
-        dma("y", "dsrc", 224, [], ["src"], T.src[112 + 4 * c:116 + 4 * c, :], T.f2[4 * x:4 * x + 4, :])
-    for p in range(N):
-        dma("ya"[p % 2], "drow", 16 * N, [], ["row1"], T.row1[p:p + 1, :], T.f1[:, :])
-    dma("y", "dcv", 32, [], ["cv.c"], T.cv[:, 4 * Z:4 * (Z + P)], T.c[:, :])
-    dma("y", "dcv", 32, [], ["cv.c"], T.cv[:, 4 * (Z + P):4 * OWN], T.v[:, :])
+        dma("a", "dsrc", ns, [], ["src"], T.src[80:96, c:c + 1], T.f1[4 * x:4 * x + 4, :])
+        dma("y", "dsrc", ns, [], ["src"], T.src[112 + 4 * c:116 + 4 * c, 0:4], T.f2[4 * x:4 * x + 4, :])
+    for h in range(2):
+        dma("ya"[h], "dsrc", ns, [], ["src"], T.src[16 * h:16 * h + 16, 4:8], T.f1[:, :])
+    for h in range(2):
+        dma("y", "dcod", 64, [], ["cod"], T.src[16 * h:16 * h + 16, 8:24], T.alt[:, :])
+        dma("y", "dcod", 64, [], ["cod"], T.src[16 * h:16 * h + 16, 24:28], T.f2[:, :])
+    for h in range(2):
+        dma("y", "dale", 32, [], ["ale"], T.ale[16 * h:16 * h + 16, :], T.alt[:, 8 * h:8 * h + 8])
+    dma("y", "dcv", 48, [], ["cv.c"], T.cv[:, 0:4 * P], T.c[:, :])
+    for h in range(2):
+        dma("y", "dcv", 48, [], ["cv.c"], T.cv[:, 4 * (P + V * h):4 * (IT + V * h)], T.v[:, :])
 
-    def begin(nm, e, k):
-        iota(nm, b(nm), [[1, 1]], 16 * k - 1 - e, e)
-        iota(nm, b(nm, 0, me + 1), [[1, 1]], 16 * k - 1, e)
-
-    iota("k4", b("k4"), [[1, 4]], NP + OB, 4)
-    iota("dd", b("dd"), [[16, 32]], 0, 1, False)
-    iota("yt", T.yt[:, 0:256], [[1, 256]], 0, 0)
-    iota("idc", b("idc"), [[1, 4]], OB, 4)
-    fill("pl0", b("pl0", 0, 32, K0, K0 + 16 * C0), 0.0)
-    iota("pl0", b("pl0", 0, 16, K0, K0 + 16 * C0), [[1, 16], [0, N - 1]], E0 * me, 0)
-    iota("dcol", b("dcol"), [[1, 1]], 0, 1)
-    iota("dcol", b("dcol", 0, me + 1), [[1, 1]], 99, 0)
-    if me:
-        iota("dcol", b("dcol", 0, me), [[1, 1]], 0, 1)
-    begin("b16", E0, K0)
-    iota("vp0", b("vp0"), [[8, 2], [1, 4], [16, 4]], Z + P, 0)
-    iota("vm0", b("vm0"), [[32, 2], [1, 16]], S0 + VB, 0)
+    iota("pi", b("pi"), [[1, 1]], 0, 1, False)
+    for r1, pattern in ((128, [[1, 128]]), (16 + AY, [[1, 16], [16, 8]]), (16, [[1, 128]]), (AY, [[1, 16], [16, 8]])):
+        iota("yt", T.yt[0:r1, 0:128], pattern, 0, 0)
+    iota("k4", b("k4"), [[1, 8]], NP + OB, 4)
+    fill("src.z", T.src[32:64, 4:28], 0)
+    fill("src.z2", T.src[64:128, 4:28], 0)
+    sb("p15", "pi", 15, A.bitwise_and)
+    sb("p3", "pi", 3, A.bitwise_and)
+    sb("m14", "p15", float(AY), A.is_ge)
+    for n in (1, 2, 4):
+        sb("bc%d" % n, "m14", float(n * (P - SI)), A.mult, float(n * SI), A.add)
+    sb("tag", "m14", -2.0 * TAG, A.mult, 2.0 * TAG, A.add)
     fill("ones", b("ones"), 1.0)
-    fill("k32", b("k32"), 1.0)
-    fill("k32", T.k32[:, 0:IT:32], 0.0)
-    fill("md", T.md[0:32, :], 0.0)
-    fill("md1", T.md1[0:32, :], 0.0)
-    fill("val0", b("val0"), 0.0)
-    fill("slot.z", T.slot[:, S0 + NO:S0 + NO + 8], 0.0)
-    fill("cv.z", T.cv[:, 0:4 * Z], 0.0)
-    fill("keep", T.keep[:, 0:16], 1.0)
-    fill("keep", T.keep[:, 0:1], 0.0)
-    for nm in ("of1", "ofq", "ofz", "ofw"):
-        copy(["dd"], [nm], b(nm), b("dd"))
-    copy(["dd"], ["ofp0"], b("ofp0"), T.dd[:, 0:2])
-    copy(["dd"], ["ofp"], b("ofp"), T.dd[:, 0:10])
+    fill("mk.z", T.mk[:, IT + V:NI], 1.0)
+    fill("slot.z", T.slot[:, NO:NO + 8], float(ZC))
+    fill("cv.z", T.cv[:, 4 * (IT + V):4 * NI], 0.0)
 
-    sb("sy", "src", 4, A.arith_shift_right)
-    sb("shh", "src", 8, A.arith_shift_right, 4095, A.bitwise_and)
-    sb("sa", "src", 16.0, A.mult)
-    sb("sb", "sy", -255.0, A.mult)
-    sb("sc", "shh", 240.0, A.mult)
-    tb("s1", "sa", "sb", A.add)
-    tb("s2", "s1", "sc", A.add)
+    sk = ["src", "src.z", "src.z2"]
+    tsc(sk, ["b1"], b("b1"), T.src[:, 0:8], 0xF80, A.bitwise_and)
+    tsc(sk, ["b2"], b("b2"), T.src[:, 0:8], 4, A.arith_shift_right, 7, A.bitwise_and)
+    tsc(sk, ["b3"], b("b3"), T.src[:, 0:8], 15, A.bitwise_and)
+    tb("s1", "b1", "b2", A.add)
+    sb("s3", "b3", 8.0, A.mult)
+    tb("s2", "s1", "s3", A.add)
     tb("sv", "s2", "k4", A.min)
     need("g", wr["sv"])
-    spread("aL", lambda d: (b("sv"), T.lists[me]))
-    tsc(["src"], ["em"], b("em"), b("src"), 0.0, A.is_lt, float(NO), A.mult)
-    tb("idf", "em", "idc", A.max)
-    dma("y", "dhd", 16, ["shh"], ["hbd"], T.hbd[:, :], b("shh"))
-    dma("y", "down", 16, ["sv"], ["lown"], T.lists[me], b("sv"))
-    dma("y", "did", 16, ["idf"], ["idd"], T.idd[:, :], T.idf[0:64, :])
-    for p in range(N):
-        dma("y", "dhb", 32 * N, ["hbd"], ["row0"], T.row0[p:p + 1, 0:P], T.hbd[0:64, :])
-        dma("y", "dhb", 32 * N, ["hbd"], ["row0"], T.row0[p:p + 1, P:IT], T.hbd[96:112, :])
+    spread("aL", lambda d: (T.sv[:, 0:4], T.lists[me]))
+    dma("y", "down", 16, ["sv"], ["lown"], T.lists[me], T.sv[:, 0:4])
 
-    for n in (256, 512, 1024):
-        copy(["yt"], ["yt"], T.yt[:, n:2 * n], T.yt[:, 0:n], "a", n)
-    copy(["yt"], ["xt"], T.xt[:, 0:NP], T.yt[:, :], "a")
-    wr["xf"] = wr["xt"]
-    copy(["yt"], ["v1"], b("v1"), T.yt[:, 0:CH], "a", NP)
+    def double(buf, e, sizes):
+        for n in sizes:
+            plus = 128.0 if n == 128 else b("bc%d" % (n // P))
+            copy([buf, "bc1", "bc2", "bc4"], [buf], T[buf][:, n:2 * n], T[buf][:, 0:n], e, plus)
 
+    copy(["yt"], ["xt"], T.xt[:, 0:128], T.yt[:, 0:128])
+    double("yt", "a", (128, 256, 512, 1024))
+    double("xt", "v", (128, 256, 512))
+    copy(["yt"], ["xh"], T.xt[:, 1024:NP], T.yt[:, 1024:NP], "a")
+
+    iota("v1", T.v1[:, 0:V], [[1, 16], [16, 4]], TAG + P, 0)
+    iota("dd", b("dd"), [[16, 32]], 0, 1, False)
     iota("jm", b("jm"), [[1, 16]], 0, 0)
-    iota("pi", b("pi"), [[1, 1]], 0, 1, False)
-    iota("gli", b("gli"), [[16, 20]], 0, 1, False)
-    iota("gli", b("gli", 0, 16), [[16, 20]], OB, 1, False)
-    begin("b48", E1, K1)
-    for k, rm, rw in ((1, 128, 24), (0, 16, 8)):
-        iota("val.c", b("val", 0, rm, 0, 128), [[32, 8], [1, 16]], S0 + OB + 16 * k, 0)
-        iota("val.c", b("val", 0, rw, 0, 128), [[2, 8], [16, 16]], Z + k, 0)
-        iota("val.v", b("val", 0, rm, 128, 160), [[32, 2], [1, 16]], S0 + VB + 16 * k, 0)
-        iota("val.v", b("val", 0, rw, 128, 160), [[8, 2], [1, 4], [16, 4]], Z + P + 4 * k, 0)
+    iota("kk", T.kk[:, 0:32], [[0, 32]], 0, 0)
+    iota("kd", T.kk[:, 32:64], [[0, 32]], 99, 0)
+    cuts = sorted(set([0, 4, min(me, N - 1), N - 1]))
+    for k0, k1 in zip(cuts[:-1], cuts[1:]):
+        iota("kd", T.kk[:, 32 + lc(k0):32 + lc(k0) + 3 * (k1 - k0)], [[1, k1 - k0], [0, 3]], others[k0], 0)
+    iota("x1", T.xt[:, NP:NP + 1024], [[1, 1024]], NP, 0)
+    for a, (r0, r1) in enumerate(quads):
+        iota("kk", T.kk[r0:r1, 0:12], [[0, 4], [16, 3]], 4 * a, 1)
+        iota("kk", T.kk[r0:r1, 16:25], [[0, 3], [16, 3]], 4 * a, 1)
+    need("g", wr["kk"])
+    for r1, base, mult in ((128, 0, 0), (32, OB - 128, 8), (16, OB, 8)):
+        iota("gli", b("gli", 0, r1), [[128, 2], [1, 8]], base, mult, False)
+    iota("slot.own", T.slot[:, SI * me:SI * me + IT], [[1, IT]], 0, 0)
+    iota("sl", b("sl"), [[1, (N - 1) * E]], NI, 0)
 
-    def compact(n, marks, key, base, width, of, val, vkeys, pl):
-        k = n // 32
-
-        def s(name, w=k):
-            return b(name, 0, 32, 0, w)
-        scan(["ones", base, key], ["pf"], s("pf", n), s("ones", n), marks, b(base, 0, 32))
-        tt(["pf", key], ["qq"], s("qq", n), s("pf", n), marks, A.mult)
-        op("v", g.vector.transpose, ["qq"], ["tq"], s("tq", n), s("qq", n))
-        scan(["tq", "k32"], ["ts"], s("ts", n), s("k32", n), s("tq", n), 0.0)
-        u = T.ts[0:32, 31:n:32]
-        tsc(["ts"], ["hi"], s("hi"), u, 1.0 / 16, A.mult, -0.46875, A.add)
-        tsc(["ts"], ["lo"], s("lo"), u, float(width), A.mult)
-        tsc(["hi"], ["l2"], s("l2"), s("hi"), 1.0 - 16.0 * width, A.mult)
-        tt(["l2", "lo"], ["sm2"], s("sm2"), s("l2"), s("lo"), A.add)
-        tt(["sm2", "dd"], ["mx2"], s("mx2"), s("sm2"), s("dd"), A.max)
-        copy(["mx2"], [of], s(of), s("mx2"))
-        copy([of] + vkeys, [pl], T[pl][:, :].indirect(T[of][:, 0:k]), T[val][:, :])
-
-    def wrap(k):
-        c, a = CC[k], KK[k]
-        both = [("dpm", 8, ("ma", "mb")), ("dpl", 0, ("la", "lb"))]
-        for sem, r, nms in both if k == "1" else both[::-1]:
-            for i, nm in enumerate(nms):
-                dma("y", sem + k, 32, ["pl" + k], [nm + k], b(nm + k), T["pl" + k][16 * i + r:16 * i + r + 8, a:a + 16 * c])
-
-    for r1, nm, plus in ((32, "vm0", 16), (24, "vp0", 4), (16, "vm0", 0), (8, "vp0", 0)):
-        tsc([nm], ["val0"], b("val0", 0, r1), b(nm, 0, r1), float(plus), A.add)
-    fill("pl0", b("pl0", 0, 8, K0, K0 + 16 * C0), 0.0)
-    tsc(["row1"], ["hb1"], T.hb1[0:N, :], T.row1[0:N, :], 8, A.arith_shift_right)
-    tsc(["hb1", "dcol"], ["md1"], T.md1[0:N, :], T.hb1[0:N, :], b("dcol", 0, N), A.is_equal)
-    compact(V, T.md1[0:32, :], "md1", "b16", C0, "ofp0", "val0", ["val0"], "pl0")
-    wrap("0")
-    for p in range(N):
-        dma("y", "demp", 16 * N, ["idd", "xf"], ["xo"], T.xt[p:p + 1, OB:OB + P], T.idd[:, :])
-    op("v", g.vector.quantize_mx, ["cv.z", "cv.c"], ["qo.own"], T.qo[:, 0:OWN], T.qos[:, 0:OWN], T.cv[:, :])
-    copy(["gli"], ["gl"], T.gl[:, 0:16], T.gli[:, 0:16])
-    sb("pm", "pi", 15, A.bitwise_and)
-    copy(["pm"], ["pmf"], b("pmf"), b("pm"))
-    tsc(["jm", "pmf"], ["mask"], T.mask[:, 0:16], b("jm"), b("pmf"), A.is_equal)
-    tsc(["row0", "dcol"], ["md"], T.md[0:N, :], T.row0[0:N, :], b("dcol", 0, N), A.is_equal)
+    for n in (1, 2, 4):
+        copy(["v1"], ["v1"], T.v1[:, V * n:2 * V * n], T.v1[:, 0:V * n], "v", float(n * SI))
+    for nm in ("of1", "ofq", "ofz", "ofw"):
+        copy(["dd"], [nm], b(nm), b("dd"))
+    tsc(sk + ["cod"], ["rk"], b("rk"), T.src[:, 4:28], 8, A.arith_shift_right, 15, A.bitwise_and)
+    tt(["rk"], ["eq"], b("eq"), b("rk", 0, 128, 0, 4), b("rk", 0, 128, 20, 24), A.is_equal)
+    sb("e15", "eq", 15.0, A.mult)
+    tt(["rk", "e15"], ["r2"], b("r2"), b("rk", 0, 128, 20, 24), b("e15"), A.max)
+    copy(["rk"], ["ow.c"], T.ow[:, 0:16], b("rk", 0, 128, 4, 20))
+    copy(["rk"], ["ow.1"], T.ow[:, 20:24], b("rk", 0, 128, 0, 4), "v", 32.0)
+    copy(["r2"], ["ow.2"], T.ow[:, 16:20], b("r2"), "v", 16.0)
+    copy(["sv"], ["gl.v"], T.gl[:, 16:20], T.sv[:, 4:8])
+    op("v", g.vector.quantize_mx, ["cv.z", "cv.c"], ["qo"], b("qo"), b("qos"), b("cv"))
 
     arrive("aL", "lfar")
+    lk = ["lfar", "lown"]
     for r in range(N):
-        dma("y", "df1", 128, ["lfar", "lown"], ["f1f"], T.f1f[0:32, 4 * r:4 * r + 4], T.lists[r, 64:96, :])
+        dma("y", "df1", 128, lk, ["f1f"], T.f1f[0:32, 4 * r:4 * r + 4], T.lists[r, 64:96, :])
     for h in range(2):
         p = 16 * h + AD
-        dma("a", "dfan", 32, ["lfar", "lown"], ["xt"], T.xt[p:p + 1, 0:NP], T.lists[:, 0:64, :])
+        dma("a", "dv1", 32, lk, ["v1"], T.v1[p:p + 1, :], T.lists[:, 96 + 16 * h:112 + 16 * h, :])
     for h in range(2):
         p = 16 * h + AD
-        dma("a", "dv1", 32, ["lfar", "lown"], ["v1"], T.v1[p:p + 1, :], T.lists[:, 96 + 16 * h:112 + 16 * h, :])
+        dma("a", "dfan", 32, lk, ["xt", "xh"], T.xt[p:p + 1, 0:NP], T.lists[:, 0:64, :])
+    for h in range(2):
+        p = 16 * h + AY
+        dma("a", "dfay", 32, lk, ["yt"], T.yt[p:p + 1, :], T.lists[:, 0:64, :])
     load_w("y", 0)
     load_w("y", 1)
-    dma("y", "dfw", 32, ["qo.own"], ["fw.own"], T.fw[:, 0:OWN].bitcast(dt.uint8), T.qo[:, 0:OWN].bitcast(dt.uint8))
-    dma("y", "dfw", 32, ["qo.own"], ["fw.own"], T.fws[:, 0:OWN], T.qos[:, 0:OWN])
-    copy(["yt"], ["x1"], T.xt[:, NP:2 * NP], T.yt[:, :], "a", 2 * NP)
+    dma("y", "dfw", 32, ["qo"], ["fw.own"], T.fw[:, 0:NI].bitcast(dt.uint8), b("qo").bitcast(dt.uint8))
+    dma("y", "dfw", 32, ["qo"], ["fw.own"], T.fws[:, 0:NI], b("qos"))
 
-    def look(table, keys, of, ok, gm, gk, n):
-        tt(keys + [ok, "mask"], [gk], gm, table.indirect(of), T.mask[:, 0:n], A.mult)
+    X = ["xt", "xh", "x1", "x2"]
 
-    X = ["xt", "x1", "x2"]
+    def step(keys, table, of, gm):
+        copy(keys + [of, "tag"], [gm], b(gm), table.indirect(b(of)), "a", b("tag"))
 
-    def step(t, of, gm):
-        copy(X[0:t + 1] + ["xo", of], [gm], b(gm), T.xt[:, 0:NP * (t + 1)].indirect(b(of)))
+    def turn(gm, row, of):
+        flip([gm], ["tr"], T.tr[0:32, :], T[gm][0:32, :])
+        copy(["tr"], [of], b(of, 0, 32), T.tr[0:32, row:CH:16])
 
-    def turn(gm, of):
-        op("v", g.vector.transpose, [gm], ["tr"], T.tr[0:32, :], T[gm][0:32, :])
-        copy(["tr"], [of], b(of, 0, 32), T.tr[0:32, AD:CH:16])
+    def put(n, of, val):
+        copy([of, val], X[0:2 * n], T.xt[:, 0:NP * n].indirect(b(of)), b(val))
 
-    def put(t, of, val):
-        copy([of, val], X[0:t + 1], T.xt[:, 0:NP * (t + 1)].indirect(b(of)), b(val))
+    def snap(t):
+        row = T.xt[0:1, OB:OB + P]
+        if t < R - 1:
+            copy(X[0:2], ["xs%d" % t], T.xs[0:1, P * t:P * t + P], row, "a")
+            return lambda: dma("y", "di", 16 * R, ["xs%d" % t], ["idw"], T.idw[32 * t:32 * t + 32, :], T.xs[0:1, P * t:P * t + P])
+        return lambda: dma("y", "di", 16 * R, X[0:2], ["idw"], T.idw[32 * t:32 * t + 32, :], row)
 
-    def picks(k):
-        la, lb, ma, mb, pku, dst, px, mt = [x + k for x in ("la", "lb", "ma", "mb", "pk", "sn", "px", "mt")]
-        pku, dss, mtu = pku + "u", dst + "s", mt + "u"
-
-        def slots_of():
-            tb(mt, ma, mb, A.max)
-            copy([mt], [mtu], b(mtu), b(mt))
-        if k == "1":
-            slots_of()
-        tb(px, la, lb, A.max)
-        copy([px], [pku], b(pku), b(px))
-        copy(["qo.own", pku], [dst], b(dst).bitcast(dt.uint32), b("qo").bitcast(dt.uint32).indirect(b(pku)))
-        copy(["qo.own", pku], [dss], b(dss), b("qos").indirect(b(pku)), "a")
-        if k == "0":
-            slots_of()
-
-    def send(k, first, e):
-        mtu, meta, dst, dss, w = "mt" + k + "u", "meta" + k, "sn" + k, "sn" + k + "s", W[k]
-        need("g", wr[mtu])
-        spread("aM" + k, lambda d: (T[mtu][:, w * at(d, me):w * at(d, me) + w], T[meta][:, w * at(me, d):w * at(me, d) + w]))
-        need("g", wr[dst])
-        spread("aC" + k, lambda d: (T[dst][:, e * at(d, me):e * at(d, me) + e].bitcast(dt.uint8),
-                                    T.fw[:, first + e * at(me, d):first + e * at(me, d) + e].bitcast(dt.uint8)))
-        need("g", wr[dss])
-        spread("aS" + k, lambda d: (T[dss][:, e * at(d, me):e * at(d, me) + e],
-                                    T.fws[:, first + e * at(me, d):first + e * at(me, d) + e]))
-        arrive("aM" + k, meta)
-        arrive("aC" + k, "fw" + k)
-        arrive("aS" + k, "fws" + k)
-
-    picks("0")
     copy(["f1f"], ["of1"], b("of1", 0, 32), b("f1f", 0, 32))
-    copy(["yt", "of1"], ["v2"], b("v2"), b("yt").indirect(b("of1")), "a")
-    step(0, "of1", "gm0")
-    need("g", wr["of1"])
-    send("0", OWN, E0)
-    iota("a0", b("a0", 0, 128, 0, P), [[1, P]], OB, 0)
-    iota("a0.v", b("a0", 0, 128, P, IT), [[1, V]], VB, 0)
-    iota("pl1", b("pl1", 0, 32, K1, K1 + 16 * C1), [[0, 16 * C1]], 0, 0)
-    iota("pl1", b("pl1", 0, 16, K1, K1 + 16 * C1), [[1, 16], [0, N - 1], [16, 3]], E1 * me, 0)
-    iota("pl1", b("pl1", 0, 8, K1, K1 + 16 * C1), [[0, 16 * C1]], 0, 0)
-    iota("slot.own", b("slot", 0, 128, S0 + OB, S0 + OB + P), [[1, 16], [16, 16]], Z, 0)
-    iota("slot.own", b("slot", 0, 128, S0 + VB, S0 + VB + V), [[1, 16], [16, 4]], Z + P, 0)
-    iota("sl0", b("sl0"), [[1, (N - 1) * E0]], OWN, 0)
-    iota("sl1", b("sl1"), [[1, (N - 1) * E1]], W1, 0)
+    step(["yt"], b("yt"), "of1", "g0")
+    put(1, "of1", "v1")
+    copy(["yt"], ["x2"], T.xt[:, NP + 1024:2 * NP], T.yt[:, 1024:NP], "a", float(NP))
+    snap(0)()
+    turn("g0", AY, "ofq")
+    step(X, b("xt"), "ofq", "g1")
+    flip(["kk", "kd"], ["kt"], b("kt"), b("kk"))
+    dcol = T.kt[:, 32:33]
+    tsc(["jm", "kt"], ["ne"], b("ne"), b("jm"), dcol, A.not_equal, BIG, A.mult)
+    tsc(["jm", "kt"], ["thr.1"], T.thr[:, 32:48], b("jm"), dcol, A.is_equal)
+    copy(["ne"], ["thr.c"], T.thr[:, 0:16], b("ne"), "v", TAG - 0.5)
+    copy(["ne"], ["thr.2"], T.thr[:, 16:32], b("ne"), "v", 2 * TAG - 0.5)
+    copy(["kt"], ["uu"], b("uu"), T.kt[:, 0:4], "v", 0.5)
+    tk = ["thr.1", "thr.c", "thr.2"]
+    copy(tk + ["ow.1"], ["mk.1"], T.mk[:, IT:IT + V], b("thr").indirect(T.ow[:, 20:24]))
+    copy(tk + ["ow.c", "ow.2"], ["th"], b("th"), b("thr").indirect(T.ow[:, 0:20]))
+    put(2, "ofq", "g0")
+    snap(1)()
+    turn("g1", AD, "ofz")
+    step(X, b("xt"), "ofz", "g2")
+    tsc(["tr"], ["m2"], b("m2", 0, 32), T.tr[0:32, AD:CH:16], float(NP), A.is_ge)
+    copy(["gli"], ["gl.c"], T.gl[:, 0:16], b("gli"))
+    tt(["tr", "m2"], ["d2"], b("d2", 0, 32), b("m2", 0, 32), T.tr[0:32, AD:CH:16], A.mult)
+    sb("bi", "p3", 3.0, A.is_lt, float(NI), A.mult)
+    for r0, r1 in quads:
+        tsc(["ale"], ["emw%d" % r0], b("emw", r0, r1), T.ale[0:32, :], 0.0, A.is_lt, float(NO), A.mult)
+    sb("bi2", "bi", 2.0 * (SI * me - V), A.add)
+    sb("thc", "bi", -1.0, A.mult, 2.0 * IT, A.add)
+    pack(0)
+    put(2, "ofz", "g1")
+    snap(2)()
 
-    OX = T.xt[0:16, OB:OB + P]
-    put(0, "of1", "v1")
-    copy(["xt"], ["x1s"], T.x1s[0:16, :], OX, "a")
-    copy(["yt"], ["x2"], T.xt[:, 2 * NP:3 * NP], T.yt[:, :], "a", 2 * NP)
-    turn("gm0", "ofq")
-    step(1, "ofq", "gm1")
-    put(1, "ofq", "v2")
-    copy(["xt"], ["x2s"], T.x2s[0:16, :], OX, "a")
-    turn("gm1", "ofz")
-    step(2, "ofz", "gm2")
-    copy(["of1"], ["gl.v"], T.gl[:, 16:20], T.of1[:, 4 * me:4 * me + 4])
-    put(2, "ofz", "gm1")
+    tt(X[0:2] + ["gl.c", "gl.v", "th"], ["mk"], T.mk[:, 0:IT], T.xt[:, 0:NP].indirect(b("gl")), b("th"), A.is_gt)
+    for r0, r1 in quads[0:2]:
+        op("v", g.vector.tensor_tensor_scan, ["ones", "mk", "mk.1", "mk.z"], ["pf%d" % r0], T.pf[r0:r1, :], T.ones[0:32, :],
+           T.mk[0:32, :], 0.0, A.mult, A.add)
+    copy(["pf0", "pf32"], ["pf64"], T.pf[64:128, :], T.pf[0:64, :])
+    pk = ["pf0", "pf32", "pf64", "uu"]
+    for c in range(3):
+        op("a", g.scalar.activation, pk, ["ja", "cnt%d" % c], b("ja"), b("pf"), F.Sign, bias=b("uu", 0, 128, c, c + 1), scale=-1.0,
+           accum_out=T.cnt[:, c:c + 1])
+    tsc(pk, ["jv"], b("jv"), b("pf"), b("uu", 0, 128, 3, 4), A.is_lt, 2.0, A.mult)
+    op("v", g.vector.tensor_reduce, ["jv"], ["cnt3"], T.cnt[:, 3:4], b("jv"), AX.X, A.add)
+    flip(["g2"], ["tr"], T.tr[0:32, :], T.g2[0:32, :])
+    tt(["tr", "d2"], ["t3"], b("t3", 0, 32), T.tr[0:32, AD:CH:16], b("d2", 0, 32), A.max)
+    copy(["t3"], ["ofw"], b("ofw", 0, 32), b("t3", 0, 32))
+    ck = ["cnt0", "cnt1", "cnt2", "cnt3"]
+    copy(ck, ["cnt4"], T.cnt[0:64, 4:8], T.cnt[64:128, 0:4])
+    copy(ck + ["cnt4"], ["cnt8"], T.cnt[0:32, 8:16], T.cnt[32:64, 0:8])
+    copy(ck + ["cnt4", "cnt8"], ["cnt16"], T.cnt[0:32, 16:32], T.cnt[0:32, 0:16])
+    flip(ck + ["cnt4", "cnt8", "cnt16"], ["ct"], T.ct[0:32, :], T.cnt[0:32, :])
+    ct = T.ct[0:32, 0:MC]
+    tsc(["ct", "bi2"], ["i2"], b("i2", 0, 32), ct, b("bi2", 0, 32), A.add, 0.5, A.mult)
+    tsc(["ct", "thc"], ["tm"], b("tm", 0, 32), ct, b("thc", 0, 32), A.is_lt, float(V), A.mult)
+    tsc(["ct", "bi"], ["fl.p"], T.fl[0:32, 0:MC], ct, b("bi", 0, 32), A.add, 0.5, A.mult)
+    tt(["i2", "tm"], ["fl.m"], T.fl[0:32, MC:2 * MC], b("i2", 0, 32), b("tm", 0, 32), A.add)
+    pm = ["pm%d" % r0 for r0, r1 in quads]
+    for r0, r1 in quads:
+        copy(["fl.p", "fl.m"], ["pm%d" % r0], T.pm[r0:r1, :], T.fl[0:32, :])
+    need("g", wr[pm[3]])
+    spread("aM", lambda d: (T.pm[:, MC + lc(at(d, me)):MC + lc(at(d, me)) + 3], T.meta[:, 3 * at(me, d):3 * at(me, d) + 3]))
+    copy(["qo"] + pm, ["sn"], b("sn").bitcast(dt.uint32), b("qo").bitcast(dt.uint32).indirect(T.pm[:, 0:LC]))
+    copy(["qo"] + pm, ["sns"], b("sns"), b("qos").indirect(T.pm[:, 0:LC]), "a")
 
-    tt(["xt", "gl", "gl.v", "a0", "a0.v"], ["ei"], b("ei"), T.xt[:, 0:NP].indirect(b("gl")), b("a0"), A.not_equal)
-    tt(["ei", "md"], ["gg"], T.gg[0:32, :], T.ei[0:32, :], T.md[0:32, :], A.mult)
-    compact(IT, T.gg[0:32, :], "gg", "b48", C1, "ofp", "val", ["val.c", "val.v"], "pl1")
-    for t, nm in enumerate(("x1s", "x2s")):
-        dma("y", "di%d" % t, 16, [nm], ["idw%d" % t], T.idw[:, 16 * t:16 * t + 16], T[nm][0:8, :])
-    wrap("1")
-    copy(["xt"], ["x3s"], T.x3s[0:16, :], OX, "a")
-    dma("y", "di2", 16, ["x3s"], ["idw2"], T.idw[:, 32:48], T.x3s[0:8, :])
-    for nm in ("mask", "keep"):
-        n = 16
-        while n < CH:
-            copy([nm], [nm], T[nm][:, n:2 * n], T[nm][:, 0:n], "a")
-            n *= 2
+    def piece(src, dst, d):
+        a, c = 16 * lc(at(d, me)), NI + E * at(me, d)
+        return T[src][:, a:a + E], T[dst][:, c:c + E]
 
-    def fill_slots(k):
-        copy(["meta" + k, "sl" + k], ["slot", "slot.own", "slot.z"],
-             b("slot").indirect(T["meta" + k][:, 0:W[k] * (N - 1)]), b("sl" + k))
+    need("g", wr["sn"])
+    spread("aC", lambda d: [x.bitcast(dt.uint8) for x in piece("sn", "fw", d)])
+    need("g", wr["sns"])
+    spread("aS", lambda d: piece("sns", "fws", d))
+    arrive("aM", "meta")
+    arrive("aC", "fw.far")
+    arrive("aS", "fws.far")
 
-    def slots(keys, c0, c1):
-        tsc(keys, ["idu%d" % t for t in range(c0, c1, 16)], T.idu[:, c0:c1], T.idw[:, c0:c1], float(S0), A.add)
-
-    def stand(c0, c1):
-        gk, w, n = "gs%d" % c0, slice(16 * c0, 16 * c1), 16 * (c1 - c0)
-        look(b("slot"), ["slot", "slot.own", "slot.z"], T.idu[:, c0:c1], "idu%d" % c0, T.gs[:, w], gk, n)
-        scan([gk, "keep"], [gk + "c"], T.gsc[:, w], T.keep[:, 0:n], T.gs[:, w], 0.0)
-        op("v", g.vector.tensor_copy, [gk + "c"], ["so%d" % t for t in range(c0 // 16, c1 // 16)], T.so[:, c0:c1],
-           T.gsc[:, 16 * c0 + 15:16 * c1:16])
-
-    def place(t):
-        copy(["fw.own", "so%d" % t] + ["fw%d" % k for k in range(min(t, 1) + 1)], ["pk%d" % t], b("pk%d" % t).bitcast(dt.uint32),
-             T.fw[:, 0:WW if t else W1].bitcast(dt.uint32).indirect(T.so[:, 16 * t:16 * t + 16]))
+    put(2, "ofw", "g2")
+    snap(3)()
+    copy(["meta", "sl"], ["slot", "slot.own", "slot.z"], b("slot").indirect(b("meta")), b("sl"))
+    pack(1)
+    tt(["idw"] + ["emw%d" % r0 for r0, r1 in quads], ["idi"], b("idi"), b("idw"), b("emw"), A.max)
+    sb("idj", "idi", TAG - 1, A.bitwise_and)
+    for h in range(2):
+        copy(["idj"], ["idu%d" % h], T.idu[:, h:16:2], b("idj"))
+    copy(["slot", "slot.own", "slot.z", "idu0", "idu1"], ["gs"], b("gs"), b("slot").indirect(b("idu")), "a")
+    flip(["gs"], ["gt"], b("gt"), b("gs"))
+    for h in range(2):
+        copy(["gt"], ["sf%d" % h], T.sf[:, 8 * h:8 * h + 8], T.gt[:, 16 * h:P:32])
+    for t, (r0, r1) in enumerate(quads):
+        copy(["sf0", "sf1"], ["so.%d" % t], T.so[0:32, 16 * t:16 * t + 16], T.sf[r0:r1, :])
+    sk = ["so.%d" % t for t in range(R)]
+    for r0, r1 in quads[1:]:
+        copy(sk, ["so%d" % r0], T.so[r0:r1, :], T.so[0:32, :])
+    sk = sk + ["so%d" % r0 for r0, r1 in quads[1:]]
 
     def products(t):
-        pk, ps = "pk%d" % t, "ps%d" % t
-        copy(["fw.own", "so%d" % t] + ["fws%d" % k for k in range(min(t, 1) + 1)], [ps], b(ps),
-             T.fws[:, 0:WW if t else W1].indirect(T.so[:, 16 * t:16 * t + 16]), "a")
+        pk, ps, of = "pk%d" % t, "ps%d" % t, T.so[:, 16 * t:16 * t + 16]
+        copy(["fw.own", "fw.far"] + sk, [pk], b(pk).bitcast(dt.uint32), b("fw").bitcast(dt.uint32).indirect(of))
+        copy(["fw.own", "fws.far"] + sk, [ps], b(ps), b("fws").indirect(of), "a")
         for i in range(O * t, O * t + O):
             w = slice(128 * i, 128 * i + 128)
             op("p", g.tensor.matmul_mx, ["wq%d" % (i // 4), pk, ps], ["acc%d" % i], T.acc[:, 512 * i:512 * i + P],
                T.wq[:, w], T.wqs[:, w], b(pk), b(ps), True, True)
 
-    def out(t, es):
+    def out(t):
         for o in range(O):
             i = O * t + o
             w = slice(P * i, P * i + P)
-            copy(["acc%d" % i], ["ys%d" % i], T.ys[:, w], T.acc[:, 512 * i:512 * i + P], es[o])
+            copy(["acc%d" % i], ["ys%d" % i], T.ys[:, w], T.acc[:, 512 * i:512 * i + P], "va"[o])
             dma("y", "dy", 16 * R * O, ["ys%d" % i], ["y%d" % i], T.y[:, w], T.ys[:, w])
 
-    turn("gm2", "ofw")
-    put(2, "ofw", "gm2")
-    picks("1")
-    send("1", W1, E1)
-    dma("y", "di3", 16, ["xt"], ["idw3"], T.idw[:, 48:64], T.xt[0:8, OB:OB + P])
-    slots(["idw0", "idw1", "idw2"], 0, 48)
-    fill_slots("0")
-    stand(0, 16)
-    place(0)
-    pack(0)
-    products(0)
-    out(0, "aa")
-    fill_slots("1")
-    slots(["idw3"], 48, 64)
-    stand(16, 48)
-    place(1)
-    products(1)
-    place(2)
-    pack(1)
-    products(2)
-    out(1, "aa")
-    stand(48, 64)
-    place(3)
-    products(3)
-    out(2, "va")
-    out(3, "va")
+    for t in range(R + 1):
+        if t < R:
+            products(t)
+        if t:
+            out(t - 1)
     need("y", [("dy", 16 * R * O)])
     need("g", [("lsent", sent[0])])

@@ -35,18 +35,19 @@ def _pool(buf, dtype, **cols):
     SCRATCH[buf] = ("sbuf", [128, a], dtype)
 
 
-_sb("int32", src=28, ale=8, pi=1, dd=32, gli=16)
-_sb("float32", sv=8, k4=8, jm=16, g0=CH, g1=CH, g2=CH, tr=CH, f1f=32, v1=CH, xt=2 * NP, yt=NP, xs=3 * P, th=IT, thr=48, kk=64, kt=64,
-    cnt=32, ct=32, fl=2 * MC, slot=NO + 8, sl=(N - 1) * E, idw=8, gs=P, gt=P, ys=2048)
-_sb("uint16", of1=32, ofq=32, ofz=32, ofw=32, gl=20, ow=24, pm=2 * MC, meta=3 * (N - 1), idu=16, sf=16, so=64)
-_sb("bfloat16", cv=4 * NI, wt=4096, ones=NI, mk=NI, pf=NI, ja=NI, jv=NI)
+_sb("int32", src=28, ale=8, pi=1, dd=32, gli=16, gri=16)
+_sb("float32", ydf=128, yid=128, x3=P, x3t=P, sv=8, k4=8, jm=16, g0=CH, g1=CH, g2=CH, tr=CH, f1f=32, v1=CH, xt=2 * NP, yt=NP, xs=3 * P, th=IT, thr=48, kk=64, kt=64,
+    cnt=32, ct=32, fl=2 * MC, slot=NO + 8, sl=(N - 1) * E, idw=8, idm=8, gs=P, gt=P, ys=2048)
+_sb("uint16", of1=32, ofq=32, ofz=32, ofw=32, gl=20, gr=16, ow=24, pm=2 * MC, meta=3 * (N - 1), idu=16, sf=16, so=64)
+_sb("bfloat16", cv=4 * NI, wt=4096, ones=2 * NI, m2q=IT, mk=NI, pf=NI, ja=2 * NI, jv=2 * NI)
+_sb("float16", jh=2 * NI)
 _sb("float8_e4m3fn_x4", wq=1024, qo=NI, sn=16 * LC, fw=WW, pk0=P, pk1=P, pk2=P, pk3=P)
 _sb("uint8", wqs=1024, qos=NI, sns=16 * LC, fws=WW, ps0=P, ps1=P, ps2=P, ps3=P)
-_pool("tf", "float32", s1=8, s2=8, s3=8, m14=1, bc1=1, bc2=1, bc4=1, tag=1, bi=1, bi2=1, thc=1, ne=16, uu=4, emw=8, tm=MC, i2=MC,
-      m2=32, d2=32, t3=32)
+_pool("tf", "float32", s1=8, s2=8, s3=8, m14=1, bc1=1, bc2=1, bc4=1, tag=1, tag3=1, bi=1, bi2=1, thc=1, ne=16, uu=4, emw=8, tm=MC, i2=MC,
+      m2=32, d2=32, t3=32, x3a=8, x3b=8)
 _pool("ti", "int32", b1=8, b2=8, b3=8, p15=1, p3=1, rk=24, eq=4, e15=4, r2=4, idi=8, idj=8)
-SEMAPHORES = ["vv", "aa", "pp", "gq", "lsent", "aL", "aM", "aC", "aS", "dsrc", "dcod", "dale", "dcv", "dw0", "dw1", "dfw", "down",
-              "dfan", "dfay", "df1", "dv1", "di", "dy"]
+SEMAPHORES = ["vv", "aa", "pp", "gq", "lsent", "aL", "aM", "aC", "aS", "dsrc", "dcod", "dale", "dcv", "dw0", "dw1", "down",
+              "dfan", "dfay", "df1", "dv1", "di", "dm", "dy"]
 
 
 def rank_program(g, core, T, topo):
@@ -201,23 +202,22 @@ def rank_program(g, core, T, topo):
     dma("y", "dcv", 48, [], ["cv.c"], T.cv[:, 0:4 * P], T.c[:, :])
     for h in range(2):
         dma("y", "dcv", 48, [], ["cv.c"], T.cv[:, 4 * (P + V * h):4 * (IT + V * h)], T.v[:, :])
+    load_w("y", 0)
 
     iota("pi", b("pi"), [[1, 1]], 0, 1, False)
-    for r1, pattern in ((128, [[1, 128]]), (16 + AY, [[1, 16], [16, 8]]), (16, [[1, 128]]), (AY, [[1, 16], [16, 8]])):
-        iota("yt", T.yt[0:r1, 0:128], pattern, 0, 0)
+    iota("ydf", b("ydf"), [[7, 16], [-15, 8]], 0, 0)
+    iota("yid", b("yid"), [[1, 16], [16, 8]], 0, 0)
     iota("k4", b("k4"), [[1, 8]], NP + OB, 4)
+    fill("yt", T.yt[:, 0:128], -float(TAG))
     fill("src.z", T.src[32:64, 4:28], 0)
     fill("src.z2", T.src[64:128, 4:28], 0)
-    sb("p15", "pi", 15, A.bitwise_and)
-    sb("p3", "pi", 3, A.bitwise_and)
+    sb("p15", "pi", 0x6F, A.bitwise_and)
     sb("m14", "p15", float(AY), A.is_ge)
+    fill("v1", T.v1[:, 0:V], -float(TAG))
+    tsc(["m14"], ["ydf"], b("ydf", 0, 32), b("ydf", 0, 32), b("m14", 0, 32), A.mult)
     for n in (1, 2, 4):
         sb("bc%d" % n, "m14", float(n * (P - SI)), A.mult, float(n * SI), A.add)
-    sb("tag", "m14", -2.0 * TAG, A.mult, 2.0 * TAG, A.add)
-    fill("ones", b("ones"), 1.0)
-    fill("mk.z", T.mk[:, IT + V:NI], 1.0)
-    fill("slot.z", T.slot[:, NO:NO + 8], float(ZC))
-    fill("cv.z", T.cv[:, 4 * (IT + V):4 * NI], 0.0)
+    tt(["ydf", "yid"], ["yt"], T.yt[0:32, 0:128], b("ydf", 0, 32), b("yid", 0, 32), A.add)
 
     sk = ["src", "src.z", "src.z2"]
     tsc(sk, ["b1"], b("b1"), T.src[:, 0:8], 0xF80, A.bitwise_and)
@@ -231,39 +231,54 @@ def rank_program(g, core, T, topo):
     spread("aL", lambda d: (T.sv[:, 0:4], T.lists[me]))
     dma("y", "down", 16, ["sv"], ["lown"], T.lists[me], T.sv[:, 0:4])
 
+    fill("kk", T.kk[:, 0:32], 0.0)
+    fill("kd", T.kk[:, 32:64], 99.0)
+    fill("gli", b("gli"), 0)
+    fill("gri", b("gri"), 0)
+
     def double(buf, e, sizes):
         for n in sizes:
             plus = 128.0 if n == 128 else b("bc%d" % (n // P))
             copy([buf, "bc1", "bc2", "bc4"], [buf], T[buf][:, n:2 * n], T[buf][:, 0:n], e, plus)
 
-    copy(["yt"], ["xt"], T.xt[:, 0:128], T.yt[:, 0:128])
+    wr["yb"] = wr["yt"]
     double("yt", "a", (128, 256, 512, 1024))
+    copy(["yb"], ["xt"], T.xt[:, 0:128], T.yt[:, 0:128])
     double("xt", "v", (128, 256, 512))
     copy(["yt"], ["xh"], T.xt[:, 1024:NP], T.yt[:, 1024:NP], "a")
 
-    iota("v1", T.v1[:, 0:V], [[1, 16], [16, 4]], TAG + P, 0)
+    iota("v1", T.v1[0:32, 0:V], [[1, 16], [16, 4]], TAG + P, 0)
     iota("dd", b("dd"), [[16, 32]], 0, 1, False)
     iota("jm", b("jm"), [[1, 16]], 0, 0)
-    iota("kk", T.kk[:, 0:32], [[0, 32]], 0, 0)
-    iota("kd", T.kk[:, 32:64], [[0, 32]], 99, 0)
     cuts = sorted(set([0, 4, min(me, N - 1), N - 1]))
     for k0, k1 in zip(cuts[:-1], cuts[1:]):
         iota("kd", T.kk[:, 32 + lc(k0):32 + lc(k0) + 3 * (k1 - k0)], [[1, k1 - k0], [0, 3]], others[k0], 0)
-    iota("x1", T.xt[:, NP:NP + 1024], [[1, 1024]], NP, 0)
+    for r1, base in ((32, OB - 128), (16, OB)):
+        iota("gli", b("gli", 0, r1), [[128, 2], [1, 8]], base, 8, False)
+    iota("gri", b("gri", 0, 16), [[1, 8], [128, 2]], OB, 8, False)
     for a, (r0, r1) in enumerate(quads):
+        need("g", wr["gri"])
         iota("kk", T.kk[r0:r1, 0:12], [[0, 4], [16, 3]], 4 * a, 1)
         iota("kk", T.kk[r0:r1, 16:25], [[0, 3], [16, 3]], 4 * a, 1)
     need("g", wr["kk"])
-    for r1, base, mult in ((128, 0, 0), (32, OB - 128, 8), (16, OB, 8)):
-        iota("gli", b("gli", 0, r1), [[128, 2], [1, 8]], base, mult, False)
+    iota("mk.z", T.mk[:, IT + V:NI], [[0, E]], 1, 0)
+    iota("ones", b("ones"), [[0, 2 * NI]], 1, 0)
+    iota("ones", T.ones[:, NI:NI + 1], [[0, 1]], 0, 0)
+    iota("slot.z", T.slot[:, NO:NO + 8], [[0, 8]], ZC, 0)
     iota("slot.own", T.slot[:, SI * me:SI * me + IT], [[1, IT]], 0, 0)
     iota("sl", b("sl"), [[1, (N - 1) * E]], NI, 0)
 
+    copy(["yt"], ["x1"], T.xt[:, NP:NP + 1024], T.yt[:, 0:1024], "a", float(NP))
     for n in (1, 2, 4):
         copy(["v1"], ["v1"], T.v1[:, V * n:2 * V * n], T.v1[:, 0:V * n], "v", float(n * SI))
-    for nm in ("of1", "ofq", "ofz", "ofw"):
+    for nm in ("of1", "ofq", "ofz"):
         copy(["dd"], [nm], b(nm), b("dd"))
+    sb("tag", "m14", -2.0 * TAG, A.mult, 2.0 * TAG, A.add)
+    sb("tag3", "m14", -8.0 * TAG, A.mult, 8.0 * TAG, A.add)
+    sb("p3", "pi", 3, A.bitwise_and)
+    fill("cv.z", T.cv[:, 4 * (IT + V):4 * NI], 0.0)
     tsc(sk + ["cod"], ["rk"], b("rk"), T.src[:, 4:28], 8, A.arith_shift_right, 15, A.bitwise_and)
+    copy([], ["rk"], b("rk", 32, 64), b("rk", 0, 32))
     tt(["rk"], ["eq"], b("eq"), b("rk", 0, 128, 0, 4), b("rk", 0, 128, 20, 24), A.is_equal)
     sb("e15", "eq", 15.0, A.mult)
     tt(["rk", "e15"], ["r2"], b("r2"), b("rk", 0, 128, 20, 24), b("e15"), A.max)
@@ -272,6 +287,15 @@ def rank_program(g, core, T, topo):
     copy(["r2"], ["ow.2"], T.ow[:, 16:20], b("r2"), "v", 16.0)
     copy(["sv"], ["gl.v"], T.gl[:, 16:20], T.sv[:, 4:8])
     op("v", g.vector.quantize_mx, ["cv.z", "cv.c"], ["qo"], b("qo"), b("qos"), b("cv"))
+    sb("bi", "p3", 2.0, A.is_lt, float(NI), A.mult)
+    for r0, r1 in quads[0:3]:
+        tsc(["ale"], ["emw%d" % r0], b("emw", r0, r1), T.ale[0:32, :], 0.0, A.is_lt, float(NO), A.mult)
+    tsc(["ale"], ["emw96"], b("emw", 96, 128), T.ale[0:32, :], 0.0, A.is_lt, float(NO), A.mult)
+    sb("bi2", "bi", 2.0 * (SI * me - V), A.add)
+    sb("thc", "bi", -1.0, A.mult, 2.0 * IT, A.add)
+    for r0, r1 in quads:
+        copy(["gri"], ["gr%d" % r0], b("gr", r0, r1), b("gri", 0, 32))
+
 
     arrive("aL", "lfar")
     lk = ["lfar", "lown"]
@@ -285,11 +309,8 @@ def rank_program(g, core, T, topo):
         dma("a", "dfan", 32, lk, ["xt", "xh"], T.xt[p:p + 1, 0:NP], T.lists[:, 0:64, :])
     for h in range(2):
         p = 16 * h + AY
-        dma("a", "dfay", 32, lk, ["yt"], T.yt[p:p + 1, :], T.lists[:, 0:64, :])
-    load_w("y", 0)
+        dma("a", "dfay", 32, lk, ["yt", "yb"], T.yt[p:p + 1, :], T.lists[:, 0:64, :])
     load_w("y", 1)
-    dma("y", "dfw", 32, ["qo"], ["fw.own"], T.fw[:, 0:NI].bitcast(dt.uint8), b("qo").bitcast(dt.uint8))
-    dma("y", "dfw", 32, ["qo"], ["fw.own"], T.fws[:, 0:NI], b("qos"))
 
     X = ["xt", "xh", "x1", "x2"]
 
@@ -304,11 +325,8 @@ def rank_program(g, core, T, topo):
         copy([of, val], X[0:2 * n], T.xt[:, 0:NP * n].indirect(b(of)), b(val))
 
     def snap(t):
-        row = T.xt[0:1, OB:OB + P]
-        if t < R - 1:
-            copy(X[0:2], ["xs%d" % t], T.xs[0:1, P * t:P * t + P], row, "a")
-            return lambda: dma("y", "di", 16 * R, ["xs%d" % t], ["idw"], T.idw[32 * t:32 * t + 32, :], T.xs[0:1, P * t:P * t + P])
-        return lambda: dma("y", "di", 16 * R, X[0:2], ["idw"], T.idw[32 * t:32 * t + 32, :], row)
+        copy(X[0:2], ["xs%d" % t], T.xs[0:1, P * t:P * t + P], T.xt[0:1, OB:OB + P], "a")
+        return lambda: dma("y", "di", 16 * (R - 1), ["xs%d" % t], ["idw"], T.idw[32 * t:32 * t + 32, :], T.xs[0:1, P * t:P * t + P])
 
     copy(["f1f"], ["of1"], b("of1", 0, 32), b("f1f", 0, 32))
     step(["yt"], b("yt"), "of1", "g0")
@@ -318,46 +336,47 @@ def rank_program(g, core, T, topo):
     turn("g0", AY, "ofq")
     step(X, b("xt"), "ofq", "g1")
     flip(["kk", "kd"], ["kt"], b("kt"), b("kk"))
+    copy(["gli"], ["gl.c"], T.gl[:, 0:16], b("gli"))
     dcol = T.kt[:, 32:33]
     tsc(["jm", "kt"], ["ne"], b("ne"), b("jm"), dcol, A.not_equal, BIG, A.mult)
     tsc(["jm", "kt"], ["thr.1"], T.thr[:, 32:48], b("jm"), dcol, A.is_equal)
+    copy(["gl.c", "gl.v"], ["gl.2"], T.gl[32:64, :], T.gl[0:32, :])
     copy(["ne"], ["thr.c"], T.thr[:, 0:16], b("ne"), "v", TAG - 0.5)
     copy(["ne"], ["thr.2"], T.thr[:, 16:32], b("ne"), "v", 2 * TAG - 0.5)
     copy(["kt"], ["uu"], b("uu"), T.kt[:, 0:4], "v", 0.5)
-    tk = ["thr.1", "thr.c", "thr.2"]
-    copy(tk + ["ow.1"], ["mk.1"], T.mk[:, IT:IT + V], b("thr").indirect(T.ow[:, 20:24]))
-    copy(tk + ["ow.c", "ow.2"], ["th"], b("th"), b("thr").indirect(T.ow[:, 0:20]))
+    op("v", g.vector.quantize_mx, ["cv.z", "cv.c"], ["fw.own"], T.fw[:, 0:NI], T.fws[:, 0:NI], b("cv"))
+    copy(["g1"], ["g0"], T.g0[32:64, :], T.g1[0:32, :], "a", 4.0 * TAG)
+    flip(["g1"], ["tr"], T.tr[0:32, :], T.g1[0:32, :])
+    copy(["tr"], ["ofq"], b("ofq", 32, 64), T.tr[0:32, AD:CH:16])
     put(2, "ofq", "g0")
-    snap(1)()
-    turn("g1", AD, "ofz")
-    step(X, b("xt"), "ofz", "g2")
-    tsc(["tr"], ["m2"], b("m2", 0, 32), T.tr[0:32, AD:CH:16], float(NP), A.is_ge)
-    copy(["gli"], ["gl.c"], T.gl[:, 0:16], b("gli"))
-    tt(["tr", "m2"], ["d2"], b("d2", 0, 32), b("m2", 0, 32), T.tr[0:32, AD:CH:16], A.mult)
-    sb("bi", "p3", 3.0, A.is_lt, float(NI), A.mult)
-    for r0, r1 in quads:
-        tsc(["ale"], ["emw%d" % r0], b("emw", r0, r1), T.ale[0:32, :], 0.0, A.is_lt, float(NO), A.mult)
-    sb("bi2", "bi", 2.0 * (SI * me - V), A.add)
-    sb("thc", "bi", -1.0, A.mult, 2.0 * IT, A.add)
-    pack(0)
-    put(2, "ofz", "g1")
-    snap(2)()
+    tk = ["thr.1", "thr.c", "thr.2"]
+    copy(tk + ["ow.c", "ow.2"], ["th"], b("th"), b("thr").indirect(T.ow[:, 0:20]), "a")
+    copy(tk + ["ow.1"], ["mk.1"], T.mk[:, IT:IT + V], b("thr").indirect(T.ow[:, 20:24]), "a")
+    copy(X[0:2], ["xs1"], T.xs[0:64, P:2 * P], T.xt[0:64, OB:OB + P], "a")
+    for t in (1, 2):
+        dma("y", "di", 48, ["xs1"], ["idw"], T.idw[32 * t:32 * t + 32, :], T.xs[0:1, P:2 * P])
+        dma("y", "dm", 32, ["xs1"], ["idm"], T.idm[32 * t + 32:32 * t + 64, :], T.xs[32:33, P:2 * P])
 
-    tt(X[0:2] + ["gl.c", "gl.v", "th"], ["mk"], T.mk[:, 0:IT], T.xt[:, 0:NP].indirect(b("gl")), b("th"), A.is_gt)
+    tt(X[0:2] + ["gl.c", "gl.v", "gl.2", "th"], ["m2q"], b("m2q"), T.xt[:, 0:NP].indirect(b("gl")), b("th"), A.is_gt)
+    copy(["tr"], ["ofz"], b("ofz", 0, 32), T.tr[0:32, AD:CH:16])
+    copy(X + ["ofz", "tag3"], ["g2"], b("g2"), b("xt").indirect(b("ofz")), "a", b("tag3"))
+    tt(["m2q"], ["mk"], T.mk[0:32, 0:IT], b("m2q", 0, 32), b("m2q", 32, 64), A.max)
     for r0, r1 in quads[0:2]:
-        op("v", g.vector.tensor_tensor_scan, ["ones", "mk", "mk.1", "mk.z"], ["pf%d" % r0], T.pf[r0:r1, :], T.ones[0:32, :],
+        op("v", g.vector.tensor_tensor_scan, ["ones", "mk", "mk.1", "mk.z"], ["pf%d" % r0], T.pf[r0:r1, :], T.ones[0:32, 0:NI],
            T.mk[0:32, :], 0.0, A.mult, A.add)
     copy(["pf0", "pf32"], ["pf64"], T.pf[64:128, :], T.pf[0:64, :])
+    tsc(["tr"], ["m2"], b("m2", 0, 32), T.tr[0:32, AD:CH:16], float(NP), A.is_ge)
     pk = ["pf0", "pf32", "pf64", "uu"]
-    for c in range(3):
-        op("a", g.scalar.activation, pk, ["ja", "cnt%d" % c], b("ja"), b("pf"), F.Sign, bias=b("uu", 0, 128, c, c + 1), scale=-1.0,
-           accum_out=T.cnt[:, c:c + 1])
-    tsc(pk, ["jv"], b("jv"), b("pf"), b("uu", 0, 128, 3, 4), A.is_lt, 2.0, A.mult)
-    op("v", g.vector.tensor_reduce, ["jv"], ["cnt3"], T.cnt[:, 3:4], b("jv"), AX.X, A.add)
-    flip(["g2"], ["tr"], T.tr[0:32, :], T.g2[0:32, :])
-    tt(["tr", "d2"], ["t3"], b("t3", 0, 32), T.tr[0:32, AD:CH:16], b("d2", 0, 32), A.max)
-    copy(["t3"], ["ofw"], b("ofw", 0, 32), b("t3", 0, 32))
-    ck = ["cnt0", "cnt1", "cnt2", "cnt3"]
+    for c in range(2):
+        op("a", g.scalar.activation, pk, ["ja%d" % c, "cnt%d" % c], T.ja[:, NI * c:NI * c + NI], b("pf"), F.Sign,
+           bias=b("uu", 0, 128, c, c + 1), scale=-1.0, accum_out=T.cnt[:, c:c + 1])
+    for c in range(2):
+        tsc(pk, ["jv%d" % c], T.jv[:, NI * c:NI * c + NI], b("pf"), b("uu", 0, 128, 2 + c, 3 + c), A.is_lt, 2.0, A.mult)
+    op("v", g.vector.tensor_tensor_scan, ["ones", "jv0", "jv1"], ["jh"], b("jh"), b("ones"), b("jv"), 0.0, A.mult, A.add)
+    copy(["jh"], ["cnt2"], T.cnt[:, 2:4], T.jh[:, NI - 1:2 * NI:NI])
+    for a in range(1, 4):
+        copy(["g2"], ["g2.%d" % a], T.g2[32 * a:32 * a + 32, 0:128], T.g2[0:32, 128 * a:128 * a + 128], "a")
+    ck = ["cnt0", "cnt1", "cnt2"]
     copy(ck, ["cnt4"], T.cnt[0:64, 4:8], T.cnt[64:128, 0:4])
     copy(ck + ["cnt4"], ["cnt8"], T.cnt[0:32, 8:16], T.cnt[32:64, 0:8])
     copy(ck + ["cnt4", "cnt8"], ["cnt16"], T.cnt[0:32, 16:32], T.cnt[0:32, 0:16])
@@ -387,15 +406,26 @@ def rank_program(g, core, T, topo):
     arrive("aC", "fw.far")
     arrive("aS", "fws.far")
 
-    put(2, "ofw", "g2")
-    snap(3)()
-    copy(["meta", "sl"], ["slot", "slot.own", "slot.z"], b("slot").indirect(b("meta")), b("sl"))
-    pack(1)
-    tt(["idw"] + ["emw%d" % r0 for r0, r1 in quads], ["idi"], b("idi"), b("idw"), b("emw"), A.max)
-    sb("idj", "idi", TAG - 1, A.bitwise_and)
+    tt(["tr", "m2"], ["d2"], b("d2", 0, 32), b("m2", 0, 32), T.tr[0:32, AD:CH:16], A.mult)
+    flip(["g2"], ["tr"], T.tr[0:32, :], T.g2[0:32, :])
+    tt(["tr", "d2"], ["t3"], b("t3", 0, 32), T.tr[0:32, AD:CH:16], b("d2", 0, 32), A.max)
+    for a, (r0, r1) in enumerate(quads):
+        copy(["t3"], ["ofw%d" % a], T.ofw[r0:r1, 0:8], b("t3", 0, 32, 8 * a, 8 * a + 8))
+    copy(["ofw%d" % a for a in range(4)] + ["g2", "g2.1", "g2.2", "g2.3"], X, b("xt").indirect(T.ofw[:, 0:8]), T.g2[:, 0:128])
+    copy(X[0:2] + ["gr%d" % r0 for r0, r1 in quads], ["x3"], b("x3"), T.xt[:, 0:NP].indirect(b("gr")), "a")
+    tt(["idm"], ["emw64", "emw96"], b("emw", 64, 128), b("emw", 64, 128), T.idm[64:128, :], A.max)
+    pack(0)
+    tt(["idw", "emw0", "emw32", "emw64"], ["idi"], b("idi", 0, 96), b("idw", 0, 96), b("emw", 0, 96), A.max)
+    flip(["x3"], ["x3t"], b("x3t"), b("x3"))
+    tt(["x3t"], ["x3a"], b("x3a", 0, 64), T.x3t[0:64, 0:P:32], T.x3t[64:128, 0:P:32], A.max)
+    tt(["x3a", "emw96"], ["x3b"], b("x3b", 0, 32), b("x3a", 32, 64), b("emw", 96, 128), A.max)
+    tt(["x3a", "x3b"], ["idi3"], b("idi", 96, 128), b("x3a", 0, 32), b("x3b", 0, 32), A.max)
+    tsc(["idi", "idi3"], ["idj"], b("idj"), b("idi"), TAG - 1, A.bitwise_and)
     for h in range(2):
         copy(["idj"], ["idu%d" % h], T.idu[:, h:16:2], b("idj"))
+    copy(["meta", "sl"], ["slot", "slot.own", "slot.z"], b("slot").indirect(b("meta")), b("sl"))
     copy(["slot", "slot.own", "slot.z", "idu0", "idu1"], ["gs"], b("gs"), b("slot").indirect(b("idu")), "a")
+    pack(1)
     flip(["gs"], ["gt"], b("gt"), b("gs"))
     for h in range(2):
         copy(["gt"], ["sf%d" % h], T.sf[:, 8 * h:8 * h + 8], T.gt[:, 16 * h:P:32])
@@ -415,17 +445,17 @@ def rank_program(g, core, T, topo):
             op("p", g.tensor.matmul_mx, ["wq%d" % (i // 4), pk, ps], ["acc%d" % i], T.acc[:, 512 * i:512 * i + P],
                T.wq[:, w], T.wqs[:, w], b(pk), b(ps), True, True)
 
-    def out(t):
-        for o in range(O):
-            i = O * t + o
-            w = slice(P * i, P * i + P)
-            copy(["acc%d" % i], ["ys%d" % i], T.ys[:, w], T.acc[:, 512 * i:512 * i + P], "va"[o])
-            dma("y", "dy", 16 * R * O, ["ys%d" % i], ["y%d" % i], T.y[:, w], T.ys[:, w])
+    def out(i, e):
+        w = slice(P * i, P * i + P)
+        copy(["acc%d" % i], ["ys%d" % i], T.ys[:, w], T.acc[:, 512 * i:512 * i + P], e)
+        dma("y", "dy", 16 * R * O, ["ys%d" % i], ["y%d" % i], T.y[:, w], T.ys[:, w])
 
-    for t in range(R + 1):
-        if t < R:
-            products(t)
-        if t:
-            out(t - 1)
+    for t in range(R - 1):
+        products(t)
+    out(0, "v")
+    out(1, "v")
+    products(R - 1)
+    for i in range(O, R * O):
+        out(i, "va"[i % 2])
     need("y", [("dy", 16 * R * O)])
     need("g", [("lsent", sent[0])])

@@ -7,8 +7,8 @@ NP = N * P
 AD, AY = 15, 14
 E = 48
 IT = P + V
-NI = IT + V + E
-SI = IT + E
+NI = IT + E
+SI = NI
 NO = N * SI
 ZC = NI - 8
 TAG = 4096
@@ -36,17 +36,17 @@ def _pool(buf, dtype, **cols):
 
 
 _sb("int32", src=28, ale=8, pi=1, dd=32, gli=16, gri=16)
-_sb("float32", ydf=128, yid=128, x3=P, x3t=P, sv=8, k4=8, jm=16, g0=CH, g1=CH, g2=CH, tr=CH, f1f=32, v1=CH, xt=2 * NP, yt=NP, xs=3 * P, th=IT, thr=48, kk=64, kt=64,
-    cnt=32, ct=32, fl=2 * MC, slot=NO + 8, sl=(N - 1) * E, idw=8, idm=8, gs=P, gt=P, ys=2048)
-_sb("uint16", of1=32, ofq=32, ofz=32, ofw=32, gl=20, gr=16, ow=24, pm=2 * MC, meta=3 * (N - 1), idu=16, sf=16, so=64)
+_sb("float32", ydf=128, yid=128, x3=P, x3t=P, sv=8, k4=8, jm=144, ne=80, n1=64, n2=64, g0=CH, g1=CH, g2=CH, tr=CH, f1f=32, v1=CH, xt=2 * NP, yt=NP, xs=3 * P, th=IT, thr=80, kk=64, kt=64,
+    cnt=32, ct=32, slot=NO + 8, sl=(N - 1) * E, idw=8, idm=8, gs=P, gt=P, ys=2048)
+_sb("uint16", of1=32, ofq=32, ofz=32, ofw=32, gl=20, gr=16, ow=20, pm=2 * MC, meta=3 * (N - 1), idu=16, sf=16, so=64)
 _sb("bfloat16", cv=4 * NI, wt=4096, ones=2 * NI, m2q=IT, mk=NI, pf=NI, ja=2 * NI, jv=2 * NI)
 _sb("float16", jh=2 * NI)
 _sb("float8_e4m3fn_x4", wq=1024, qo=NI, sn=16 * LC, fw=WW, pk0=P, pk1=P, pk2=P, pk3=P)
 _sb("uint8", wqs=1024, qos=NI, sns=16 * LC, fws=WW, ps0=P, ps1=P, ps2=P, ps3=P)
-_pool("tf", "float32", s1=8, s2=8, s3=8, m14=1, bc1=1, bc2=1, bc4=1, tag=1, tag3=1, bi=1, bi2=1, thc=1, ne=16, uu=4, emw=8, tm=MC, i2=MC,
+_pool("tf", "float32", s1=8, s2=8, s3=8, m14=1, bc1=1, bc2=1, bc4=1, tag=1, tag3=1, bi=1, bi2=1, a4=1, u0=1, uu=4, emw=8,
       m2=32, d2=32, t3=32, x3a=8, x3b=8)
-_pool("ti", "int32", b1=8, b2=8, b3=8, p15=1, p3=1, rk=24, eq=4, e15=4, r2=4, idi=8, idj=8)
-SEMAPHORES = ["vv", "aa", "pp", "gq", "lsent", "aL", "aM", "aC", "aS", "dsrc", "dcod", "dale", "dcv", "dw0", "dw1", "down",
+_pool("ti", "int32", b1=8, b2=8, b3=8, p15=1, p3=1, p5=1, rk=24, r1=4, r2=4, idi=8, idj=8)
+SEMAPHORES = ["vv", "aa", "pp", "gq", "lsent", "aL", "aM", "aC", "aS", "dsrc", "dcod", "dale", "dcv", "dw0", "dw1", "dfw", "down",
               "dfan", "dfay", "df1", "dv1", "di", "dm", "dy"]
 
 
@@ -197,12 +197,8 @@ def rank_program(g, core, T, topo):
     for h in range(2):
         dma("y", "dcod", 64, [], ["cod"], T.src[16 * h:16 * h + 16, 8:24], T.alt[:, :])
         dma("y", "dcod", 64, [], ["cod"], T.src[16 * h:16 * h + 16, 24:28], T.f2[:, :])
-    for h in range(2):
-        dma("y", "dale", 32, [], ["ale"], T.ale[16 * h:16 * h + 16, :], T.alt[:, 8 * h:8 * h + 8])
-    dma("y", "dcv", 48, [], ["cv.c"], T.cv[:, 0:4 * P], T.c[:, :])
-    for h in range(2):
-        dma("y", "dcv", 48, [], ["cv.c"], T.cv[:, 4 * (P + V * h):4 * (IT + V * h)], T.v[:, :])
-    load_w("y", 0)
+    dma("y", "dcv", 32, [], ["cv.c"], T.cv[:, 0:4 * P], T.c[:, :])
+    dma("y", "dcv", 32, [], ["cv.c"], T.cv[:, 4 * P:4 * IT], T.v[:, :])
 
     iota("pi", b("pi"), [[1, 1]], 0, 1, False)
     iota("ydf", b("ydf"), [[7, 16], [-15, 8]], 0, 0)
@@ -218,6 +214,12 @@ def rank_program(g, core, T, topo):
     for n in (1, 2, 4):
         sb("bc%d" % n, "m14", float(n * (P - SI)), A.mult, float(n * SI), A.add)
     tt(["ydf", "yid"], ["yt"], T.yt[0:32, 0:128], b("ydf", 0, 32), b("yid", 0, 32), A.add)
+    sb("tag", "m14", -2.0 * TAG, A.mult, 2.0 * TAG, A.add)
+    sb("p3", "pi", 3, A.bitwise_and)
+    sb("p5", "pi", 5, A.arith_shift_right)
+    fill("cv.z", T.cv[:, 4 * IT:4 * NI], 0.0)
+    iota("v1", T.v1[0:32, 0:V], [[1, 16], [16, 4]], TAG + P, 0)
+    iota("dd", b("dd"), [[16, 32]], 0, 1, False)
 
     sk = ["src", "src.z", "src.z2"]
     tsc(sk, ["b1"], b("b1"), T.src[:, 0:8], 0xF80, A.bitwise_and)
@@ -246,71 +248,68 @@ def rank_program(g, core, T, topo):
     copy(["yb"], ["xt"], T.xt[:, 0:128], T.yt[:, 0:128])
     double("xt", "v", (128, 256, 512))
     copy(["yt"], ["xh"], T.xt[:, 1024:NP], T.yt[:, 1024:NP], "a")
+    copy(["yt"], ["x1"], T.xt[:, NP:NP + 256], T.yt[:, 0:256], "a", float(NP))
 
-    iota("v1", T.v1[0:32, 0:V], [[1, 16], [16, 4]], TAG + P, 0)
-    iota("dd", b("dd"), [[16, 32]], 0, 1, False)
-    iota("jm", b("jm"), [[1, 16]], 0, 0)
+    iota("jm.0", T.jm[:, 0:16], [[1, 16]], 0, 0)
+    iota("jm.1", T.jm[:, 16:80], [[0, N], [1, N]], 0, 0)
+    iota("jm", T.jm[:, 80:144], [[1, N], [0, N]], 0, 0)
     cuts = sorted(set([0, 4, min(me, N - 1), N - 1]))
+    kkeys = ["kk", "kd"]
     for k0, k1 in zip(cuts[:-1], cuts[1:]):
-        iota("kd", T.kk[:, 32 + lc(k0):32 + lc(k0) + 3 * (k1 - k0)], [[1, k1 - k0], [0, 3]], others[k0], 0)
+        wr["kd%d" % k0], wr["kk%d" % k0] = wr["kd"], wr["kk"]
+        iota("kd%d" % k0, T.kk[:, 32 + lc(k0):32 + lc(k0) + 3 * (k1 - k0)], [[1, k1 - k0], [0, 3]], others[k0], 0)
+        iota("kk%d" % k0, T.kk[:, lc(k0):lc(k0) + 3 * (k1 - k0)], [[0, k1 - k0], [16, 3]], 0, 0)
+        kkeys += ["kd%d" % k0, "kk%d" % k0]
     for r1, base in ((32, OB - 128), (16, OB)):
         iota("gli", b("gli", 0, r1), [[128, 2], [1, 8]], base, 8, False)
-    iota("gri", b("gri", 0, 16), [[1, 8], [128, 2]], OB, 8, False)
-    for a, (r0, r1) in enumerate(quads):
-        need("g", wr["gri"])
-        iota("kk", T.kk[r0:r1, 0:12], [[0, 4], [16, 3]], 4 * a, 1)
-        iota("kk", T.kk[r0:r1, 16:25], [[0, 3], [16, 3]], 4 * a, 1)
-    need("g", wr["kk"])
-    iota("mk.z", T.mk[:, IT + V:NI], [[0, E]], 1, 0)
+    iota("mk.z", T.mk[:, IT:NI], [[0, E]], 1, 0)
     iota("ones", b("ones"), [[0, 2 * NI]], 1, 0)
     iota("ones", T.ones[:, NI:NI + 1], [[0, 1]], 0, 0)
+    for r0, r1 in quads:
+        need("g", [(csem["g"], cnt["g"])])
+        iota("gri", b("gri", r0, r0 + 16), [[1, 8], [128, 2]], OB, 8, False)
+    need("g", wr["gri"])
     iota("slot.z", T.slot[:, NO:NO + 8], [[0, 8]], ZC, 0)
     iota("slot.own", T.slot[:, SI * me:SI * me + IT], [[1, IT]], 0, 0)
     iota("sl", b("sl"), [[1, (N - 1) * E]], NI, 0)
 
-    copy(["yt"], ["x1"], T.xt[:, NP:NP + 1024], T.yt[:, 0:1024], "a", float(NP))
     for n in (1, 2, 4):
         copy(["v1"], ["v1"], T.v1[:, V * n:2 * V * n], T.v1[:, 0:V * n], "v", float(n * SI))
     for nm in ("of1", "ofq", "ofz"):
         copy(["dd"], [nm], b(nm), b("dd"))
-    sb("tag", "m14", -2.0 * TAG, A.mult, 2.0 * TAG, A.add)
-    sb("tag3", "m14", -8.0 * TAG, A.mult, 8.0 * TAG, A.add)
-    sb("p3", "pi", 3, A.bitwise_and)
-    fill("cv.z", T.cv[:, 4 * (IT + V):4 * NI], 0.0)
     tsc(sk + ["cod"], ["rk"], b("rk"), T.src[:, 4:28], 8, A.arith_shift_right, 15, A.bitwise_and)
     copy([], ["rk"], b("rk", 32, 64), b("rk", 0, 32))
-    tt(["rk"], ["eq"], b("eq"), b("rk", 0, 128, 0, 4), b("rk", 0, 128, 20, 24), A.is_equal)
-    sb("e15", "eq", 15.0, A.mult)
-    tt(["rk", "e15"], ["r2"], b("r2"), b("rk", 0, 128, 20, 24), b("e15"), A.max)
+    tsc(["rk"], ["r1"], b("r1"), b("rk", 0, 128, 0, 4), float(N), A.mult, 16.0, A.add)
     copy(["rk"], ["ow.c"], T.ow[:, 0:16], b("rk", 0, 128, 4, 20))
-    copy(["rk"], ["ow.1"], T.ow[:, 20:24], b("rk", 0, 128, 0, 4), "v", 32.0)
-    copy(["r2"], ["ow.2"], T.ow[:, 16:20], b("r2"), "v", 16.0)
+    tt(["rk", "r1"], ["r2"], b("r2"), b("rk", 0, 128, 20, 24), b("r1"), A.add)
+    copy(["r2"], ["ow.2"], T.ow[:, 16:20], b("r2"))
     copy(["sv"], ["gl.v"], T.gl[:, 16:20], T.sv[:, 4:8])
-    op("v", g.vector.quantize_mx, ["cv.z", "cv.c"], ["qo"], b("qo"), b("qos"), b("cv"))
     sb("bi", "p3", 2.0, A.is_lt, float(NI), A.mult)
-    for r0, r1 in quads[0:3]:
-        tsc(["ale"], ["emw%d" % r0], b("emw", r0, r1), T.ale[0:32, :], 0.0, A.is_lt, float(NO), A.mult)
-    tsc(["ale"], ["emw96"], b("emw", 96, 128), T.ale[0:32, :], 0.0, A.is_lt, float(NO), A.mult)
-    sb("bi2", "bi", 2.0 * (SI * me - V), A.add)
-    sb("thc", "bi", -1.0, A.mult, 2.0 * IT, A.add)
-    for r0, r1 in quads:
-        copy(["gri"], ["gr%d" % r0], b("gr", r0, r1), b("gri", 0, 32))
+    sb("a4", "p5", 4.0, A.mult, 0.5, A.add)
+    sb("tag3", "m14", -8.0 * TAG, A.mult, 8.0 * TAG, A.add)
+    sb("bi2", "bi", 2.0 * SI * me, A.add)
+    op("v", g.vector.quantize_mx, ["cv.z", "cv.c"], ["qo"], b("qo"), b("qos"), b("cv"))
 
 
     arrive("aL", "lfar")
     lk = ["lfar", "lown"]
     for r in range(N):
-        dma("y", "df1", 128, lk, ["f1f"], T.f1f[0:32, 4 * r:4 * r + 4], T.lists[r, 64:96, :])
+        dma("ya"[r % 2], "df1", 128, lk, ["f1f"], T.f1f[0:32, 4 * r:4 * r + 4], T.lists[r, 64:96, :])
     for h in range(2):
         p = 16 * h + AD
-        dma("a", "dv1", 32, lk, ["v1"], T.v1[p:p + 1, :], T.lists[:, 96 + 16 * h:112 + 16 * h, :])
-    for h in range(2):
-        p = 16 * h + AD
-        dma("a", "dfan", 32, lk, ["xt", "xh"], T.xt[p:p + 1, 0:NP], T.lists[:, 0:64, :])
-    for h in range(2):
+        dma("ya"[h], "dfan", 32, lk, ["xt", "xh"], T.xt[p:p + 1, 0:NP], T.lists[:, 0:64, :])
+        dma("ya"[h], "dv1", 32, lk, ["v1"], T.v1[p:p + 1, :], T.lists[:, 96 + 16 * h:112 + 16 * h, :])
         p = 16 * h + AY
-        dma("a", "dfay", 32, lk, ["yt", "yb"], T.yt[p:p + 1, :], T.lists[:, 0:64, :])
+        dma("ya"[h], "dfay", 32, lk, ["yt", "yb"], T.yt[p:p + 1, :], T.lists[:, 0:64, :])
+    for n in (256, 512):
+        copy([], ["x1"], T.xt[:, NP + n:NP + 2 * n], T.xt[:, NP:NP + n], "a", float(n))
+    need("y", wr["yt"])
+    load_w("y", 0)
     load_w("y", 1)
+    dma("y", "dfw", 32, ["qo"], ["fw.own"], T.fw[:, 0:NI].bitcast(dt.uint8), b("qo").bitcast(dt.uint8))
+    dma("y", "dfw", 32, ["qo"], ["fw.own"], T.fws[:, 0:NI], b("qos"))
+    for h in range(8):
+        dma("y", "dale", 128, [], ["ale"], T.ale[16 * h:16 * h + 16, :], T.alt[:, 8 * (h % 2):8 * (h % 2) + 8])
 
     X = ["xt", "xh", "x1", "x2"]
 
@@ -331,41 +330,39 @@ def rank_program(g, core, T, topo):
     copy(["f1f"], ["of1"], b("of1", 0, 32), b("f1f", 0, 32))
     step(["yt"], b("yt"), "of1", "g0")
     put(1, "of1", "v1")
-    copy(["yt"], ["x2"], T.xt[:, NP + 1024:2 * NP], T.yt[:, 1024:NP], "a", float(NP))
+    copy(["x1"], ["x2"], T.xt[:, NP + 1024:2 * NP], T.xt[:, NP:NP + 1024], "a", 1024.0)
     snap(0)()
     turn("g0", AY, "ofq")
     step(X, b("xt"), "ofq", "g1")
-    flip(["kk", "kd"], ["kt"], b("kt"), b("kk"))
+    flip(kkeys, ["kt"], b("kt"), b("kk"))
     copy(["gli"], ["gl.c"], T.gl[:, 0:16], b("gli"))
     dcol = T.kt[:, 32:33]
-    tsc(["jm", "kt"], ["ne"], b("ne"), b("jm"), dcol, A.not_equal, BIG, A.mult)
-    tsc(["jm", "kt"], ["thr.1"], T.thr[:, 32:48], b("jm"), dcol, A.is_equal)
+    tsc(["jm", "kt"], ["ne"], b("ne"), T.jm[:, 0:80], dcol, A.not_equal, BIG, A.mult)
+    tsc(["jm", "kt"], ["n1"], b("n1"), T.jm[:, 80:144], dcol, A.not_equal)
+    tt(["kt", "a4"], ["u0"], b("u0"), T.kt[:, 0:1], b("a4"), A.add)
     copy(["gl.c", "gl.v"], ["gl.2"], T.gl[32:64, :], T.gl[0:32, :])
-    copy(["ne"], ["thr.c"], T.thr[:, 0:16], b("ne"), "v", TAG - 0.5)
-    copy(["ne"], ["thr.2"], T.thr[:, 16:32], b("ne"), "v", 2 * TAG - 0.5)
-    copy(["kt"], ["uu"], b("uu"), T.kt[:, 0:4], "v", 0.5)
-    op("v", g.vector.quantize_mx, ["cv.z", "cv.c"], ["fw.own"], T.fw[:, 0:NI], T.fws[:, 0:NI], b("cv"))
+    tsc(["ne"], ["n2"], b("n2"), b("ne", 0, 128, 16, 80), 2 * TAG - 0.5, A.add)
+    copy(["ne"], ["thr.c"], T.thr[:, 0:16], b("ne", 0, 128, 0, 16), "v", TAG - 0.5)
+    copy(["jm", "u0"], ["uu"], b("uu"), T.jm[:, 0:4], "v", b("u0"))
+    tt(["n1", "n2"], ["thr.2"], T.thr[:, 16:80], b("n1"), b("n2"), A.mult)
     copy(["g1"], ["g0"], T.g0[32:64, :], T.g1[0:32, :], "a", 4.0 * TAG)
     flip(["g1"], ["tr"], T.tr[0:32, :], T.g1[0:32, :])
     copy(["tr"], ["ofq"], b("ofq", 32, 64), T.tr[0:32, AD:CH:16])
     put(2, "ofq", "g0")
-    tk = ["thr.1", "thr.c", "thr.2"]
-    copy(tk + ["ow.c", "ow.2"], ["th"], b("th"), b("thr").indirect(T.ow[:, 0:20]), "a")
-    copy(tk + ["ow.1"], ["mk.1"], T.mk[:, IT:IT + V], b("thr").indirect(T.ow[:, 20:24]), "a")
+    copy(["thr.c", "thr.2", "ow.c", "ow.2"], ["th"], b("th"), b("thr").indirect(b("ow")), "a")
     copy(X[0:2], ["xs1"], T.xs[0:64, P:2 * P], T.xt[0:64, OB:OB + P], "a")
     for t in (1, 2):
         dma("y", "di", 48, ["xs1"], ["idw"], T.idw[32 * t:32 * t + 32, :], T.xs[0:1, P:2 * P])
-        dma("y", "dm", 32, ["xs1"], ["idm"], T.idm[32 * t + 32:32 * t + 64, :], T.xs[32:33, P:2 * P])
+    dma("y", "dm", 16, ["xs1"], ["idm"], T.idm[64:96, :], T.xs[32:33, P:2 * P])
 
     tt(X[0:2] + ["gl.c", "gl.v", "gl.2", "th"], ["m2q"], b("m2q"), T.xt[:, 0:NP].indirect(b("gl")), b("th"), A.is_gt)
     copy(["tr"], ["ofz"], b("ofz", 0, 32), T.tr[0:32, AD:CH:16])
     copy(X + ["ofz", "tag3"], ["g2"], b("g2"), b("xt").indirect(b("ofz")), "a", b("tag3"))
     tt(["m2q"], ["mk"], T.mk[0:32, 0:IT], b("m2q", 0, 32), b("m2q", 32, 64), A.max)
     for r0, r1 in quads[0:2]:
-        op("v", g.vector.tensor_tensor_scan, ["ones", "mk", "mk.1", "mk.z"], ["pf%d" % r0], T.pf[r0:r1, :], T.ones[0:32, 0:NI],
+        op("v", g.vector.tensor_tensor_scan, ["ones", "mk", "mk.z"], ["pf%d" % r0], T.pf[r0:r1, :], T.ones[0:32, 0:NI],
            T.mk[0:32, :], 0.0, A.mult, A.add)
     copy(["pf0", "pf32"], ["pf64"], T.pf[64:128, :], T.pf[0:64, :])
-    tsc(["tr"], ["m2"], b("m2", 0, 32), T.tr[0:32, AD:CH:16], float(NP), A.is_ge)
     pk = ["pf0", "pf32", "pf64", "uu"]
     for c in range(2):
         op("a", g.scalar.activation, pk, ["ja%d" % c, "cnt%d" % c], T.ja[:, NI * c:NI * c + NI], b("pf"), F.Sign,
@@ -382,13 +379,11 @@ def rank_program(g, core, T, topo):
     copy(ck + ["cnt4", "cnt8"], ["cnt16"], T.cnt[0:32, 16:32], T.cnt[0:32, 0:16])
     flip(ck + ["cnt4", "cnt8", "cnt16"], ["ct"], T.ct[0:32, :], T.cnt[0:32, :])
     ct = T.ct[0:32, 0:MC]
-    tsc(["ct", "bi2"], ["i2"], b("i2", 0, 32), ct, b("bi2", 0, 32), A.add, 0.5, A.mult)
-    tsc(["ct", "thc"], ["tm"], b("tm", 0, 32), ct, b("thc", 0, 32), A.is_lt, float(V), A.mult)
-    tsc(["ct", "bi"], ["fl.p"], T.fl[0:32, 0:MC], ct, b("bi", 0, 32), A.add, 0.5, A.mult)
-    tt(["i2", "tm"], ["fl.m"], T.fl[0:32, MC:2 * MC], b("i2", 0, 32), b("tm", 0, 32), A.add)
+    tsc(["ct", "bi2"], ["pm.m"], T.pm[0:32, MC:2 * MC], ct, b("bi2", 0, 32), A.add, 0.5, A.mult)
+    tsc(["ct", "bi"], ["pm0"], T.pm[0:32, 0:MC], ct, b("bi", 0, 32), A.add, 0.5, A.mult)
     pm = ["pm%d" % r0 for r0, r1 in quads]
-    for r0, r1 in quads:
-        copy(["fl.p", "fl.m"], ["pm%d" % r0], T.pm[r0:r1, :], T.fl[0:32, :])
+    for r0, r1 in quads[1:]:
+        copy(["pm0", "pm.m"], ["pm%d" % r0], T.pm[r0:r1, :], T.pm[0:32, :])
     need("g", wr[pm[3]])
     spread("aM", lambda d: (T.pm[:, MC + lc(at(d, me)):MC + lc(at(d, me)) + 3], T.meta[:, 3 * at(me, d):3 * at(me, d) + 3]))
     copy(["qo"] + pm, ["sn"], b("sn").bitcast(dt.uint32), b("qo").bitcast(dt.uint32).indirect(T.pm[:, 0:LC]))
@@ -406,19 +401,22 @@ def rank_program(g, core, T, topo):
     arrive("aC", "fw.far")
     arrive("aS", "fws.far")
 
+    tsc(["tr"], ["m2"], b("m2", 0, 32), T.tr[0:32, AD:CH:16], float(NP), A.is_ge)
+    flip(["g2"], ["tr2"], T.tr[32:64, :], T.g2[0:32, :])
     tt(["tr", "m2"], ["d2"], b("d2", 0, 32), b("m2", 0, 32), T.tr[0:32, AD:CH:16], A.mult)
-    flip(["g2"], ["tr"], T.tr[0:32, :], T.g2[0:32, :])
-    tt(["tr", "d2"], ["t3"], b("t3", 0, 32), T.tr[0:32, AD:CH:16], b("d2", 0, 32), A.max)
+    copy(["gri"], ["gr"], b("gr"), b("gri"))
+    tt(["tr2", "d2"], ["t3"], b("t3", 0, 32), T.tr[32:64, AD:CH:16], b("d2", 0, 32), A.max)
+    sb("emw", "ale", 0.0, A.is_lt, float(NO), A.mult)
     for a, (r0, r1) in enumerate(quads):
         copy(["t3"], ["ofw%d" % a], T.ofw[r0:r1, 0:8], b("t3", 0, 32, 8 * a, 8 * a + 8))
     copy(["ofw%d" % a for a in range(4)] + ["g2", "g2.1", "g2.2", "g2.3"], X, b("xt").indirect(T.ofw[:, 0:8]), T.g2[:, 0:128])
-    copy(X[0:2] + ["gr%d" % r0 for r0, r1 in quads], ["x3"], b("x3"), T.xt[:, 0:NP].indirect(b("gr")), "a")
-    tt(["idm"], ["emw64", "emw96"], b("emw", 64, 128), b("emw", 64, 128), T.idm[64:128, :], A.max)
+    copy(X[0:2] + ["gr"], ["x3"], b("x3"), T.xt[:, 0:NP].indirect(b("gr")), "a")
+    tt(["idm"], ["emw"], b("emw", 64, 96), b("emw", 64, 96), T.idm[64:96, :], A.max)
     pack(0)
-    tt(["idw", "emw0", "emw32", "emw64"], ["idi"], b("idi", 0, 96), b("idw", 0, 96), b("emw", 0, 96), A.max)
+    tt(["idw", "emw"], ["idi"], b("idi", 0, 96), b("idw", 0, 96), b("emw", 0, 96), A.max)
     flip(["x3"], ["x3t"], b("x3t"), b("x3"))
     tt(["x3t"], ["x3a"], b("x3a", 0, 64), T.x3t[0:64, 0:P:32], T.x3t[64:128, 0:P:32], A.max)
-    tt(["x3a", "emw96"], ["x3b"], b("x3b", 0, 32), b("x3a", 32, 64), b("emw", 96, 128), A.max)
+    tt(["x3a", "emw"], ["x3b"], b("x3b", 0, 32), b("x3a", 32, 64), b("emw", 96, 128), A.max)
     tt(["x3a", "x3b"], ["idi3"], b("idi", 96, 128), b("x3a", 0, 32), b("x3b", 0, 32), A.max)
     tsc(["idi", "idi3"], ["idj"], b("idj"), b("idi"), TAG - 1, A.bitwise_and)
     for h in range(2):

@@ -15,6 +15,7 @@ TAG = 4096
 LC = 25
 MC = 26
 WW = NI + (N - 1) * E
+RE = 2
 BIG = 1.0e9
 
 SCRATCH = {"lists": ("dram", [8, 128, 4], "float32"), "acc": ("psum", [128, 4096], "float32")}
@@ -38,24 +39,49 @@ def _pool(buf, dtype, **cols):
 _sb("int32", src=28, ale=8, pi=1, dd=32, gli=16, gri=16)
 _sb("float32", ydf=128, yid=128, x3=P, x3t=P, sv=8, k4=8, jm=144, ne=80, n1=64, n2=64, g0=CH, g1=CH, g2=CH, tr=CH, f1f=32, v1=CH, xt=2 * NP, yt=NP, xs=3 * P, th=IT, thr=80, kk=64, kt=64,
     cnt=32, ct=32, slot=NO + 8, sl=(N - 1) * E, idw=8, idm=8, gs=P, gt=P, ys=2048)
-_sb("uint16", of1=32, ofq=32, ofz=32, ofw=32, gl=20, gr=16, ow=20, pm=2 * MC, meta=3 * (N - 1), idu=16, sf=16, so=64)
+_sb("uint16", of1=32, ofq=32, ofz=32, ofw=8, gl=20, gr=16, ow=20, pm=2 * MC, meta=3 * (N - 1), idu=16, so=64)
 _sb("bfloat16", cv=4 * NI, wt=4096, ones=2 * NI, m2q=IT, mk=NI, pf=NI, ja=2 * NI, jv=2 * NI)
 _sb("float16", jh=2 * NI)
 _sb("float8_e4m3fn_x4", wq=1024, qo=NI, sn=16 * LC, fw=WW, pk0=P, pk1=P, pk2=P, pk3=P)
-_sb("uint8", wqs=1024, qos=NI, sns=16 * LC, fws=WW, ps0=P, ps1=P, ps2=P, ps3=P)
+_sb("uint8", wqs=1024, qos=NI, sns=16 * LC, rls=4 * E, fws=WW, ps0=P, ps1=P, ps2=P, ps3=P)
 _pool("tf", "float32", s1=8, s2=8, s3=8, m14=1, bc1=1, bc2=1, bc4=1, tag=1, tag3=1, bi=1, bi2=1, a4=1, u0=1, uu=4, emw=8,
-      m2=32, d2=32, t3=32, x3a=8, x3b=8)
+      d2=8, t3=8, x3a=8, x3b=8)
 _pool("ti", "int32", b1=8, b2=8, b3=8, p15=1, p3=1, p5=1, rk=24, r1=4, r2=4, idi=8, idj=8)
-SEMAPHORES = ["vv", "aa", "pp", "gq", "lsent", "aL", "aM", "aC", "aS", "dsrc", "dcod", "dale", "dcv", "dw0", "dw1", "dfw", "down",
+SEMAPHORES = ["vv", "aa", "pp", "gq", "lsent", "aL", "aM", "aN", "aC", "aS", "aR", "dsrc", "dcod", "dale", "dcv", "dw0", "dw1", "dfw", "down",
               "dfan", "dfay", "df1", "dv1", "di", "dm", "dy"]
 
 
 def rank_program(g, core, T, topo):
     me = T.rank_of(core)
-    if me is None:
-        return
     cores = T.cores
-    others = [d for d in range(N) if d != me]
+
+    def rest(r):
+        return sorted((d for d in range(N) if d != r), key=lambda d: topo.chip(cores[d]) == topo.chip(cores[r]))
+
+    def at(s, d):
+        return rest(d).index(s)
+
+    def helper(s):
+        mine = topo.cores_of(cores[s])
+        free = [c for c in mine if c not in cores and topo.die(c) != topo.die(cores[s])]
+        return free[[c for c in mine if c in cores].index(cores[s])]
+
+    def write(to, mask, sem, src, dst):
+        rid, pid = topo.addr(to)[0:2]
+        return RemoteDMATransfer(dst_ids=[DstId(rid=rid, pnc=pid)], dma_engine_mask=sum(1 << x for x in mask), remote_sem=T.sem[sem],
+                                 src=src, dst=dst)
+
+    if me is None:
+        for s in range(N):
+            if helper(s) == core:
+                far = topo.engines(core, cores[rest(s)[0]])
+                g.wait_ge(T.sem.aR, RE)
+                g.remote_dma_fused([write(cores[d], far[2 * k:2 * k + 2], "aS", T.rls[:, E * k:E * k + E],
+                                          T.fws[:, NI + E * at(s, d):NI + E * at(s, d) + E]) for k, d in enumerate(rest(s)[0:4])],
+                                   local_sem=T.sem.lsent)
+                g.wait_ge(T.sem.lsent, 8)
+        return
+    others = rest(me)
     OB = P * me
     q = {"v": g.vector, "a": g.scalar, "p": g.tensor, "g": g, "y": g.sync}
     csem = {"v": "vv", "a": "aa", "p": "pp", "g": "gq"}
@@ -152,23 +178,16 @@ def rank_program(g, core, T, topo):
 
     sent = [0]
 
-    def spread(sem, piece):
-        ts = []
-        for d in others:
+    def spread(sem, piece, to=others, more=(), near=None):
+        ts = list(more)
+        for d in to:
             src, dst = piece(d)
-            rid, pid = topo.addr(cores[d])[0:2]
-            m = 0
-            for x in engines(core, cores[d]):
-                m |= 1 << x
-                sent[0] += 1
-            ts.append(RemoteDMATransfer(dst_ids=[DstId(rid=rid, pnc=pid)], dma_engine_mask=m, remote_sem=T.sem[sem], src=src, dst=dst))
+            sent[0] += len(engines(core, cores[d]))
+            ts.append(write(cores[d], engines(core, cores[d]), near if near and d in others[4:] else sem, src, dst))
         g.remote_dma_fused(ts, local_sem=T.sem.lsent)
 
-    def arrive(sem, key):
-        wr[key] = [(sem, sum(len(engines(cores[s], core)) for s in others))]
-
-    def at(s, d):
-        return s if s < d else s - 1
+    def arrive(sem, key, of=others):
+        wr[key] = [(sem, sum(len(engines(cores[s], core)) for s in of))]
 
     def lc(k):
         return 3 * k + (4 if k >= 4 else 0)
@@ -176,9 +195,10 @@ def rank_program(g, core, T, topo):
     def load_w(e, h):
         dma(e, "dw%d" % h, 16, [], ["wt%d" % h], T.wt[:, 2048 * h:2048 * h + 2048], T.w[:, 2048 * h:2048 * h + 2048])
 
-    def pack(h):
-        w = slice(512 * h, 512 * h + 512)
-        op("v", g.vector.quantize_mx, ["wt%d" % h], ["wq%d" % h], T.wq[:, w], T.wqs[:, w], T.wt[:, 2048 * h:2048 * h + 2048])
+    def pack(t0, t1):
+        a, c = 128 * O * t0, 128 * O * t1
+        op("v", g.vector.quantize_mx, ["wt0", "wt1"], ["wq%d" % t for t in range(t0, t1)], T.wq[:, a:c], T.wqs[:, a:c],
+           T.wt[:, 4 * a:4 * c])
 
     quads = [(32 * a, 32 * a + 32) for a in range(4)]
 
@@ -233,11 +253,6 @@ def rank_program(g, core, T, topo):
     spread("aL", lambda d: (T.sv[:, 0:4], T.lists[me]))
     dma("y", "down", 16, ["sv"], ["lown"], T.lists[me], T.sv[:, 0:4])
 
-    fill("kk", T.kk[:, 0:32], 0.0)
-    fill("kd", T.kk[:, 32:64], 99.0)
-    fill("gli", b("gli"), 0)
-    fill("gri", b("gri"), 0)
-
     def double(buf, e, sizes):
         for n in sizes:
             plus = 128.0 if n == 128 else b("bc%d" % (n // P))
@@ -247,13 +262,17 @@ def rank_program(g, core, T, topo):
     double("yt", "a", (128, 256, 512, 1024))
     copy(["yb"], ["xt"], T.xt[:, 0:128], T.yt[:, 0:128])
     double("xt", "v", (128, 256, 512))
+    copy(["yb"], ["x1", "yb"], T.xt[:, NP:NP + 128], T.yt[:, 0:128], "v", float(NP))
+    fill("kk", b("kk"), 99.0)
+    wr["kd"] = wr["kk"]
+    fill("gli", b("gli"), 0)
+    fill("gri", b("gri"), 0)
     copy(["yt"], ["xh"], T.xt[:, 1024:NP], T.yt[:, 1024:NP], "a")
-    copy(["yt"], ["x1"], T.xt[:, NP:NP + 256], T.yt[:, 0:256], "a", float(NP))
 
     iota("jm.0", T.jm[:, 0:16], [[1, 16]], 0, 0)
     iota("jm.1", T.jm[:, 16:80], [[0, N], [1, N]], 0, 0)
     iota("jm", T.jm[:, 80:144], [[1, N], [0, N]], 0, 0)
-    cuts = sorted(set([0, 4, min(me, N - 1), N - 1]))
+    cuts = [k for k in range(N - 1) if k in (0, 4) or others[k] != others[k - 1] + 1] + [N - 1]
     kkeys = ["kk", "kd"]
     for k0, k1 in zip(cuts[:-1], cuts[1:]):
         wr["kd%d" % k0], wr["kk%d" % k0] = wr["kd"], wr["kk"]
@@ -262,13 +281,13 @@ def rank_program(g, core, T, topo):
         kkeys += ["kd%d" % k0, "kk%d" % k0]
     for r1, base in ((32, OB - 128), (16, OB)):
         iota("gli", b("gli", 0, r1), [[128, 2], [1, 8]], base, 8, False)
-    iota("mk.z", T.mk[:, IT:NI], [[0, E]], 1, 0)
-    iota("ones", b("ones"), [[0, 2 * NI]], 1, 0)
-    iota("ones", T.ones[:, NI:NI + 1], [[0, 1]], 0, 0)
     for r0, r1 in quads:
         need("g", [(csem["g"], cnt["g"])])
         iota("gri", b("gri", r0, r0 + 16), [[1, 8], [128, 2]], OB, 8, False)
     need("g", wr["gri"])
+    iota("mk.z", T.mk[:, IT:NI], [[0, E]], 1, 0)
+    iota("ones", b("ones"), [[0, 2 * NI]], 1, 0)
+    iota("ones", T.ones[:, NI:NI + 1], [[0, 1]], 0, 0)
     iota("slot.z", T.slot[:, NO:NO + 8], [[0, 8]], ZC, 0)
     iota("slot.own", T.slot[:, SI * me:SI * me + IT], [[1, IT]], 0, 0)
     iota("sl", b("sl"), [[1, (N - 1) * E]], NI, 0)
@@ -284,12 +303,7 @@ def rank_program(g, core, T, topo):
     tt(["rk", "r1"], ["r2"], b("r2"), b("rk", 0, 128, 20, 24), b("r1"), A.add)
     copy(["r2"], ["ow.2"], T.ow[:, 16:20], b("r2"))
     copy(["sv"], ["gl.v"], T.gl[:, 16:20], T.sv[:, 4:8])
-    sb("bi", "p3", 2.0, A.is_lt, float(NI), A.mult)
-    sb("a4", "p5", 4.0, A.mult, 0.5, A.add)
-    sb("tag3", "m14", -8.0 * TAG, A.mult, 8.0 * TAG, A.add)
-    sb("bi2", "bi", 2.0 * SI * me, A.add)
     op("v", g.vector.quantize_mx, ["cv.z", "cv.c"], ["qo"], b("qo"), b("qos"), b("cv"))
-
 
     arrive("aL", "lfar")
     lk = ["lfar", "lown"]
@@ -301,13 +315,11 @@ def rank_program(g, core, T, topo):
         dma("ya"[h], "dv1", 32, lk, ["v1"], T.v1[p:p + 1, :], T.lists[:, 96 + 16 * h:112 + 16 * h, :])
         p = 16 * h + AY
         dma("ya"[h], "dfay", 32, lk, ["yt", "yb"], T.yt[p:p + 1, :], T.lists[:, 0:64, :])
-    for n in (256, 512):
+    for n in (128, 256, 512):
         copy([], ["x1"], T.xt[:, NP + n:NP + 2 * n], T.xt[:, NP:NP + n], "a", float(n))
     need("y", wr["yt"])
     load_w("y", 0)
     load_w("y", 1)
-    dma("y", "dfw", 32, ["qo"], ["fw.own"], T.fw[:, 0:NI].bitcast(dt.uint8), b("qo").bitcast(dt.uint8))
-    dma("y", "dfw", 32, ["qo"], ["fw.own"], T.fws[:, 0:NI], b("qos"))
     for h in range(8):
         dma("y", "dale", 128, [], ["ale"], T.ale[16 * h:16 * h + 16, :], T.alt[:, 8 * (h % 2):8 * (h % 2) + 8])
 
@@ -334,21 +346,30 @@ def rank_program(g, core, T, topo):
     snap(0)()
     turn("g0", AY, "ofq")
     step(X, b("xt"), "ofq", "g1")
-    flip(kkeys, ["kt"], b("kt"), b("kk"))
+    for a, (r0, r1) in enumerate(quads):
+        tsc(["tr"], ["d2%d" % a], b("d2", r0, r1), T.tr[0:32, 128 * a + AY:128 * a + 128:16], float(NP), A.is_ge, float(NP), A.mult)
     copy(["gli"], ["gl.c"], T.gl[:, 0:16], b("gli"))
+    copy(["gri"], ["gr"], b("gr"), b("gri"))
+    copy(["gl.c", "gl.v"], ["gl.2"], T.gl[32:64, :], T.gl[0:32, :])
+    flip(kkeys, ["kt"], b("kt"), b("kk"))
     dcol = T.kt[:, 32:33]
     tsc(["jm", "kt"], ["ne"], b("ne"), T.jm[:, 0:80], dcol, A.not_equal, BIG, A.mult)
     tsc(["jm", "kt"], ["n1"], b("n1"), T.jm[:, 80:144], dcol, A.not_equal)
-    tt(["kt", "a4"], ["u0"], b("u0"), T.kt[:, 0:1], b("a4"), A.add)
-    copy(["gl.c", "gl.v"], ["gl.2"], T.gl[32:64, :], T.gl[0:32, :])
+    sb("bi", "p3", 2.0, A.is_lt, float(NI), A.mult)
     tsc(["ne"], ["n2"], b("n2"), b("ne", 0, 128, 16, 80), 2 * TAG - 0.5, A.add)
-    copy(["ne"], ["thr.c"], T.thr[:, 0:16], b("ne", 0, 128, 0, 16), "v", TAG - 0.5)
-    copy(["jm", "u0"], ["uu"], b("uu"), T.jm[:, 0:4], "v", b("u0"))
+    sb("a4", "p5", 4.0, A.mult, 0.5, A.add)
     tt(["n1", "n2"], ["thr.2"], T.thr[:, 16:80], b("n1"), b("n2"), A.mult)
     copy(["g1"], ["g0"], T.g0[32:64, :], T.g1[0:32, :], "a", 4.0 * TAG)
     flip(["g1"], ["tr"], T.tr[0:32, :], T.g1[0:32, :])
     copy(["tr"], ["ofq"], b("ofq", 32, 64), T.tr[0:32, AD:CH:16])
     put(2, "ofq", "g0")
+    copy(["ne"], ["thr.c"], T.thr[:, 0:16], b("ne", 0, 128, 0, 16), "a", TAG - 0.5)
+    copy(["kt", "a4"], ["u0"], b("u0"), T.kt[:, 0:1], "a", b("a4"))
+    copy(["bi"], ["bi2"], b("bi2"), b("bi"), "a", 2.0 * SI * me)
+    op("a", g.scalar.activation, ["tag"], ["tag3"], b("tag3"), b("tag"), F.Identity, scale=4.0)
+    copy(["jm", "u0"], ["uu"], b("uu"), T.jm[:, 0:4], "a", b("u0"))
+    dma("y", "dfw", 32, ["qo"], ["fw.own"], T.fw[:, 0:NI].bitcast(dt.uint8), b("qo").bitcast(dt.uint8))
+    dma("y", "dfw", 32, ["qo"], ["fw.own"], T.fws[:, 0:NI], b("qos"))
     copy(["thr.c", "thr.2", "ow.c", "ow.2"], ["th"], b("th"), b("thr").indirect(b("ow")), "a")
     copy(X[0:2], ["xs1"], T.xs[0:64, P:2 * P], T.xt[0:64, OB:OB + P], "a")
     for t in (1, 2):
@@ -370,11 +391,12 @@ def rank_program(g, core, T, topo):
     for c in range(2):
         tsc(pk, ["jv%d" % c], T.jv[:, NI * c:NI * c + NI], b("pf"), b("uu", 0, 128, 2 + c, 3 + c), A.is_lt, 2.0, A.mult)
     op("v", g.vector.tensor_tensor_scan, ["ones", "jv0", "jv1"], ["jh"], b("jh"), b("ones"), b("jv"), 0.0, A.mult, A.add)
-    copy(["jh"], ["cnt2"], T.cnt[:, 2:4], T.jh[:, NI - 1:2 * NI:NI])
+    copy(["jh"], ["cnt2"], T.cnt[0:64, 2:4], T.jh[0:64, NI - 1:2 * NI:NI])
+    copy(["jh"], ["cnt6"], T.cnt[0:64, 6:8], T.jh[64:128, NI - 1:2 * NI:NI])
     for a in range(1, 4):
         copy(["g2"], ["g2.%d" % a], T.g2[32 * a:32 * a + 32, 0:128], T.g2[0:32, 128 * a:128 * a + 128], "a")
-    ck = ["cnt0", "cnt1", "cnt2"]
-    copy(ck, ["cnt4"], T.cnt[0:64, 4:8], T.cnt[64:128, 0:4])
+    ck = ["cnt0", "cnt1", "cnt2", "cnt6"]
+    copy(ck[0:2], ["cnt4"], T.cnt[0:64, 4:6], T.cnt[64:128, 0:2])
     copy(ck + ["cnt4"], ["cnt8"], T.cnt[0:32, 8:16], T.cnt[32:64, 0:8])
     copy(ck + ["cnt4", "cnt8"], ["cnt16"], T.cnt[0:32, 16:32], T.cnt[0:32, 0:16])
     flip(ck + ["cnt4", "cnt8", "cnt16"], ["ct"], T.ct[0:32, :], T.cnt[0:32, :])
@@ -385,35 +407,43 @@ def rank_program(g, core, T, topo):
     for r0, r1 in quads[1:]:
         copy(["pm0", "pm.m"], ["pm%d" % r0], T.pm[r0:r1, :], T.pm[0:32, :])
     need("g", wr[pm[3]])
-    spread("aM", lambda d: (T.pm[:, MC + lc(at(d, me)):MC + lc(at(d, me)) + 3], T.meta[:, 3 * at(me, d):3 * at(me, d) + 3]))
-    copy(["qo"] + pm, ["sn"], b("sn").bitcast(dt.uint32), b("qo").bitcast(dt.uint32).indirect(T.pm[:, 0:LC]))
-    copy(["qo"] + pm, ["sns"], b("sns"), b("qos").indirect(T.pm[:, 0:LC]), "a")
+    spread("aM", lambda d: (T.pm[:, MC + lc(at(d, me)):MC + lc(at(d, me)) + 3], T.meta[:, 3 * at(me, d):3 * at(me, d) + 3]),
+           near="aN")
 
     def piece(src, dst, d):
         a, c = 16 * lc(at(d, me)), NI + E * at(me, d)
         return T[src][:, a:a + E], T[dst][:, c:c + E]
 
-    need("g", wr["sn"])
-    spread("aC", lambda d: [x.bitcast(dt.uint8) for x in piece("sn", "fw", d)])
-    need("g", wr["sns"])
-    spread("aS", lambda d: piece("sns", "fws", d))
-    arrive("aM", "meta")
+    for k0, k1 in ((0, 4), (4, N - 1)):
+        of, w = T.pm[:, lc(k0):lc(k1 - 1) + 3], slice(16 * lc(k0), 16 * lc(k1 - 1) + E)
+        copy(["qo"] + pm, ["sn%d" % k0], T.sn[:, w].bitcast(dt.uint32), b("qo").bitcast(dt.uint32).indirect(of))
+        copy(["qo"] + pm, ["sns%d" % k0], T.sns[:, w], b("qos").indirect(of), "a")
+    used = [x for d in others for x in engines(core, cores[d])]
+    spare = [x for x in topo.engines(core, helper(me)) if x not in used]
+    need("g", wr["sn0"] + wr["sns0"])
+    spread("aC", lambda d: [x.bitcast(dt.uint8) for x in piece("sn", "fw", d)], others[0:4],
+           [write(helper(me), spare[0:RE], "aR", T.sns[:, 0:4 * E], b("rls"))])
+    sent[0] += RE
+    need("g", wr["sn4"])
+    spread("aC", lambda d: [x.bitcast(dt.uint8) for x in piece("sn", "fw", d)], others[4:])
+    need("g", wr["sns4"])
+    spread("aS", lambda d: piece("sns", "fws", d), others[4:])
+    arrive("aM", "meta0", others[0:4])
+    arrive("aN", "meta4", others[4:])
     arrive("aC", "fw.far")
     arrive("aS", "fws.far")
 
-    tsc(["tr"], ["m2"], b("m2", 0, 32), T.tr[0:32, AD:CH:16], float(NP), A.is_ge)
-    flip(["g2"], ["tr2"], T.tr[32:64, :], T.g2[0:32, :])
-    tt(["tr", "m2"], ["d2"], b("d2", 0, 32), b("m2", 0, 32), T.tr[0:32, AD:CH:16], A.mult)
-    copy(["gri"], ["gr"], b("gr"), b("gri"))
-    tt(["tr2", "d2"], ["t3"], b("t3", 0, 32), T.tr[32:64, AD:CH:16], b("d2", 0, 32), A.max)
+    gk = ["g2", "g2.1", "g2.2", "g2.3"]
+    flip(gk, ["tr"], T.tr[:, 0:128], T.g2[:, 0:128])
     sb("emw", "ale", 0.0, A.is_lt, float(NO), A.mult)
-    for a, (r0, r1) in enumerate(quads):
-        copy(["t3"], ["ofw%d" % a], T.ofw[r0:r1, 0:8], b("t3", 0, 32, 8 * a, 8 * a + 8))
-    copy(["ofw%d" % a for a in range(4)] + ["g2", "g2.1", "g2.2", "g2.3"], X, b("xt").indirect(T.ofw[:, 0:8]), T.g2[:, 0:128])
-    copy(X[0:2] + ["gr"], ["x3"], b("x3"), T.xt[:, 0:NP].indirect(b("gr")), "a")
+    tt(["tr"] + ["d2%d" % a for a in range(4)], ["t3"], b("t3"), T.tr[:, AD:128:16], b("d2"), A.add)
     tt(["idm"], ["emw"], b("emw", 64, 96), b("emw", 64, 96), T.idm[64:96, :], A.max)
-    pack(0)
+    copy(["t3"], ["ofw"], b("ofw"), b("t3"))
+    copy(["ofw"] + gk, X, b("xt").indirect(b("ofw")), T.g2[:, 0:128])
+    copy(X[0:2] + ["gr"], ["x3"], b("x3"), T.xt[:, 0:NP].indirect(b("gr")), "a")
     tt(["idw", "emw"], ["idi"], b("idi", 0, 96), b("idw", 0, 96), b("emw", 0, 96), A.max)
+    pack(0, 1)
+    copy(["meta4", "sl"], ["slot", "slot.own", "slot.z"], b("slot").indirect(T.meta[:, 12:21]), T.sl[:, 4 * E:(N - 1) * E])
     flip(["x3"], ["x3t"], b("x3t"), b("x3"))
     tt(["x3t"], ["x3a"], b("x3a", 0, 64), T.x3t[0:64, 0:P:32], T.x3t[64:128, 0:P:32], A.max)
     tt(["x3a", "emw"], ["x3b"], b("x3b", 0, 32), b("x3a", 32, 64), b("emw", 96, 128), A.max)
@@ -421,26 +451,26 @@ def rank_program(g, core, T, topo):
     tsc(["idi", "idi3"], ["idj"], b("idj"), b("idi"), TAG - 1, A.bitwise_and)
     for h in range(2):
         copy(["idj"], ["idu%d" % h], T.idu[:, h:16:2], b("idj"))
-    copy(["meta", "sl"], ["slot", "slot.own", "slot.z"], b("slot").indirect(b("meta")), b("sl"))
+    copy(["meta0", "sl"], ["slot", "slot.own", "slot.z"], b("slot").indirect(T.meta[:, 0:12]), T.sl[:, 0:4 * E])
     copy(["slot", "slot.own", "slot.z", "idu0", "idu1"], ["gs"], b("gs"), b("slot").indirect(b("idu")), "a")
-    pack(1)
+    pack(1, 3)
+    pack(3, 4)
     flip(["gs"], ["gt"], b("gt"), b("gs"))
-    for h in range(2):
-        copy(["gt"], ["sf%d" % h], T.sf[:, 8 * h:8 * h + 8], T.gt[:, 16 * h:P:32])
-    for t, (r0, r1) in enumerate(quads):
-        copy(["sf0", "sf1"], ["so.%d" % t], T.so[0:32, 16 * t:16 * t + 16], T.sf[r0:r1, :])
-    sk = ["so.%d" % t for t in range(R)]
+    for c in range(2 * R):
+        t, h = c // 2, c % 2
+        copy(["gt"], ["sa%d" % c], T.so[0:32, 8 * c:8 * c + 8], T.gt[32 * t:32 * t + 32, 16 * h:P:32])
+    wr["so0"] = wr["sa%d" % (2 * R - 1)]
     for r0, r1 in quads[1:]:
-        copy(sk, ["so%d" % r0], T.so[r0:r1, :], T.so[0:32, :])
-    sk = sk + ["so%d" % r0 for r0, r1 in quads[1:]]
+        copy(["so0"], ["so%d" % r0], T.so[r0:r1, :], T.so[0:32, :])
 
     def products(t):
         pk, ps, of = "pk%d" % t, "ps%d" % t, T.so[:, 16 * t:16 * t + 16]
+        sk = ["so%d" % r0 for r0, r1 in quads]
         copy(["fw.own", "fw.far"] + sk, [pk], b(pk).bitcast(dt.uint32), b("fw").bitcast(dt.uint32).indirect(of))
         copy(["fw.own", "fws.far"] + sk, [ps], b(ps), b("fws").indirect(of), "a")
         for i in range(O * t, O * t + O):
             w = slice(128 * i, 128 * i + 128)
-            op("p", g.tensor.matmul_mx, ["wq%d" % (i // 4), pk, ps], ["acc%d" % i], T.acc[:, 512 * i:512 * i + P],
+            op("p", g.tensor.matmul_mx, ["wq%d" % t, pk, ps], ["acc%d" % i], T.acc[:, 512 * i:512 * i + P],
                T.wq[:, w], T.wqs[:, w], b(pk), b(ps), True, True)
 
     def out(i, e):
@@ -448,12 +478,12 @@ def rank_program(g, core, T, topo):
         copy(["acc%d" % i], ["ys%d" % i], T.ys[:, w], T.acc[:, 512 * i:512 * i + P], e)
         dma("y", "dy", 16 * R * O, ["ys%d" % i], ["y%d" % i], T.y[:, w], T.ys[:, w])
 
-    for t in range(R - 1):
+    for t in range(R):
         products(t)
-    out(0, "v")
-    out(1, "v")
-    products(R - 1)
-    for i in range(O, R * O):
-        out(i, "va"[i % 2])
+        if t == R - 2:
+            out(0, "v")
+            out(1, "v")
+    for i in range(2, R * O):
+        out(i, "av"[i % 2])
     need("y", [("dy", 16 * R * O)])
     need("g", [("lsent", sent[0])])

@@ -15,7 +15,7 @@ TAG = 4096
 LC = 25
 MC = 26
 WW = NI + (N - 1) * E
-RE = 2
+RE = 4
 BIG = 1.0e9
 
 SCRATCH = {"lists": ("dram", [8, 128, 4], "float32"), "acc": ("psum", [128, 4096], "float32")}
@@ -37,18 +37,18 @@ def _pool(buf, dtype, **cols):
 
 
 _sb("int32", src=28, ale=8, pi=1, dd=32, gli=16, gri=16)
-_sb("float32", ydf=128, yid=128, x3=P, x3t=P, sv=8, k4=8, jm=144, ne=80, n1=64, n2=64, g0=CH, g1=CH, g2=CH, tr=CH, f1f=32, v1=CH, xt=2 * NP, yt=NP, xs=3 * P, th=IT, thr=80, kk=64, kt=64,
+_sb("float32", ydf=128, yid=128, x3=P, x3t=P, sv=8, k4=8, jm=144, ne=80, n1=64, n2=64, g0=CH, g1=CH, g2=CH, tr=CH, f1f=32, v1=CH, xt=3 * NP, yt=NP, xs=3 * P, th=IT, thr=80, kk=64, kt=64,
     cnt=32, ct=32, slot=NO + 8, sl=(N - 1) * E, idw=8, idm=8, gs=P, gt=P, ys=2048)
 _sb("uint16", of1=32, ofq=32, ofz=32, ofw=8, gl=20, gr=16, ow=20, pm=2 * MC, meta=3 * (N - 1), idu=16, so=64)
-_sb("bfloat16", cv=4 * NI, wt=4096, ones=2 * NI, m2q=IT, mk=NI, pf=NI, ja=2 * NI, jv=2 * NI)
+_sb("bfloat16", cv=4 * NI, wt=4096, ones=NI, m2q=IT, mk=NI, pf=NI, ja=2 * NI, jv=2 * NI)
 _sb("float16", jh=2 * NI)
 _sb("float8_e4m3fn_x4", wq=1024, qo=NI, sn=16 * LC, fw=WW, pk0=P, pk1=P, pk2=P, pk3=P)
 _sb("uint8", wqs=1024, qos=NI, sns=16 * LC, rls=4 * E, fws=WW, ps0=P, ps1=P, ps2=P, ps3=P)
-_pool("tf", "float32", s1=8, s2=8, s3=8, m14=1, bc1=1, bc2=1, bc4=1, tag=1, tag3=1, bi=1, bi2=1, a4=1, u0=1, uu=4, emw=8,
-      d2=8, t3=8, x3a=8, x3b=8)
+_pool("tf", "float32", s1=8, s3=8, m14=1, bc1=1, bc2=1, bc4=1, tag=1, tag3=1, bi=1, bi2=1, a4=1, u0=1, uu=4, emw=8,
+      d2=32, t3=32, x3a=8, em4=4)
 _pool("ti", "int32", b1=8, b2=8, b3=8, p15=1, p3=1, p5=1, rk=24, r1=4, r2=4, idi=8, idj=8)
 SEMAPHORES = ["vv", "aa", "pp", "gq", "lsent", "aL", "aM", "aN", "aC", "aS", "aR", "dsrc", "dcod", "dale", "dcv", "dw0", "dw1", "dfw", "down",
-              "dfan", "dfay", "df1", "dv1", "di", "dm", "dy"]
+              "dfan", "dfay", "df1", "dv1", "di", "dm", "dem", "dy"]
 
 
 def rank_program(g, core, T, topo):
@@ -247,8 +247,10 @@ def rank_program(g, core, T, topo):
     tsc(sk, ["b3"], b("b3"), T.src[:, 0:8], 15, A.bitwise_and)
     tb("s1", "b1", "b2", A.add)
     sb("s3", "b3", 8.0, A.mult)
-    tb("s2", "s1", "s3", A.add)
-    tb("sv", "s2", "k4", A.min)
+    for j in range(4):
+        tsc(["s1", "s3", "k4"], ["sv"] if j == 3 else [], T.sv[:, j:j + 1], b("s1", 0, 128, j, j + 1), b("s3", 0, 128, j, j + 1), A.add,
+            T.k4[:, j:j + 1], A.min)
+    tt(["s1", "s3"], ["sv.v"], T.sv[:, 4:8], b("s1", 0, 128, 4, 8), b("s3", 0, 128, 4, 8), A.add)
     need("g", wr["sv"])
     spread("aL", lambda d: (T.sv[:, 0:4], T.lists[me]))
     dma("y", "down", 16, ["sv"], ["lown"], T.lists[me], T.sv[:, 0:4])
@@ -286,8 +288,7 @@ def rank_program(g, core, T, topo):
         iota("gri", b("gri", r0, r0 + 16), [[1, 8], [128, 2]], OB, 8, False)
     need("g", wr["gri"])
     iota("mk.z", T.mk[:, IT:NI], [[0, E]], 1, 0)
-    iota("ones", b("ones"), [[0, 2 * NI]], 1, 0)
-    iota("ones", T.ones[:, NI:NI + 1], [[0, 1]], 0, 0)
+    iota("ones", b("ones"), [[0, NI]], 1, 0)
     iota("slot.z", T.slot[:, NO:NO + 8], [[0, 8]], ZC, 0)
     iota("slot.own", T.slot[:, SI * me:SI * me + IT], [[1, IT]], 0, 0)
     iota("sl", b("sl"), [[1, (N - 1) * E]], NI, 0)
@@ -302,7 +303,7 @@ def rank_program(g, core, T, topo):
     copy(["rk"], ["ow.c"], T.ow[:, 0:16], b("rk", 0, 128, 4, 20))
     tt(["rk", "r1"], ["r2"], b("r2"), b("rk", 0, 128, 20, 24), b("r1"), A.add)
     copy(["r2"], ["ow.2"], T.ow[:, 16:20], b("r2"))
-    copy(["sv"], ["gl.v"], T.gl[:, 16:20], T.sv[:, 4:8])
+    copy(["sv.v"], ["gl.v"], T.gl[:, 16:20], T.sv[:, 4:8])
     op("v", g.vector.quantize_mx, ["cv.z", "cv.c"], ["qo"], b("qo"), b("qos"), b("cv"))
 
     arrive("aL", "lfar")
@@ -320,8 +321,8 @@ def rank_program(g, core, T, topo):
     need("y", wr["yt"])
     load_w("y", 0)
     load_w("y", 1)
-    for h in range(8):
-        dma("y", "dale", 128, [], ["ale"], T.ale[16 * h:16 * h + 16, :], T.alt[:, 8 * (h % 2):8 * (h % 2) + 8])
+    for h in range(6):
+        dma("y", "dale", 96, [], ["ale"], T.ale[16 * h:16 * h + 16, :], T.alt[:, 8 * (h % 2):8 * (h % 2) + 8])
 
     X = ["xt", "xh", "x1", "x2"]
 
@@ -335,34 +336,33 @@ def rank_program(g, core, T, topo):
     def put(n, of, val):
         copy([of, val], X[0:2 * n], T.xt[:, 0:NP * n].indirect(b(of)), b(val))
 
-    def snap(t):
-        copy(X[0:2], ["xs%d" % t], T.xs[0:1, P * t:P * t + P], T.xt[0:1, OB:OB + P], "a")
-        return lambda: dma("y", "di", 16 * (R - 1), ["xs%d" % t], ["idw"], T.idw[32 * t:32 * t + 32, :], T.xs[0:1, P * t:P * t + P])
-
     copy(["f1f"], ["of1"], b("of1", 0, 32), b("f1f", 0, 32))
     step(["yt"], b("yt"), "of1", "g0")
     put(1, "of1", "v1")
     copy(["x1"], ["x2"], T.xt[:, NP + 1024:2 * NP], T.xt[:, NP:NP + 1024], "a", 1024.0)
-    snap(0)()
+    copy(X[0:2], ["xs0"], T.xs[0:1, 0:P], T.xt[0:1, OB:OB + P], "a")
+    dma("y", "di", 48, ["xs0"], ["idw"], T.idw[0:32, :], T.xs[0:1, 0:P])
     turn("g0", AY, "ofq")
     step(X, b("xt"), "ofq", "g1")
-    for a, (r0, r1) in enumerate(quads):
-        tsc(["tr"], ["d2%d" % a], b("d2", r0, r1), T.tr[0:32, 128 * a + AY:128 * a + 128:16], float(NP), A.is_ge, float(NP), A.mult)
+    tsc(["tr"], ["d2"], b("d2", 0, 32), T.tr[0:32, AY:CH:16], float(NP), A.is_ge, float(NP), A.mult)
     copy(["gli"], ["gl.c"], T.gl[:, 0:16], b("gli"))
     copy(["gri"], ["gr"], b("gr"), b("gri"))
+    tt(["tr", "d2"], ["t3"], b("t3", 0, 32), T.tr[0:32, AY:CH:16], b("d2", 0, 32), A.add)
     copy(["gl.c", "gl.v"], ["gl.2"], T.gl[32:64, :], T.gl[0:32, :])
     flip(kkeys, ["kt"], b("kt"), b("kk"))
     dcol = T.kt[:, 32:33]
     tsc(["jm", "kt"], ["ne"], b("ne"), T.jm[:, 0:80], dcol, A.not_equal, BIG, A.mult)
     tsc(["jm", "kt"], ["n1"], b("n1"), T.jm[:, 80:144], dcol, A.not_equal)
     sb("bi", "p3", 2.0, A.is_lt, float(NI), A.mult)
+    tsc(["src"], ["em4"], b("em4", 0, 64), T.src[0:64, 0:4], 0.0, A.is_lt, float(NO), A.mult)
     tsc(["ne"], ["n2"], b("n2"), b("ne", 0, 128, 16, 80), 2 * TAG - 0.5, A.add)
     sb("a4", "p5", 4.0, A.mult, 0.5, A.add)
+    copy(["t3"], ["of1"], b("of1", 0, 32), b("t3", 0, 32))
     tt(["n1", "n2"], ["thr.2"], T.thr[:, 16:80], b("n1"), b("n2"), A.mult)
     copy(["g1"], ["g0"], T.g0[32:64, :], T.g1[0:32, :], "a", 4.0 * TAG)
     flip(["g1"], ["tr"], T.tr[0:32, :], T.g1[0:32, :])
-    copy(["tr"], ["ofq"], b("ofq", 32, 64), T.tr[0:32, AD:CH:16])
-    put(2, "ofq", "g0")
+    copy(["tr"], ["of1"], b("of1", 32, 64), T.tr[0:32, AD:CH:16])
+    put(3, "of1", "g0")
     copy(["ne"], ["thr.c"], T.thr[:, 0:16], b("ne", 0, 128, 0, 16), "a", TAG - 0.5)
     copy(["kt", "a4"], ["u0"], b("u0"), T.kt[:, 0:1], "a", b("a4"))
     copy(["bi"], ["bi2"], b("bi2"), b("bi"), "a", 2.0 * SI * me)
@@ -379,34 +379,42 @@ def rank_program(g, core, T, topo):
     tt(X[0:2] + ["gl.c", "gl.v", "gl.2", "th"], ["m2q"], b("m2q"), T.xt[:, 0:NP].indirect(b("gl")), b("th"), A.is_gt)
     copy(["tr"], ["ofz"], b("ofz", 0, 32), T.tr[0:32, AD:CH:16])
     copy(X + ["ofz", "tag3"], ["g2"], b("g2"), b("xt").indirect(b("ofz")), "a", b("tag3"))
+    dma("y", "dem", 16, ["em4"], X, T.xt[96:97, OB:OB + P], b("em4", 0, 64))
     tt(["m2q"], ["mk"], T.mk[0:32, 0:IT], b("m2q", 0, 32), b("m2q", 32, 64), A.max)
-    for r0, r1 in quads[0:2]:
+    for r0, r1 in quads:
         op("v", g.vector.tensor_tensor_scan, ["ones", "mk", "mk.z"], ["pf%d" % r0], T.pf[r0:r1, :], T.ones[0:32, 0:NI],
            T.mk[0:32, :], 0.0, A.mult, A.add)
-    copy(["pf0", "pf32"], ["pf64"], T.pf[64:128, :], T.pf[0:64, :])
-    pk = ["pf0", "pf32", "pf64", "uu"]
+    tsc(["ale"], ["emw"], b("emw", 0, 96), b("ale", 0, 96), 0.0, A.is_lt, float(NO), A.mult)
+    for a in range(1, 4):
+        copy(["g2"], ["g2.%d" % a], T.g2[32 * a:32 * a + 32, 0:128], T.g2[0:32, 128 * a:128 * a + 128], "a")
+    pk = ["pf0", "pf32", "pf64", "pf96", "uu"]
     for c in range(2):
         op("a", g.scalar.activation, pk, ["ja%d" % c, "cnt%d" % c], T.ja[:, NI * c:NI * c + NI], b("pf"), F.Sign,
            bias=b("uu", 0, 128, c, c + 1), scale=-1.0, accum_out=T.cnt[:, c:c + 1])
     for c in range(2):
         tsc(pk, ["jv%d" % c], T.jv[:, NI * c:NI * c + NI], b("pf"), b("uu", 0, 128, 2 + c, 3 + c), A.is_lt, 2.0, A.mult)
-    op("v", g.vector.tensor_tensor_scan, ["ones", "jv0", "jv1"], ["jh"], b("jh"), b("ones"), b("jv"), 0.0, A.mult, A.add)
-    copy(["jh"], ["cnt2"], T.cnt[0:64, 2:4], T.jh[0:64, NI - 1:2 * NI:NI])
-    copy(["jh"], ["cnt6"], T.cnt[0:64, 6:8], T.jh[64:128, NI - 1:2 * NI:NI])
-    for a in range(1, 4):
-        copy(["g2"], ["g2.%d" % a], T.g2[32 * a:32 * a + 32, 0:128], T.g2[0:32, 128 * a:128 * a + 128], "a")
+    for c in range(2):
+        w = slice(NI * c, NI * c + NI)
+        op("v", g.vector.tensor_tensor_scan, ["ones", "jv%d" % c], ["jh%d" % c], T.jh[:, w], b("ones"), T.jv[:, w], 0.0, A.mult, A.add)
+    copy(["jh0", "jh1"], ["cnt2"], T.cnt[0:64, 2:4], T.jh[0:64, NI - 1:2 * NI:NI])
+    copy(["jh0", "jh1"], ["cnt6"], T.cnt[0:64, 6:8], T.jh[64:128, NI - 1:2 * NI:NI])
     ck = ["cnt0", "cnt1", "cnt2", "cnt6"]
     copy(ck[0:2], ["cnt4"], T.cnt[0:64, 4:6], T.cnt[64:128, 0:2])
+    gk = ["g2", "g2.1", "g2.2", "g2.3"]
+    flip(gk, ["tr"], T.tr[:, 0:128], T.g2[:, 0:128])
     copy(ck + ["cnt4"], ["cnt8"], T.cnt[0:32, 8:16], T.cnt[32:64, 0:8])
-    copy(ck + ["cnt4", "cnt8"], ["cnt16"], T.cnt[0:32, 16:32], T.cnt[0:32, 0:16])
-    flip(ck + ["cnt4", "cnt8", "cnt16"], ["ct"], T.ct[0:32, :], T.cnt[0:32, :])
+    copy(ck + ["cnt4"], ["cnt16"], T.cnt[0:32, 16:24], T.cnt[0:32, 0:8])
+    copy(ck + ["cnt4"], ["cnt24"], T.cnt[0:32, 24:32], T.cnt[32:64, 0:8])
+    tt(["idm"], ["emw"], b("emw", 64, 96), b("emw", 64, 96), T.idm[64:96, :], A.max)
+    flip(ck + ["cnt4", "cnt8", "cnt16", "cnt24"], ["ct"], T.ct[0:32, :], T.cnt[0:32, :])
+    copy(["tr"], ["ofw"], b("ofw"), T.tr[:, AD:128:16])
     ct = T.ct[0:32, 0:MC]
-    tsc(["ct", "bi2"], ["pm.m"], T.pm[0:32, MC:2 * MC], ct, b("bi2", 0, 32), A.add, 0.5, A.mult)
-    tsc(["ct", "bi"], ["pm0"], T.pm[0:32, 0:MC], ct, b("bi", 0, 32), A.add, 0.5, A.mult)
     pm = ["pm%d" % r0 for r0, r1 in quads]
-    for r0, r1 in quads[1:]:
-        copy(["pm0", "pm.m"], ["pm%d" % r0], T.pm[r0:r1, :], T.pm[0:32, :])
-    need("g", wr[pm[3]])
+    for r0, r1 in quads:
+        tsc(["ct", "bi2"], ["pn%d" % r0], T.pm[r0:r1, MC:2 * MC], ct, b("bi2", 0, 32), A.add, 0.5, A.mult)
+    for r0, r1 in quads:
+        tsc(["ct", "bi"], ["pm%d" % r0], T.pm[r0:r1, 0:MC], ct, b("bi", 0, 32), A.add, 0.5, A.mult)
+    need("g", wr["pn96"])
     spread("aM", lambda d: (T.pm[:, MC + lc(at(d, me)):MC + lc(at(d, me)) + 3], T.meta[:, 3 * at(me, d):3 * at(me, d) + 3]),
            near="aN")
 
@@ -418,8 +426,7 @@ def rank_program(g, core, T, topo):
         of, w = T.pm[:, lc(k0):lc(k1 - 1) + 3], slice(16 * lc(k0), 16 * lc(k1 - 1) + E)
         copy(["qo"] + pm, ["sn%d" % k0], T.sn[:, w].bitcast(dt.uint32), b("qo").bitcast(dt.uint32).indirect(of))
         copy(["qo"] + pm, ["sns%d" % k0], T.sns[:, w], b("qos").indirect(of), "a")
-    used = [x for d in others for x in engines(core, cores[d])]
-    spare = [x for x in topo.engines(core, helper(me)) if x not in used]
+    spare = [x for d in others[4:] for x in engines(core, cores[d])]
     need("g", wr["sn0"] + wr["sns0"])
     spread("aC", lambda d: [x.bitcast(dt.uint8) for x in piece("sn", "fw", d)], others[0:4],
            [write(helper(me), spare[0:RE], "aR", T.sns[:, 0:4 * E], b("rls"))])
@@ -433,12 +440,6 @@ def rank_program(g, core, T, topo):
     arrive("aC", "fw.far")
     arrive("aS", "fws.far")
 
-    gk = ["g2", "g2.1", "g2.2", "g2.3"]
-    flip(gk, ["tr"], T.tr[:, 0:128], T.g2[:, 0:128])
-    sb("emw", "ale", 0.0, A.is_lt, float(NO), A.mult)
-    tt(["tr"] + ["d2%d" % a for a in range(4)], ["t3"], b("t3"), T.tr[:, AD:128:16], b("d2"), A.add)
-    tt(["idm"], ["emw"], b("emw", 64, 96), b("emw", 64, 96), T.idm[64:96, :], A.max)
-    copy(["t3"], ["ofw"], b("ofw"), b("t3"))
     copy(["ofw"] + gk, X, b("xt").indirect(b("ofw")), T.g2[:, 0:128])
     copy(X[0:2] + ["gr"], ["x3"], b("x3"), T.xt[:, 0:NP].indirect(b("gr")), "a")
     tt(["idw", "emw"], ["idi"], b("idi", 0, 96), b("idw", 0, 96), b("emw", 0, 96), A.max)
@@ -446,12 +447,11 @@ def rank_program(g, core, T, topo):
     copy(["meta4", "sl"], ["slot", "slot.own", "slot.z"], b("slot").indirect(T.meta[:, 12:21]), T.sl[:, 4 * E:(N - 1) * E])
     flip(["x3"], ["x3t"], b("x3t"), b("x3"))
     tt(["x3t"], ["x3a"], b("x3a", 0, 64), T.x3t[0:64, 0:P:32], T.x3t[64:128, 0:P:32], A.max)
-    tt(["x3a", "emw"], ["x3b"], b("x3b", 0, 32), b("x3a", 32, 64), b("emw", 96, 128), A.max)
-    tt(["x3a", "x3b"], ["idi3"], b("idi", 96, 128), b("x3a", 0, 32), b("x3b", 0, 32), A.max)
+    tt(["x3a"], ["idi3"], b("idi", 96, 128), b("x3a", 0, 32), b("x3a", 32, 64), A.max)
     tsc(["idi", "idi3"], ["idj"], b("idj"), b("idi"), TAG - 1, A.bitwise_and)
+    copy(["meta0", "sl"], ["slot", "slot.own", "slot.z"], b("slot").indirect(T.meta[:, 0:12]), T.sl[:, 0:4 * E])
     for h in range(2):
         copy(["idj"], ["idu%d" % h], T.idu[:, h:16:2], b("idj"))
-    copy(["meta0", "sl"], ["slot", "slot.own", "slot.z"], b("slot").indirect(T.meta[:, 0:12]), T.sl[:, 0:4 * E])
     copy(["slot", "slot.own", "slot.z", "idu0", "idu1"], ["gs"], b("gs"), b("slot").indirect(b("idu")), "a")
     pack(1, 3)
     pack(3, 4)
@@ -476,8 +476,9 @@ def rank_program(g, core, T, topo):
     def out(i, e):
         w = slice(P * i, P * i + P)
         copy(["acc%d" % i], ["ys%d" % i], T.ys[:, w], T.acc[:, 512 * i:512 * i + P], e)
-        dma("y", "dy", 16 * R * O, ["ys%d" % i], ["y%d" % i], T.y[:, w], T.ys[:, w])
+        dma("y", "dy", NS, ["ys%d" % i], ["y%d" % i], T.y[:, w], T.ys[:, w])
 
+    NS = 16 * R * O
     for t in range(R):
         products(t)
         if t == R - 2:
@@ -485,5 +486,5 @@ def rank_program(g, core, T, topo):
             out(1, "v")
     for i in range(2, R * O):
         out(i, "av"[i % 2])
-    need("y", [("dy", 16 * R * O)])
+    need("y", [("dy", NS)])
     need("g", [("lsent", sent[0])])

@@ -3,22 +3,26 @@ from concourse.mybir import dt, AluOpType as A, ActivationFunctionType as F, Axi
 
 N, P, V, R, O = 8, 256, 64, 4, 2
 CH = N * V
+HC = CH // 2
 NP = N * P
 AD, AY = 15, 14
 E = 48
 IT = P + V
-NI = IT + E
-SI = NI
+NI = IT + 16
+NC = IT
+SI = 384
 NO = N * SI
-ZC = NI - 8
 TAG = 4096
 LC = 25
 MC = 26
 WW = NI + (N - 1) * E
 RE = 4
 BIG = 1.0e9
+LEAVE = ["", "v", "v", "avavav"]
+STORES = [0, 1, 3, 5, 7, 8]
 
-SCRATCH = {"lists": ("dram", [8, 128, 4], "float32"), "acc": ("psum", [128, 4096], "float32")}
+SCRATCH = {"lists": ("dram", [8, 128, 4], "float32"), "pfo": ("dram", [9, 128, 3], "bfloat16"), "pfi": ("dram", [8, 128, 3], "bfloat16"),
+           "acc": ("psum", [128, 4096], "float32")}
 POOL = {}
 
 
@@ -36,19 +40,19 @@ def _pool(buf, dtype, **cols):
     SCRATCH[buf] = ("sbuf", [128, a], dtype)
 
 
-_sb("int32", src=28, ale=8, pi=1, dd=32, gli=16, gri=16)
-_sb("float32", ydf=128, yid=128, x3=P, x3t=P, sv=8, k4=8, jm=144, ne=80, n1=64, n2=64, g0=CH, g1=CH, g2=CH, tr=CH, f1f=32, v1=CH, xt=3 * NP, yt=NP, xs=3 * P, th=IT, thr=80, kk=64, kt=64,
-    cnt=32, ct=32, slot=NO + 8, sl=(N - 1) * E, idw=8, idm=8, gs=P, gt=P, ys=2048)
-_sb("uint16", of1=32, ofq=32, ofz=32, ofw=8, gl=20, gr=16, ow=20, pm=2 * MC, meta=3 * (N - 1), idu=16, so=64)
-_sb("bfloat16", cv=4 * NI, wt=4096, ones=NI, m2q=IT, mk=NI, pf=NI, ja=2 * NI, jv=2 * NI)
-_sb("float16", jh=2 * NI)
-_sb("float8_e4m3fn_x4", wq=1024, qo=NI, sn=16 * LC, fw=WW, pk0=P, pk1=P, pk2=P, pk3=P)
+_sb("int32", src=28, pi=1, dd=32, gli=16)
+_sb("float32", ydf=128, yid=128, x3=P, x3t=P, sv=8, k4=8, jm=144, ne=80, n1=64, n2=64, g0=HC, g1=HC, g2=CH, g3=128, g4=128, tr=HC, tr1=HC,
+    tr2=128, f1f=16, v1=CH, xt=3 * NP, th=IT, thr=80, kk=64, kt=64, cnt=32, ct=32, idb=16, idn=16, ga=64, ys=2048)
+_sb("uint16", of1=32, ofq=16, of2=16, ofz=32, ofw=8, go=40, pm=MC, idu=16, so=64)
+_sb("bfloat16", cv=4 * NI, wt=4096, m2q=IT, mh=IT, mk=NC, pf=SI, ja=2 * NC, jv=2 * NC, tab=NO + 16, lo=SI, gs=P, gt=P)
+_sb("float16", jh=2 * NC)
+_sb("float8_e4m3fn_x4", wq=1024, qo=NI, sn=16 * LC, rlc=2 * E, fw=WW, pk0=P, pk1=P, pk2=P, pk3=P)
 _sb("uint8", wqs=1024, qos=NI, sns=16 * LC, rls=4 * E, fws=WW, ps0=P, ps1=P, ps2=P, ps3=P)
-_pool("tf", "float32", s1=8, s3=8, m14=1, bc1=1, bc2=1, bc4=1, tag=1, tag3=1, bi=1, bi2=1, a4=1, u0=1, uu=4, emw=8,
-      d2=32, t3=32, x3a=8, em4=4)
-_pool("ti", "int32", b1=8, b2=8, b3=8, p15=1, p3=1, p5=1, rk=24, r1=4, r2=4, idi=8, idj=8)
-SEMAPHORES = ["vv", "aa", "pp", "gq", "lsent", "aL", "aM", "aN", "aC", "aS", "aR", "dsrc", "dcod", "dale", "dcv", "dw0", "dw1", "dfw", "down",
-              "dfan", "dfay", "df1", "dv1", "di", "dm", "dem", "dy"]
+_pool("tf", "float32", s1=8, s3=8, m14=1, bc1=1, bc2=1, bc4=1, tag=1, tag3=1, tg0=1, e14=1, cap=1, odd=1, o4=1, c1=1, c2=1, dl=64, bi=1, bi2=1, a4=1, u0=1, u1=4, uu=4, p6=1,
+      d2=16, t3=16, em=16, hk=16, m3=8, c3=8, b4=8, p4=8)
+_pool("ti", "int32", b1=8, b2=8, b3=8, p15=1, p16=1, p3=1, p5=1, rk=24, r1=4, r2=4, idi=8, idj=8)
+SEMAPHORES = ["vv", "aa", "pp", "gq", "lsent", "aL", "aM", "aC", "aS", "aR", "aQ", "dsrc", "dcod", "dcv", "dw0", "dw1", "dfw", "down",
+              "dfan", "df1", "dv1", "dem", "dlo", "dpf", "dtab", "iss", "dy"]
 
 
 def rank_program(g, core, T, topo):
@@ -56,7 +60,10 @@ def rank_program(g, core, T, topo):
     cores = T.cores
 
     def rest(r):
-        return sorted((d for d in range(N) if d != r), key=lambda d: topo.chip(cores[d]) == topo.chip(cores[r]))
+        on = [d for d in range(N) if topo.chip(cores[d]) == topo.chip(cores[r])]
+        off = [d for d in range(N) if d not in on]
+        k = on.index(r)
+        return off[k:] + off[0:k] + on[0:k] + on[k + 1:]
 
     def at(s, d):
         return rest(d).index(s)
@@ -65,6 +72,12 @@ def rank_program(g, core, T, topo):
         mine = topo.cores_of(cores[s])
         free = [c for c in mine if c not in cores and topo.die(c) != topo.die(cores[s])]
         return free[[c for c in mine if c in cores].index(cores[s])]
+
+    def parts(engines, *sizes):
+        return [engines[sum(sizes[0:k]):sum(sizes[0:k + 1])] for k in range(len(sizes))]
+
+    def raw(x):
+        return x.bitcast(dt.uint8)
 
     def write(to, mask, sem, src, dst):
         rid, pid = topo.addr(to)[0:2]
@@ -75,11 +88,10 @@ def rank_program(g, core, T, topo):
         for s in range(N):
             if helper(s) == core:
                 far = topo.engines(core, cores[rest(s)[0]])
-                g.wait_ge(T.sem.aR, RE)
-                g.remote_dma_fused([write(cores[d], far[2 * k:2 * k + 2], "aS", T.rls[:, E * k:E * k + E],
-                                          T.fws[:, NI + E * at(s, d):NI + E * at(s, d) + E]) for k, d in enumerate(rest(s)[0:4])],
-                                   local_sem=T.sem.lsent)
-                g.wait_ge(T.sem.lsent, 8)
+                g.wait_ge(T.sem.aR, 8)
+                g.remote_dma_fused([write(cores[d], m, "aC", raw(T.rlc[:, E * k:E * k + E]), raw(T.fw[:, NI + E * at(s, d):NI + E * at(s, d) + E]))
+                                    for k, (d, m) in enumerate(zip(rest(s)[0:2], parts(far, 4, 4)))], local_sem=T.sem.lsent)
+                g.wait_ge(T.sem.lsent, len(far))
         return
     others = rest(me)
     OB = P * me
@@ -155,6 +167,9 @@ def rank_program(g, core, T, topo):
     def sb(out, in0, s1, op0, s2=None, op1=None):
         tsc([in0], [out], b(out), b(in0), s1, op0, s2, op1)
 
+    def line(out, in0, scale, bias):
+        op("a", g.scalar.activation, [in0], [out], b(out), b(in0), F.Identity, bias=bias, scale=scale)
+
     def flip(reads, writes, out, in_):
         op("v", g.vector.transpose, reads, writes, out, in_)
 
@@ -165,29 +180,16 @@ def rank_program(g, core, T, topo):
         kw = {"allow_small_or_imprecise_dtypes": True} if f else {}
         op("g", g.iota, [], [key], out, pattern, base, mult, **kw)
 
-    def engines(a, c):
-        off = [k for k in cores if k != a and topo.chip(k) != topo.chip(a)]
-        on = [k for k in cores if k != a and topo.chip(k) == topo.chip(a)]
-        far = topo.engines(a, off[0])
-        if c in off:
-            n, k = len(far) // len(off), off.index(c)
-            return far[n * k:n * k + n]
-        near = [x for x in topo.engines(a, c) if x not in far]
-        k = on.index(c)
-        return near[2 * k:2 * k + 2]
-
+    far = topo.engines(core, cores[others[0]])
+    near = [x for x in topo.engines(core, cores[others[-1]]) if x not in far]
     sent = [0]
 
-    def spread(sem, piece, to=others, more=(), near=None):
-        ts = list(more)
-        for d in to:
-            src, dst = piece(d)
-            sent[0] += len(engines(core, cores[d]))
-            ts.append(write(cores[d], engines(core, cores[d]), near if near and d in others[4:] else sem, src, dst))
-        g.remote_dma_fused(ts, local_sem=T.sem.lsent)
+    def spread(sem, piece, to, masks):
+        sent[0] += sum(len(m) for m in masks)
+        g.remote_dma_fused([write(cores[d], m, sem, *piece(d)) for d, m in zip(to, masks)], local_sem=T.sem.lsent)
 
-    def arrive(sem, key, of=others):
-        wr[key] = [(sem, sum(len(engines(cores[s], core)) for s in of))]
+    def arrive(sem, key, sizes):
+        wr[key] = [(sem, sum(sizes[at(me, s)] for s in others))]
 
     def lc(k):
         return 3 * k + (4 if k >= 4 else 0)
@@ -195,14 +197,14 @@ def rank_program(g, core, T, topo):
     def load_w(e, h):
         dma(e, "dw%d" % h, 16, [], ["wt%d" % h], T.wt[:, 2048 * h:2048 * h + 2048], T.w[:, 2048 * h:2048 * h + 2048])
 
-    def pack(t0, t1):
-        a, c = 128 * O * t0, 128 * O * t1
-        op("v", g.vector.quantize_mx, ["wt0", "wt1"], ["wq%d" % t for t in range(t0, t1)], T.wq[:, a:c], T.wqs[:, a:c],
+    def pack(i0, i1):
+        a, c = 128 * i0, 128 * i1
+        op("v", g.vector.quantize_mx, ["wt0", "wt1"], ["wq%d" % i for i in range(i0, i1)], T.wq[:, a:c], T.wqs[:, a:c],
            T.wt[:, 4 * a:4 * c])
 
     quads = [(32 * a, 32 * a + 32) for a in range(4)]
 
-    ns = 16 * 17
+    ns = 16 * 15
     for h in range(2):
         dma("y", "dsrc", ns, [], ["src"], T.src[32 * h:32 * h + 32, 0:4], T.alt[:, 8 * h:8 * h + 8])
     for c in range(4):
@@ -213,10 +215,9 @@ def rank_program(g, core, T, topo):
         dma("a", "dsrc", ns, [], ["src"], T.src[80:96, c:c + 1], T.f1[4 * x:4 * x + 4, :])
         dma("y", "dsrc", ns, [], ["src"], T.src[112 + 4 * c:116 + 4 * c, 0:4], T.f2[4 * x:4 * x + 4, :])
     for h in range(2):
-        dma("ya"[h], "dsrc", ns, [], ["src"], T.src[16 * h:16 * h + 16, 4:8], T.f1[:, :])
-    for h in range(2):
-        dma("y", "dcod", 64, [], ["cod"], T.src[16 * h:16 * h + 16, 8:24], T.alt[:, :])
-        dma("y", "dcod", 64, [], ["cod"], T.src[16 * h:16 * h + 16, 24:28], T.f2[:, :])
+        dma("y", "dcod", 96, [], ["cod"], T.src[16 * h:16 * h + 16, 8:24], T.alt[:, :])
+        dma("y", "dcod", 96, [], ["cod"], T.src[16 * h:16 * h + 16, 4:8], T.f1[:, :])
+        dma("y", "dcod", 96, [], ["cod"], T.src[16 * h:16 * h + 16, 24:28], T.f2[:, :])
     dma("y", "dcv", 32, [], ["cv.c"], T.cv[:, 0:4 * P], T.c[:, :])
     dma("y", "dcv", 32, [], ["cv.c"], T.cv[:, 4 * P:4 * IT], T.v[:, :])
 
@@ -224,52 +225,64 @@ def rank_program(g, core, T, topo):
     iota("ydf", b("ydf"), [[7, 16], [-15, 8]], 0, 0)
     iota("yid", b("yid"), [[1, 16], [16, 8]], 0, 0)
     iota("k4", b("k4"), [[1, 8]], NP + OB, 4)
-    fill("yt", T.yt[:, 0:128], -float(TAG))
-    fill("src.z", T.src[32:64, 4:28], 0)
-    fill("src.z2", T.src[64:128, 4:28], 0)
-    sb("p15", "pi", 0x6F, A.bitwise_and)
+    fill("xt", T.xt[64:128, 0:128], -float(TAG))
+    sb("p15", "pi", 0x4F, A.bitwise_and)
     sb("m14", "p15", float(AY), A.is_ge)
-    fill("v1", T.v1[:, 0:V], -float(TAG))
-    tsc(["m14"], ["ydf"], b("ydf", 0, 32), b("ydf", 0, 32), b("m14", 0, 32), A.mult)
+    tsc(["m14"], ["ydf"], b("ydf", 0, 64), b("ydf", 0, 64), b("m14", 0, 64), A.mult)
     for n in (1, 2, 4):
-        sb("bc%d" % n, "m14", float(n * (P - SI)), A.mult, float(n * SI), A.add)
-    tt(["ydf", "yid"], ["yt"], T.yt[0:32, 0:128], b("ydf", 0, 32), b("yid", 0, 32), A.add)
-    sb("tag", "m14", -2.0 * TAG, A.mult, 2.0 * TAG, A.add)
-    sb("p3", "pi", 3, A.bitwise_and)
-    sb("p5", "pi", 5, A.arith_shift_right)
-    fill("cv.z", T.cv[:, 4 * IT:4 * NI], 0.0)
-    iota("v1", T.v1[0:32, 0:V], [[1, 16], [16, 4]], TAG + P, 0)
+        line("bc%d" % n, "m14", float(n * (P - SI)), float(n * SI))
+    tt(["ydf", "yid"], ["xt"], T.xt[0:64, 0:128], b("ydf", 0, 64), b("yid", 0, 64), A.add)
+    iota("idb", b("idb", 0, 32), [[16, 16]], SI * me, 1)
+    iota("v1", T.v1[:, 0:V], [[1, 16], [16, 4]], TAG + P, 0)
+    iota("dl", b("dl"), [[0, 2], [-2, 2], [0, 16]], 1, 0)
     iota("dd", b("dd"), [[16, 32]], 0, 1, False)
 
-    sk = ["src", "src.z", "src.z2"]
-    tsc(sk, ["b1"], b("b1"), T.src[:, 0:8], 0xF80, A.bitwise_and)
-    tsc(sk, ["b2"], b("b2"), T.src[:, 0:8], 4, A.arith_shift_right, 7, A.bitwise_and)
-    tsc(sk, ["b3"], b("b3"), T.src[:, 0:8], 15, A.bitwise_and)
-    tb("s1", "b1", "b2", A.add)
-    sb("s3", "b3", 8.0, A.mult)
+    def bits(key, r1, c0):
+        x, k = T.src[0:r1, c0:c0 + 4], str(c0)
+        tsc([key], ["b1" + k], b("b1", 0, r1, c0, c0 + 4), x, 0xF80, A.bitwise_and)
+        tsc([key], ["b2" + k], b("b2", 0, r1, c0, c0 + 4), x, 4, A.arith_shift_right, 7, A.bitwise_and)
+        tsc([key], ["b3" + k], b("b3", 0, r1, c0, c0 + 4), x, 15, A.bitwise_and)
+
+    def sums(r1, c0):
+        k = str(c0)
+        tt(["b1" + k, "b2" + k], ["s1" + k], b("s1", 0, r1, c0, c0 + 4), b("b1", 0, r1, c0, c0 + 4), b("b2", 0, r1, c0, c0 + 4), A.add)
+        tsc(["b3" + k], ["s3" + k], b("s3", 0, r1, c0, c0 + 4), b("b3", 0, r1, c0, c0 + 4), 8.0, A.mult)
+
+    bits("src", 128, 0)
+    sums(128, 0)
     for j in range(4):
-        tsc(["s1", "s3", "k4"], ["sv"] if j == 3 else [], T.sv[:, j:j + 1], b("s1", 0, 128, j, j + 1), b("s3", 0, 128, j, j + 1), A.add,
+        tsc(["s10", "s30", "k4"], ["sv"] if j == 3 else [], T.sv[:, j:j + 1], b("s1", 0, 128, j, j + 1), b("s3", 0, 128, j, j + 1), A.add,
             T.k4[:, j:j + 1], A.min)
-    tt(["s1", "s3"], ["sv.v"], T.sv[:, 4:8], b("s1", 0, 128, 4, 8), b("s3", 0, 128, 4, 8), A.add)
     need("g", wr["sv"])
-    spread("aL", lambda d: (T.sv[:, 0:4], T.lists[me]))
+    spread("aL", lambda d: (T.sv[:, 0:4], T.lists[me]), others, parts(far, 2, 2, 2, 2) + parts(near, 2, 2, 2))
     dma("y", "down", 16, ["sv"], ["lown"], T.lists[me], T.sv[:, 0:4])
 
-    def double(buf, e, sizes):
-        for n in sizes:
-            plus = 128.0 if n == 128 else b("bc%d" % (n // P))
-            copy([buf, "bc1", "bc2", "bc4"], [buf], T[buf][:, n:2 * n], T[buf][:, 0:n], e, plus)
-
-    wr["yb"] = wr["yt"]
-    double("yt", "a", (128, 256, 512, 1024))
-    copy(["yb"], ["xt"], T.xt[:, 0:128], T.yt[:, 0:128])
-    double("xt", "v", (128, 256, 512))
-    copy(["yb"], ["x1", "yb"], T.xt[:, NP:NP + 128], T.yt[:, 0:128], "v", float(NP))
+    for n in (128, 256, 512, 1024):
+        plus = 128.0 if n == 128 else b("bc%d" % (n // P))
+        copy(["xt", "bc1", "bc2", "bc4"], ["xt"], T.xt[:, n:2 * n], T.xt[:, 0:n], "a", plus)
+        if n == 128:
+            wr["xb"] = wr["xt"]
+    full = wr["xt"]
+    tsc(["cod"], ["em"], b("em", 0, 32), T.src[0:32, 8:24], 0.0, A.is_lt, float(NO), A.mult)
+    sb("p16", "pi", 16, A.bitwise_and)
+    sb("p5", "pi", 32, A.bitwise_and)
     fill("kk", b("kk"), 99.0)
     wr["kd"] = wr["kk"]
     fill("gli", b("gli"), 0)
-    fill("gri", b("gri"), 0)
-    copy(["yt"], ["xh"], T.xt[:, 1024:NP], T.yt[:, 1024:NP], "a")
+    tt(["em", "idb"], ["idn"], b("idn", 0, 32), b("em", 0, 32), b("idb", 0, 32), A.max)
+    sb("o4", "p16", 0.25, A.mult)
+    sb("c1", "p5", 4 * SI / 32.0, A.mult)
+    sb("c2", "p5", -8 * SI / 32.0, A.mult, 4.0 * SI, A.add)
+    sb("cap", "m14", -16.0 * TAG, A.mult, 15.0 * TAG, A.add)
+    copy(["xb"], ["x1"], T.xt[:, NP:NP + 256], T.xt[:, 0:256], "v", float(NP))
+    seed = wr["x1"]
+    sb("tag", "m14", -2.0 * TAG, A.mult, 2.0 * TAG, A.add)
+    sb("e14", "p15", float(AY), A.is_equal, float(TAG), A.mult)
+    copy(["tag", "e14"], ["tg0"], b("tg0"), b("e14"), "a", b("tag"))
+    need("y", full + seed)
+    for p in (0, 16, 48):
+        for h in range(2):
+            dma("y", "dem", 96, ["idn"], ["xe"], T.xt[p:p + 1, OB + 128 * h:OB + 128 * h + 128], T.idn[0:16, 8 * h:8 * h + 8])
 
     iota("jm.0", T.jm[:, 0:16], [[1, 16]], 0, 0)
     iota("jm.1", T.jm[:, 16:80], [[0, N], [1, N]], 0, 0)
@@ -283,185 +296,200 @@ def rank_program(g, core, T, topo):
         kkeys += ["kd%d" % k0, "kk%d" % k0]
     for r1, base in ((32, OB - 128), (16, OB)):
         iota("gli", b("gli", 0, r1), [[128, 2], [1, 8]], base, 8, False)
-    for r0, r1 in quads:
-        need("g", [(csem["g"], cnt["g"])])
-        iota("gri", b("gri", r0, r0 + 16), [[1, 8], [128, 2]], OB, 8, False)
-    need("g", wr["gri"])
-    iota("mk.z", T.mk[:, IT:NI], [[0, E]], 1, 0)
-    iota("ones", b("ones"), [[0, NI]], 1, 0)
-    iota("slot.z", T.slot[:, NO:NO + 8], [[0, 8]], ZC, 0)
-    iota("slot.own", T.slot[:, SI * me:SI * me + IT], [[1, IT]], 0, 0)
-    iota("sl", b("sl"), [[1, (N - 1) * E]], NI, 0)
+    need("g", wr["gli"])
+    iota("pf.z", T.pf[:, IT:SI], [[0, SI - IT]], 0, 0)
+    iota("lo", b("lo", 0, 32), [[0, SI // 16], [1, 16]], 1, 0)
+    iota("tab.z", T.tab[:, NO:NO + 16], [[0, 16]], IT // 2 + 4, 0)
+    iota("tab%d" % me, T.tab[:, SI * me:SI * me + IT], [[16, IT // 16], [0, 16]], 0, 0)
+    for s in others:
+        iota("tab%d" % s, T.tab[:, SI * s:SI * s + IT], [[0, IT]], NI + E * at(s, me), 0)
+    tabs = ["tab%d" % s for s in range(N)]
 
-    for n in (1, 2, 4):
-        copy(["v1"], ["v1"], T.v1[:, V * n:2 * V * n], T.v1[:, 0:V * n], "v", float(n * SI))
+    tsc(["dl", "o4"], ["dl"], b("dl"), b("dl"), b("o4"), A.mult)
+    tsc(["cap", "c1"], ["v1"], T.v1[:, 0:V], T.v1[:, 0:V], b("c1"), A.add, b("cap"), A.min)
+    fill("cv.z", T.cv[:, 4 * IT:4 * NI], 0.0)
+    tt(["dl", "v1"], ["v1"], T.v1[:, 0:V], T.v1[:, 0:V], b("dl"), A.add)
     for nm in ("of1", "ofq", "ofz"):
-        copy(["dd"], [nm], b(nm), b("dd"))
-    tsc(sk + ["cod"], ["rk"], b("rk"), T.src[:, 4:28], 8, A.arith_shift_right, 15, A.bitwise_and)
-    copy([], ["rk"], b("rk", 32, 64), b("rk", 0, 32))
-    tsc(["rk"], ["r1"], b("r1"), b("rk", 0, 128, 0, 4), float(N), A.mult, 16.0, A.add)
-    copy(["rk"], ["ow.c"], T.ow[:, 0:16], b("rk", 0, 128, 4, 20))
-    tt(["rk", "r1"], ["r2"], b("r2"), b("rk", 0, 128, 20, 24), b("r1"), A.add)
-    copy(["r2"], ["ow.2"], T.ow[:, 16:20], b("r2"))
-    copy(["sv.v"], ["gl.v"], T.gl[:, 16:20], T.sv[:, 4:8])
+        copy(["dd"], [nm], b(nm, 64, 128), b("dd", 64, 128, 0, POOL[nm][2]))
+    tsc(["cod"], ["rk"], b("rk", 0, 32), T.src[0:32, 4:28], 8, A.arith_shift_right, 15, A.bitwise_and)
+    bits("cod", 32, 4)
+    copy(["v1"], ["v1"], T.v1[:, V:2 * V], T.v1[:, 0:V], "v", float(SI))
+    sums(32, 4)
+    tsc(["rk"], ["r1"], b("r1", 0, 32), b("rk", 0, 32, 0, 4), float(N), A.mult, 16.0, A.add)
+    copy(["rk"], ["ow.c"], T.go[0:32, 20:36], b("rk", 0, 32, 4, 20))
+    copy(["v1"], ["v1"], T.v1[:, 2 * V:4 * V], T.v1[:, 0:2 * V], "v", float(2 * SI))
+    tt(["rk", "r1"], ["r2"], b("r2", 0, 32), b("rk", 0, 32, 20, 24), b("r1", 0, 32), A.add)
+    tt(["s14", "s34"], ["sv.v"], T.sv[0:32, 4:8], b("s1", 0, 32, 4, 8), b("s3", 0, 32, 4, 8), A.add)
+    copy(["v1", "c2"], ["v1"], T.v1[:, 4 * V:8 * V], T.v1[:, 0:4 * V], "v", b("c2"))
+    copy(["sv.v"], ["gl.v"], T.go[0:32, 16:20], T.sv[0:32, 4:8])
+    copy(["r2"], ["ow.2"], T.go[0:32, 36:40], b("r2", 0, 32))
     op("v", g.vector.quantize_mx, ["cv.z", "cv.c"], ["qo"], b("qo"), b("qos"), b("cv"))
 
-    arrive("aL", "lfar")
+    arrive("aL", "lfar", [2] * 7)
     lk = ["lfar", "lown"]
-    for r in range(N):
-        dma("ya"[r % 2], "df1", 128, lk, ["f1f"], T.f1f[0:32, 4 * r:4 * r + 4], T.lists[r, 64:96, :])
-    for h in range(2):
+    for r in range(4):
+        dma("ya"[r % 2], "df1", 64, lk, ["f1f"], T.f1f[0:64, 4 * r:4 * r + 4], T.lists[r:N:4, 64:96, :])
+    for h in range(4):
         p = 16 * h + AD
-        dma("ya"[h], "dfan", 32, lk, ["xt", "xh"], T.xt[p:p + 1, 0:NP], T.lists[:, 0:64, :])
-        dma("ya"[h], "dv1", 32, lk, ["v1"], T.v1[p:p + 1, :], T.lists[:, 96 + 16 * h:112 + 16 * h, :])
-        p = 16 * h + AY
-        dma("ya"[h], "dfay", 32, lk, ["yt", "yb"], T.yt[p:p + 1, :], T.lists[:, 0:64, :])
-    for n in (128, 256, 512):
+        need("ya"[h % 2], seed)
+        dma("ya"[h % 2], "dfan", 64, lk, ["xt"], T.xt[p:p + 1, 0:NP], T.lists[:, 0:64, :])
+    for h in range(2):
+        p, w = 16 * h + AD, slice(96 + 16 * h, 112 + 16 * h)
+        dma("y", "dv1", 96, lk, ["v1"], T.v1[p:p + 1, :], T.lists[:, w, :])
+        for a in range(2):
+            dma("y", "dv1", 96, lk, ["v1"], T.v1[32 + p:33 + p, HC * a:HC * a + HC], T.lists[4 - 4 * a:8 - 4 * a, w, :])
+    for n in (256, 512):
         copy([], ["x1"], T.xt[:, NP + n:NP + 2 * n], T.xt[:, NP:NP + n], "a", float(n))
-    need("y", wr["yt"])
+    need("y", wr["v1"])
     load_w("y", 0)
     load_w("y", 1)
-    for h in range(6):
-        dma("y", "dale", 96, [], ["ale"], T.ale[16 * h:16 * h + 16, :], T.alt[:, 8 * (h % 2):8 * (h % 2) + 8])
+    dma("y", "dlo", 16, ["lo"], ["pfown"], T.pfi[me], b("lo", 0, 1))
 
-    X = ["xt", "xh", "x1", "x2"]
-
-    def step(keys, table, of, gm):
-        copy(keys + [of, "tag"], [gm], b(gm), table.indirect(b(of)), "a", b("tag"))
-
-    def turn(gm, row, of):
-        flip([gm], ["tr"], T.tr[0:32, :], T[gm][0:32, :])
-        copy(["tr"], [of], b(of, 0, 32), T.tr[0:32, row:CH:16])
-
-    def put(n, of, val):
-        copy([of, val], X[0:2 * n], T.xt[:, 0:NP * n].indirect(b(of)), b(val))
-
-    copy(["f1f"], ["of1"], b("of1", 0, 32), b("f1f", 0, 32))
-    step(["yt"], b("yt"), "of1", "g0")
-    put(1, "of1", "v1")
+    X = ["xt", "xe", "x1", "x2"]
+    copy(["f1f"], ["og"], b("of1", 0, 64, 0, 16), b("f1f", 0, 64))
+    for a in range(2):
+        copy(["f1f"], ["of1%d" % a], b("of1", 32 * a, 32 * a + 32, 16, 32), b("f1f", 32 - 32 * a, 64 - 32 * a))
+    copy(X[0:2] + ["of1", "og", "tg0"], ["g0"], b("g0"), T.xt[:, 0:NP].indirect(T.of1[:, 0:16]), "a", b("tg0"))
     copy(["x1"], ["x2"], T.xt[:, NP + 1024:2 * NP], T.xt[:, NP:NP + 1024], "a", 1024.0)
-    copy(X[0:2], ["xs0"], T.xs[0:1, 0:P], T.xt[0:1, OB:OB + P], "a")
-    dma("y", "di", 48, ["xs0"], ["idw"], T.idw[0:32, :], T.xs[0:1, 0:P])
-    turn("g0", AY, "ofq")
-    step(X, b("xt"), "ofq", "g1")
-    tsc(["tr"], ["d2"], b("d2", 0, 32), T.tr[0:32, AY:CH:16], float(NP), A.is_ge, float(NP), A.mult)
-    copy(["gli"], ["gl.c"], T.gl[:, 0:16], b("gli"))
-    copy(["gri"], ["gr"], b("gr"), b("gri"))
-    tt(["tr", "d2"], ["t3"], b("t3", 0, 32), T.tr[0:32, AY:CH:16], b("d2", 0, 32), A.add)
-    copy(["gl.c", "gl.v"], ["gl.2"], T.gl[32:64, :], T.gl[0:32, :])
     flip(kkeys, ["kt"], b("kt"), b("kk"))
+    copy(["gli"], ["gl.c"], T.go[0:32, 0:16], b("gli", 0, 32))
+    sb("p3", "pi", 3, A.bitwise_and)
+    sb("p6", "pi", 64.0, A.is_ge, 4.0, A.mult)
     dcol = T.kt[:, 32:33]
     tsc(["jm", "kt"], ["ne"], b("ne"), T.jm[:, 0:80], dcol, A.not_equal, BIG, A.mult)
     tsc(["jm", "kt"], ["n1"], b("n1"), T.jm[:, 80:144], dcol, A.not_equal)
-    sb("bi", "p3", 2.0, A.is_lt, float(NI), A.mult)
-    tsc(["src"], ["em4"], b("em4", 0, 64), T.src[0:64, 0:4], 0.0, A.is_lt, float(NO), A.mult)
+    flip(["g0"], ["tr"], T.tr[0:64, :], T.g0[0:64, :])
     tsc(["ne"], ["n2"], b("n2"), b("ne", 0, 128, 16, 80), 2 * TAG - 0.5, A.add)
-    sb("a4", "p5", 4.0, A.mult, 0.5, A.add)
-    copy(["t3"], ["of1"], b("of1", 0, 32), b("t3", 0, 32))
+    copy(["tr"], ["ofq0"], b("ofq", 0, 64), T.tr[0:64, AD:HC:16])
+    copy(["of1", "og", "of10", "of11", "v1"], X[0:2], T.xt[:, 0:NP].indirect(b("of1")), b("v1"))
+    copy(X + ["ofq", "ofq0", "tag"], ["g1"], b("g1"), b("xt").indirect(b("ofq")), "a", b("tag"))
+    tsc(["tr"], ["d2"], b("d2", 0, 64), T.tr[0:64, AD:HC:16], float(NP), A.is_ge, float(NP), A.mult)
+    gk = ["gl.c", "gl.v", "ow.c", "ow.2"]
+    for r0, r1 in quads[1:]:
+        copy(gk, ["go%d" % r0], T.go[r0:r1, :], T.go[0:32, :])
+    gk += ["go32", "go64", "go96"]
+    tt(["tr", "d2"], ["t3"], b("t3", 0, 64), T.tr[0:64, AD:HC:16], b("d2", 0, 64), A.add)
     tt(["n1", "n2"], ["thr.2"], T.thr[:, 16:80], b("n1"), b("n2"), A.mult)
-    copy(["g1"], ["g0"], T.g0[32:64, :], T.g1[0:32, :], "a", 4.0 * TAG)
-    flip(["g1"], ["tr"], T.tr[0:32, :], T.g1[0:32, :])
-    copy(["tr"], ["of1"], b("of1", 32, 64), T.tr[0:32, AD:CH:16])
-    put(3, "of1", "g0")
+    copy(["t3"], ["of2a"], b("of2", 0, 64), b("t3", 0, 64))
+    copy(["g1"], ["g0"], T.g0[64:128, :], T.g1[0:64, :], "a", 4.0 * TAG)
+    flip(["g1"], ["tr1"], T.tr1[0:64, :], T.g1[0:64, :])
+    tsc(["p5", "p6"], ["a4"], b("a4"), b("p5"), 0.25, A.mult, b("p6"), A.add)
+    copy(["tr1"], ["of2b"], b("of2", 64, 128), T.tr1[0:64, AD:HC:16])
+    copy(["tr1"], ["ofz0"], b("ofz", 0, 64, 0, 16), T.tr1[0:64, AD:HC:16])
+    copy(["of2a", "of2b", "g0"], X, b("xt").indirect(b("of2")), b("g0"))
     copy(["ne"], ["thr.c"], T.thr[:, 0:16], b("ne", 0, 128, 0, 16), "a", TAG - 0.5)
+    copy(["thr.c", "thr.2"] + gk, ["th"], b("th"), b("thr").indirect(T.go[:, 20:40]), "a")
     copy(["kt", "a4"], ["u0"], b("u0"), T.kt[:, 0:1], "a", b("a4"))
-    copy(["bi"], ["bi2"], b("bi2"), b("bi"), "a", 2.0 * SI * me)
     op("a", g.scalar.activation, ["tag"], ["tag3"], b("tag3"), b("tag"), F.Identity, scale=4.0)
-    copy(["jm", "u0"], ["uu"], b("uu"), T.jm[:, 0:4], "a", b("u0"))
+    op("a", g.scalar.activation, ["o4"], ["odd"], b("odd"), b("o4"), F.Identity, scale=NP / 4.0)
+    copy(["jm", "u0"], ["u1"], b("u1"), T.jm[:, 0:4], "a", b("u0"))
+    copy(["u1"], ["uu"], b("uu"), b("u1"), "a", 0.5)
     dma("y", "dfw", 32, ["qo"], ["fw.own"], T.fw[:, 0:NI].bitcast(dt.uint8), b("qo").bitcast(dt.uint8))
     dma("y", "dfw", 32, ["qo"], ["fw.own"], T.fws[:, 0:NI], b("qos"))
-    copy(["thr.c", "thr.2", "ow.c", "ow.2"], ["th"], b("th"), b("thr").indirect(b("ow")), "a")
-    copy(X[0:2], ["xs1"], T.xs[0:64, P:2 * P], T.xt[0:64, OB:OB + P], "a")
-    for t in (1, 2):
-        dma("y", "di", 48, ["xs1"], ["idw"], T.idw[32 * t:32 * t + 32, :], T.xs[0:1, P:2 * P])
-    dma("y", "dm", 16, ["xs1"], ["idm"], T.idm[64:96, :], T.xs[32:33, P:2 * P])
 
-    tt(X[0:2] + ["gl.c", "gl.v", "gl.2", "th"], ["m2q"], b("m2q"), T.xt[:, 0:NP].indirect(b("gl")), b("th"), A.is_gt)
-    copy(["tr"], ["ofz"], b("ofz", 0, 32), T.tr[0:32, AD:CH:16])
-    copy(X + ["ofz", "tag3"], ["g2"], b("g2"), b("xt").indirect(b("ofz")), "a", b("tag3"))
-    dma("y", "dem", 16, ["em4"], X, T.xt[96:97, OB:OB + P], b("em4", 0, 64))
-    tt(["m2q"], ["mk"], T.mk[0:32, 0:IT], b("m2q", 0, 32), b("m2q", 32, 64), A.max)
+    for a in range(2):
+        copy(["tr1"], ["ofz%d" % (a + 1)], b("ofz", 32 * a, 32 * a + 32, 16, 32), T.tr1[32 - 32 * a:64 - 32 * a, AD:HC:16])
+    tt(X[0:2] + gk + ["th"], ["m2q"], b("m2q"), T.xt[:, 0:NP].indirect(T.go[:, 0:20]), b("th"), A.is_gt)
+    copy(X + ["ofz", "ofz0", "ofz1", "ofz2", "tag3"], ["g2"], b("g2"), b("xt").indirect(b("ofz")), "a", b("tag3"))
+    sb("bi", "p3", 2.0, A.is_lt, float(NC), A.mult)
+    tt(["m2q"], ["mh"], b("mh", 0, 64), b("m2q", 0, 64), b("m2q", 64, 128), A.max)
+    tt(["mh"], ["mk"], b("mk", 0, 32, 0, IT), b("mh", 0, 32), b("mh", 32, 64), A.max)
     for r0, r1 in quads:
-        op("v", g.vector.tensor_tensor_scan, ["ones", "mk", "mk.z"], ["pf%d" % r0], T.pf[r0:r1, :], T.ones[0:32, 0:NI],
-           T.mk[0:32, :], 0.0, A.mult, A.add)
-    tsc(["ale"], ["emw"], b("emw", 0, 96), b("ale", 0, 96), 0.0, A.is_lt, float(NO), A.mult)
-    for a in range(1, 4):
-        copy(["g2"], ["g2.%d" % a], T.g2[32 * a:32 * a + 32, 0:128], T.g2[0:32, 128 * a:128 * a + 128], "a")
+        op("v", g.vector.tensor_tensor_scan, ["mk", "mk.z"], ["pf%d" % r0], T.pf[r0:r1, 0:NC], b("mk", 0, 32), b("mk", 0, 32), 0.0, A.add, A.max)
+    dma("y", "dpf", 16, ["pf0", "pf.z"], ["pfo"], T.pfo[:], T.pf[0:LC:3, :])
+    need("g", wr["pfo"])
+    spread("aM", lambda d: (T.pfo[(lc(at(d, me)) + 2) // 3], T.pfi[me]), others, parts(far, 2, 2, 2, 2) + parts(near, 2, 2, 4))
+    arrive("aM", "pffar", [2, 2, 2, 2, 2, 2, 4])
+    copy(["g2"], ["g2.u"], T.g2[64:128, 0:128], T.g2[0:64, 128:256], "a")
+    for a in range(4):
+        o = 32 - 32 * (a % 2)
+        copy(["g2"], ["g3.%d" % a], T.g3[32 * a:32 * a + 32, :], T.g2[o:o + 32, 256 + 128 * (a // 2):384 + 128 * (a // 2)], "a")
     pk = ["pf0", "pf32", "pf64", "pf96", "uu"]
     for c in range(2):
-        op("a", g.scalar.activation, pk, ["ja%d" % c, "cnt%d" % c], T.ja[:, NI * c:NI * c + NI], b("pf"), F.Sign,
+        op("a", g.scalar.activation, pk, ["ja%d" % c, "cnt%d" % c], T.ja[:, NC * c:NC * c + NC], T.pf[:, 0:NC], F.Sign,
            bias=b("uu", 0, 128, c, c + 1), scale=-1.0, accum_out=T.cnt[:, c:c + 1])
     for c in range(2):
-        tsc(pk, ["jv%d" % c], T.jv[:, NI * c:NI * c + NI], b("pf"), b("uu", 0, 128, 2 + c, 3 + c), A.is_lt, 2.0, A.mult)
+        tsc(pk, ["jv%d" % c], T.jv[:, NC * c:NC * c + NC], T.pf[:, 0:NC], b("uu", 0, 128, 2 + c, 3 + c), A.is_lt, 2.0, A.mult)
     for c in range(2):
-        w = slice(NI * c, NI * c + NI)
-        op("v", g.vector.tensor_tensor_scan, ["ones", "jv%d" % c], ["jh%d" % c], T.jh[:, w], b("ones"), T.jv[:, w], 0.0, A.mult, A.add)
-    copy(["jh0", "jh1"], ["cnt2"], T.cnt[0:64, 2:4], T.jh[0:64, NI - 1:2 * NI:NI])
-    copy(["jh0", "jh1"], ["cnt6"], T.cnt[0:64, 6:8], T.jh[64:128, NI - 1:2 * NI:NI])
+        w = slice(NC * c, NC * c + NC)
+        op("v", g.vector.tensor_tensor_scan, ["jv%d" % c], ["jh%d" % c], T.jh[:, w], T.jv[:, w], T.jv[:, w], 0.0, A.add, A.max)
+    tt(["g2", "g2.u", "g3.0", "g3.1", "g3.2", "g3.3"], ["g4"], b("g4"), T.g2[:, 0:128], b("g3"), A.max)
+    copy(["jh0", "jh1"], ["cnt2"], T.cnt[0:64, 2:4], T.jh[0:64, NC - 1:2 * NC:NC])
+    copy(["jh0", "jh1"], ["cnt6"], T.cnt[0:64, 6:8], T.jh[64:128, NC - 1:2 * NC:NC])
     ck = ["cnt0", "cnt1", "cnt2", "cnt6"]
     copy(ck[0:2], ["cnt4"], T.cnt[0:64, 4:6], T.cnt[64:128, 0:2])
-    gk = ["g2", "g2.1", "g2.2", "g2.3"]
-    flip(gk, ["tr"], T.tr[:, 0:128], T.g2[:, 0:128])
+    flip(["g4"], ["tr2"], b("tr2"), b("g4"))
     copy(ck + ["cnt4"], ["cnt8"], T.cnt[0:32, 8:16], T.cnt[32:64, 0:8])
     copy(ck + ["cnt4"], ["cnt16"], T.cnt[0:32, 16:24], T.cnt[0:32, 0:8])
     copy(ck + ["cnt4"], ["cnt24"], T.cnt[0:32, 24:32], T.cnt[32:64, 0:8])
-    tt(["idm"], ["emw"], b("emw", 64, 96), b("emw", 64, 96), T.idm[64:96, :], A.max)
+    tsc(["tr2"], ["m3"], b("m3"), T.tr2[:, AY:128:16], float(TAG), A.is_ge, BIG, A.mult)
+    tsc(["tr2"], ["c3"], b("c3"), T.tr2[:, AY:128:16], -float(TAG), A.add)
     flip(ck + ["cnt4", "cnt8", "cnt16", "cnt24"], ["ct"], T.ct[0:32, :], T.cnt[0:32, :])
-    copy(["tr"], ["ofw"], b("ofw"), T.tr[:, AD:128:16])
-    ct = T.ct[0:32, 0:MC]
+    tt(["tr2", "m3"], ["b4"], b("b4"), T.tr2[:, AD:128:16], b("m3"), A.subtract)
     pm = ["pm%d" % r0 for r0, r1 in quads]
     for r0, r1 in quads:
-        tsc(["ct", "bi2"], ["pn%d" % r0], T.pm[r0:r1, MC:2 * MC], ct, b("bi2", 0, 32), A.add, 0.5, A.mult)
-    for r0, r1 in quads:
-        tsc(["ct", "bi"], ["pm%d" % r0], T.pm[r0:r1, 0:MC], ct, b("bi", 0, 32), A.add, 0.5, A.mult)
-    need("g", wr["pn96"])
-    spread("aM", lambda d: (T.pm[:, MC + lc(at(d, me)):MC + lc(at(d, me)) + 3], T.meta[:, 3 * at(me, d):3 * at(me, d) + 3]),
-           near="aN")
+        tsc(["ct", "bi"], ["pm%d" % r0], T.pm[r0:r1, :], T.ct[0:32, 0:MC], b("bi", 0, 32), A.add, 0.5, A.mult)
+    tb("p4", "b4", "c3", A.max)
 
     def piece(src, dst, d):
         a, c = 16 * lc(at(d, me)), NI + E * at(me, d)
         return T[src][:, a:a + E], T[dst][:, c:c + E]
 
-    for k0, k1 in ((0, 4), (4, N - 1)):
+    def pick(k0, k1, e):
         of, w = T.pm[:, lc(k0):lc(k1 - 1) + 3], slice(16 * lc(k0), 16 * lc(k1 - 1) + E)
-        copy(["qo"] + pm, ["sn%d" % k0], T.sn[:, w].bitcast(dt.uint32), b("qo").bitcast(dt.uint32).indirect(of))
-        copy(["qo"] + pm, ["sns%d" % k0], T.sns[:, w], b("qos").indirect(of), "a")
-    spare = [x for d in others[4:] for x in engines(core, cores[d])]
-    need("g", wr["sn0"] + wr["sns0"])
-    spread("aC", lambda d: [x.bitcast(dt.uint8) for x in piece("sn", "fw", d)], others[0:4],
-           [write(helper(me), spare[0:RE], "aR", T.sns[:, 0:4 * E], b("rls"))])
-    sent[0] += RE
-    need("g", wr["sn4"])
-    spread("aC", lambda d: [x.bitcast(dt.uint8) for x in piece("sn", "fw", d)], others[4:])
-    need("g", wr["sns4"])
-    spread("aS", lambda d: piece("sns", "fws", d), others[4:])
-    arrive("aM", "meta0", others[0:4])
-    arrive("aN", "meta4", others[4:])
-    arrive("aC", "fw.far")
-    arrive("aS", "fws.far")
+        if e == "v":
+            copy(["qo"] + pm, ["sn%d" % k0], T.sn[:, w].bitcast(dt.uint32), b("qo").bitcast(dt.uint32).indirect(of))
+        else:
+            copy(["qo"] + pm, ["sns%d" % k0], T.sns[:, w], b("qos").indirect(of), "a")
 
-    copy(["ofw"] + gk, X, b("xt").indirect(b("ofw")), T.g2[:, 0:128])
-    copy(X[0:2] + ["gr"], ["x3"], b("x3"), T.xt[:, 0:NP].indirect(b("gr")), "a")
-    tt(["idw", "emw"], ["idi"], b("idi", 0, 96), b("idw", 0, 96), b("emw", 0, 96), A.max)
-    pack(0, 1)
-    copy(["meta4", "sl"], ["slot", "slot.own", "slot.z"], b("slot").indirect(T.meta[:, 12:21]), T.sl[:, 4 * E:(N - 1) * E])
+    def codes(d):
+        return [raw(x) for x in piece("sn", "fw", d)]
+
+    pick(0, 2, "v")
+    tsc(["p4", "odd"], ["ofw"], b("ofw"), b("p4"), b("odd"), A.add)
+    pick(2, 4, "v")
+    for k0, k1 in ((0, 2), (2, 4), (4, N - 1)):
+        pick(k0, k1, "a")
+    copy(["ofw", "g4"], X, b("xt").indirect(b("ofw")), b("g4"))
+    pick(4, N - 1, "v")
+    need("g", wr["sn0"])
+    g.remote_dma_fused([write(helper(me), near, "aR", raw(T.sn[:, 0:2 * E]), raw(b("rlc")))], local_sem=T.sem.lsent)
+    sent[0] += len(near)
+    need("g", wr["sn2"])
+    spread("aC", codes, others[2:4], parts(far, 4, 4))
+    need("g", wr["sns4"])
+    spread("aS", lambda d: piece("sns", "fws", d), others, parts(far, 2, 2, 2, 2) + parts(near, 4, 2, 2))
+    need("g", wr["sn4"] + [("iss", 1)])
+    spread("aC", codes, others[4:], parts(near, 2, 2, 4))
+    arrive("aC", "fw.far", [4, 4, 4, 4, 2, 2, 4])
+    arrive("aS", "fws.far", [2, 2, 2, 2, 4, 2, 2])
+    for p in range(0, 128, 16):
+        dma("y", "dtab", 128, ["pffar", "pfown"], tabs, T.tab[p:p + 1, 0:NO], T.pfi[:])
+    g.sync.sem_inc(T.sem.iss, 1)
+
+    copy(X[0:2] + gk, ["x3"], b("x3"), T.xt[:, 0:NP].indirect(T.go[:, 0:16]), "a")
+    pack(0, 2)
     flip(["x3"], ["x3t"], b("x3t"), b("x3"))
-    tt(["x3t"], ["x3a"], b("x3a", 0, 64), T.x3t[0:64, 0:P:32], T.x3t[64:128, 0:P:32], A.max)
-    tt(["x3a"], ["idi3"], b("idi", 96, 128), b("x3a", 0, 32), b("x3a", 32, 64), A.max)
-    tsc(["idi", "idi3"], ["idj"], b("idj"), b("idi"), TAG - 1, A.bitwise_and)
-    copy(["meta0", "sl"], ["slot", "slot.own", "slot.z"], b("slot").indirect(T.meta[:, 0:12]), T.sl[:, 0:4 * E])
+    pack(2, 3)
+    lo_, hi_ = T.x3t[0:32, 16:P:32], T.x3t[32:64, 16:P:32]
+    tt(["x3t"], ["hk"], b("hk", 0, 64), T.x3t[0:64, 0:P:16], T.x3t[64:128, 0:P:16], A.max)
+    tt(["x3t"], ["idi0"], b("idi", 0, 32), lo_, hi_, A.min)
+    tt(["x3t"], ["idi1"], b("idi", 32, 64), lo_, hi_, A.max)
+    hk = POOL["hk"][1]
+    for t in (2, 3):
+        w = slice(hk + 3 - t, hk + 16, 2)
+        tt(["hk"], ["idi%d" % t], b("idi", 32 * t, 32 * t + 32), T.tf[0:32, w], T.tf[32:64, w], A.max)
+    tsc(["idi%d" % t for t in range(R)], ["idj"], b("idj"), b("idi"), TAG - 1, A.bitwise_and)
+    pack(3, 4)
     for h in range(2):
         copy(["idj"], ["idu%d" % h], T.idu[:, h:16:2], b("idj"))
-    copy(["slot", "slot.own", "slot.z", "idu0", "idu1"], ["gs"], b("gs"), b("slot").indirect(b("idu")), "a")
-    pack(1, 3)
-    pack(3, 4)
+    copy(tabs + ["tab.z", "idu0", "idu1"], ["gs"], b("gs"), b("tab").indirect(b("idu")), "a")
+    pack(4, 8)
     flip(["gs"], ["gt"], b("gt"), b("gs"))
-    for c in range(2 * R):
-        t, h = c // 2, c % 2
-        copy(["gt"], ["sa%d" % c], T.so[0:32, 8 * c:8 * c + 8], T.gt[32 * t:32 * t + 32, 16 * h:P:32])
-    wr["so0"] = wr["sa%d" % (2 * R - 1)]
-    for r0, r1 in quads[1:]:
-        copy(["so0"], ["so%d" % r0], T.so[r0:r1, :], T.so[0:32, :])
+    for t, (r0, r1) in enumerate(quads):
+        tt(["gt"], ["ga%d" % t], b("ga", 0, 32, 16 * t, 16 * t + 16), T.gt[r0:r1, 0:P:16], T.gt[r0:r1, 1:P:16], A.add)
+    for r0, r1 in quads:
+        tsc(["ga%d" % t for t in range(R)], ["so%d" % r0], T.so[r0:r1, :], b("ga", 0, 32), -1.0, A.add)
 
     def products(t):
         pk, ps, of = "pk%d" % t, "ps%d" % t, T.so[:, 16 * t:16 * t + 16]
@@ -470,21 +498,23 @@ def rank_program(g, core, T, topo):
         copy(["fw.own", "fws.far"] + sk, [ps], b(ps), b("fws").indirect(of), "a")
         for i in range(O * t, O * t + O):
             w = slice(128 * i, 128 * i + 128)
-            op("p", g.tensor.matmul_mx, ["wq%d" % t, pk, ps], ["acc%d" % i], T.acc[:, 512 * i:512 * i + P],
+            op("p", g.tensor.matmul_mx, ["wq%d" % i, pk, ps], ["acc%d" % i], T.acc[:, 512 * i:512 * i + P],
                T.wq[:, w], T.wqs[:, w], b(pk), b(ps), True, True)
 
     def out(i, e):
         w = slice(P * i, P * i + P)
         copy(["acc%d" % i], ["ys%d" % i], T.ys[:, w], T.acc[:, 512 * i:512 * i + P], e)
-        dma("y", "dy", NS, ["ys%d" % i], ["y%d" % i], T.y[:, w], T.ys[:, w])
+        if i + 1 in STORES:
+            i0 = STORES[STORES.index(i + 1) - 1]
+            w = slice(P * i0, P * i + P)
+            dma("y", "dy", NS, ["ys%d" % k for k in range(i0, i + 1)], ["y%d" % i], T.y[:, w], T.ys[:, w])
 
-    NS = 16 * R * O
+    NS = 16 * (len(STORES) - 1)
+    left = [0]
     for t in range(R):
         products(t)
-        if t == R - 2:
-            out(0, "v")
-            out(1, "v")
-    for i in range(2, R * O):
-        out(i, "av"[i % 2])
+        for e in LEAVE[t]:
+            out(left[0], e)
+            left[0] += 1
     need("y", [("dy", NS)])
     need("g", [("lsent", sent[0])])

@@ -18,8 +18,12 @@ MC = 26
 WW = NI + (N - 1) * E
 RE = 4
 BIG = 1.0e9
-LEAVE = ["", "v", "v", "avavav"]
-STORES = [0, 1, 3, 5, 7, 8]
+SIM = 64
+CALLS = {"hdhd": [[0, 1], [2, 3]], "ohdd": [[0, 1], [2, 3]], "ohhd": [[0, 1], [2, 3]]}
+WAYS = ["hdhd", "ohdd", "ohhd"]
+PARTS = [(i, 0, P, i) for i in range(R * O - 1)] + [(R * O - 1, 0, P // 2, R * O - 1), (R * O - 1, P // 2, P, 0)]
+LEAVE = ["", "v", "v", "avavava"]
+STORES = {0: (0, 1), 2: (1, 3), 4: (3, 5), 5: (5, 6), 6: (6, 7), 8: (7, 8)}
 
 SCRATCH = {"lists": ("dram", [8, 128, 4], "float32"), "pfo": ("dram", [9, 128, 3], "bfloat16"), "pfi": ("dram", [8, 128, 3], "bfloat16"),
            "acc": ("psum", [128, 4096], "float32")}
@@ -40,19 +44,19 @@ def _pool(buf, dtype, **cols):
     SCRATCH[buf] = ("sbuf", [128, a], dtype)
 
 
-_sb("int32", src=28, pi=1, dd=32, gli=16)
-_sb("float32", ydf=128, yid=128, x3=P, x3t=P, sv=8, k4=8, jm=144, ne=80, n1=64, n2=64, g0=HC, g1=HC, g2=CH, g3=128, g4=128, tr=HC, tr1=HC,
+_sb("int32", src=28, pi=1, dd=32)
+_sb("float32", ydf=64, yid=64, x3=P, x3t=P, sv=8, k4=4, jm=144, ne=80, n1=64, n2=64, g0=HC, g1=HC, g2=CH, g3=128, g4=128, tr=HC, tr1=HC,
     tr2=128, f1f=16, v1=CH, xt=3 * NP, th=IT, thr=80, kk=64, kt=64, cnt=32, ct=32, idb=16, idn=16, ga=64, ys=2048)
 _sb("uint16", of1=32, ofq=16, of2=16, ofz=32, ofw=8, go=40, pm=MC, idu=16, so=64)
 _sb("bfloat16", cv=4 * NI, wt=4096, m2q=IT, mh=IT, mk=NC, pf=SI, ja=2 * NC, jv=2 * NC, tab=NO + 16, lo=SI, gs=P, gt=P)
 _sb("float16", jh=2 * NC)
-_sb("float8_e4m3fn_x4", wq=1024, qo=NI, sn=16 * LC, rlc=2 * E, fw=WW, pk0=P, pk1=P, pk2=P, pk3=P)
+_sb("float8_e4m3fn_x4", wq=1024, qo=NI, sn=16 * LC, rlc=4 * E, fw=WW, pk0=P, pk1=P, pk2=P, pk3=P)
 _sb("uint8", wqs=1024, qos=NI, sns=16 * LC, rls=4 * E, fws=WW, ps0=P, ps1=P, ps2=P, ps3=P)
-_pool("tf", "float32", s1=8, s3=8, m14=1, bc1=1, bc2=1, bc4=1, tag=1, tag3=1, tg0=1, e14=1, cap=1, odd=1, o4=1, c1=1, c2=1, dl=64, bi=1, bi2=1, a4=1, u0=1, u1=4, uu=4, p6=1,
+_pool("tf", "float32", s1=8, s3=8, m14=1, bc64=1, bc128=1, bc256=1, bc512=1, bc1024=1, tag=1, tag3=1, tg0=1, e14=1, cap=1, odd=1, row=1, o4=1, c1=1, c2=1, dl=64, bi=1, bi2=1, a4=1, u0=1, u1=4, uu=4, p6=1,
       d2=16, t3=16, em=16, hk=16, m3=8, c3=8, b4=8, p4=8)
-_pool("ti", "int32", b1=8, b2=8, b3=8, p15=1, p16=1, p3=1, p5=1, rk=24, r1=4, r2=4, idi=8, idj=8)
-SEMAPHORES = ["vv", "aa", "pp", "gq", "lsent", "aL", "aM", "aC", "aS", "aR", "aQ", "dsrc", "dcod", "dcv", "dw0", "dw1", "dfw", "down",
-              "dfan", "df1", "dv1", "dem", "dlo", "dpf", "dtab", "iss", "dy"]
+_pool("ti", "int32", b1=8, b2=8, b3=8, p15=1, pl=1, p16=1, p3=1, p5=1, rk=24, r1=4, r2=4, idi=8, idj=8)
+SEMAPHORES = ["vv", "aa", "pp", "gq", "lsent", "aL", "aM", "aC", "aS", "aR0", "aR1", "dsrc", "dcod", "dcv", "dw0", "dw1", "dfw", "down",
+              "dfan", "df1", "dv1", "dem", "dlo", "dpf", "dtab", "dy"]
 
 
 def rank_program(g, core, T, topo):
@@ -84,14 +88,32 @@ def rank_program(g, core, T, topo):
         return RemoteDMATransfer(dst_ids=[DstId(rid=rid, pnc=pid)], dma_engine_mask=sum(1 << x for x in mask), remote_sem=T.sem[sem],
                                  src=src, dst=dst)
 
+    def beyond(s):
+        to = cores[rest(s)[0]]
+        there = [c for c in range(SIM) if topo.mates(topo.chip(c), topo.chip(to)) and topo.die(c) == topo.die(cores[s]) and topo.may_write(c, to)]
+        able = [c for c in topo.cores_of(cores[s]) if c in cores and topo.may_write(c, there[0])]
+        return there[able.index(cores[s])] if cores[s] in able else None
+
+    def ways(s):
+        return WAYS[0] if beyond(s) is None else WAYS[1 + s % 2]
+
+    def dealt(s, k):
+        w = ways(s)
+        like = [j for call in CALLS[w] if k in call for j in call if (w[j] == "h") == (w[k] == "h")] or [k]
+        return 8 // len(like) * like.index(k), 8 // len(like)
+
     if me is None:
         for s in range(N):
-            if helper(s) == core:
-                far = topo.engines(core, cores[rest(s)[0]])
-                g.wait_ge(T.sem.aR, 8)
-                g.remote_dma_fused([write(cores[d], m, "aC", raw(T.rlc[:, E * k:E * k + E]), raw(T.fw[:, NI + E * at(s, d):NI + E * at(s, d) + E]))
-                                    for k, (d, m) in enumerate(zip(rest(s)[0:2], parts(far, 4, 4)))], local_sem=T.sem.lsent)
-                g.wait_ge(T.sem.lsent, len(far))
+            for way, via in (("h", helper(s)), ("o", beyond(s))):
+                ks = [k for k in range(4) if ways(s)[k] == way]
+                if via == core and ks:
+                    far = topo.engines(core, cores[rest(s)[0]])
+                    for j, k in enumerate(ks):
+                        c = NI + E * at(s, rest(s)[k])
+                        g.wait_ge(T.sem["aR%d" % j], dealt(s, k)[1])
+                        g.remote_dma_fused([write(cores[rest(s)[k]], far[j::len(ks)], "aC", raw(T.rlc[:, E * k:E * k + E]), raw(T.fw[:, c:c + E]))],
+                                           local_sem=T.sem.lsent)
+                    g.wait_ge(T.sem.lsent, len(far))
         return
     others = rest(me)
     OB = P * me
@@ -204,11 +226,10 @@ def rank_program(g, core, T, topo):
 
     quads = [(32 * a, 32 * a + 32) for a in range(4)]
 
-    ns = 16 * 15
-    for h in range(2):
-        dma("y", "dsrc", ns, [], ["src"], T.src[32 * h:32 * h + 32, 0:4], T.alt[:, 8 * h:8 * h + 8])
+    ns = 16 * 14
+    dma("y", "dsrc", ns, [], ["src"], T.src[0:64, 0:4], T.alt[:, :])
     for c in range(4):
-        dma("a", "dsrc", ns, [], ["src"], T.src[64:80, c:c + 1], T.f1[4 * c:4 * c + 4, :])
+        dma("yaaa"[c], "dsrc", ns, [], ["src"], T.src[64:80, c:c + 1], T.f1[4 * c:4 * c + 4, :])
     dma("y", "dsrc", ns, [], ["src"], T.src[96:112, 0:4], T.f2[:, :])
     for c in range(4):
         x = c + 1 - 2 * (c % 2)
@@ -222,31 +243,45 @@ def rank_program(g, core, T, topo):
     dma("y", "dcv", 32, [], ["cv.c"], T.cv[:, 4 * P:4 * IT], T.v[:, :])
 
     iota("pi", b("pi"), [[1, 1]], 0, 1, False)
-    iota("ydf", b("ydf"), [[7, 16], [-15, 8]], 0, 0)
-    iota("yid", b("yid"), [[1, 16], [16, 8]], 0, 0)
-    iota("k4", b("k4"), [[1, 8]], NP + OB, 4)
-    fill("xt", T.xt[64:128, 0:128], -float(TAG))
+    iota("ydf", b("ydf"), [[15, 4], [-15, 16]], 0, 0)
+    iota("yid", b("yid"), [[1, 4], [16, 16]], 0, 0)
+    iota("k4", b("k4"), [[1, 4]], NP + OB, 4)
+    fill("xt", T.xt[64:128, 0:64], -float(TAG))
+    fill("kk", b("kk"), 99.0)
+    wr["kd"] = wr["kk"]
+    fill("cv.z", T.cv[:, 4 * IT:4 * NI], 0.0)
     sb("p15", "pi", 0x4F, A.bitwise_and)
+    sb("pl", "pi", 15, A.bitwise_and)
+    sb("p16", "pi", 16, A.bitwise_and)
+    sb("p5", "pi", 32, A.bitwise_and)
     sb("m14", "p15", float(AY), A.is_ge)
+    sb("o4", "p16", 0.25, A.mult)
+    sb("e14", "p15", float(AY), A.is_equal, float(TAG), A.mult)
     tsc(["m14"], ["ydf"], b("ydf", 0, 64), b("ydf", 0, 64), b("m14", 0, 64), A.mult)
-    for n in (1, 2, 4):
-        line("bc%d" % n, "m14", float(n * (P - SI)), float(n * SI))
-    tt(["ydf", "yid"], ["xt"], T.xt[0:64, 0:128], b("ydf", 0, 64), b("yid", 0, 64), A.add)
+    sb("c1", "p5", 4 * SI / 32.0, A.mult)
+    sb("c2", "p5", -8 * SI / 32.0, A.mult, 4.0 * SI, A.add)
+    tt(["ydf", "yid"], ["xt"], T.xt[0:64, 0:64], b("ydf", 0, 64), b("yid", 0, 64), A.add)
+    steps = (64, 128, 256, 512, 1024)
+    for n in steps:
+        more = n // 16 if n < P else n // P * SI
+        line("bc%d" % n, "m14", float(n - more), float(more))
     iota("idb", b("idb", 0, 32), [[16, 16]], SI * me, 1)
     iota("v1", T.v1[:, 0:V], [[1, 16], [16, 4]], TAG + P, 0)
     iota("dl", b("dl"), [[0, 2], [-2, 2], [0, 16]], 1, 0)
     iota("dd", b("dd"), [[16, 32]], 0, 1, False)
+    iota("jm.0", T.jm[:, 0:16], [[1, 16]], 0, 0)
+    iota("jm.1", T.jm[:, 16:80], [[0, N], [1, N]], 0, 0)
 
     def bits(key, r1, c0):
         x, k = T.src[0:r1, c0:c0 + 4], str(c0)
-        tsc([key], ["b1" + k], b("b1", 0, r1, c0, c0 + 4), x, 0xF80, A.bitwise_and)
-        tsc([key], ["b2" + k], b("b2", 0, r1, c0, c0 + 4), x, 4, A.arith_shift_right, 7, A.bitwise_and)
+        tsc([key], ["b1" + k], b("b1", 0, r1, c0, c0 + 4), x, 0xF00, A.bitwise_and)
+        tsc([key], ["b2" + k], b("b2", 0, r1, c0, c0 + 4), x, 4, A.arith_shift_right, 15, A.bitwise_and)
         tsc([key], ["b3" + k], b("b3", 0, r1, c0, c0 + 4), x, 15, A.bitwise_and)
 
     def sums(r1, c0):
         k = str(c0)
         tt(["b1" + k, "b2" + k], ["s1" + k], b("s1", 0, r1, c0, c0 + 4), b("b1", 0, r1, c0, c0 + 4), b("b2", 0, r1, c0, c0 + 4), A.add)
-        tsc(["b3" + k], ["s3" + k], b("s3", 0, r1, c0, c0 + 4), b("b3", 0, r1, c0, c0 + 4), 8.0, A.mult)
+        tsc(["b3" + k], ["s3" + k], b("s3", 0, r1, c0, c0 + 4), b("b3", 0, r1, c0, c0 + 4), 16.0, A.mult)
 
     bits("src", 128, 0)
     sums(128, 0)
@@ -254,39 +289,30 @@ def rank_program(g, core, T, topo):
         tsc(["s10", "s30", "k4"], ["sv"] if j == 3 else [], T.sv[:, j:j + 1], b("s1", 0, 128, j, j + 1), b("s3", 0, 128, j, j + 1), A.add,
             T.k4[:, j:j + 1], A.min)
     need("g", wr["sv"])
-    spread("aL", lambda d: (T.sv[:, 0:4], T.lists[me]), others, parts(far, 2, 2, 2, 2) + parts(near, 2, 2, 2))
+    spread("aL", lambda d: (T.sv[:, 0:4], T.lists[me]), others[0:4], parts(far, 2, 2, 2, 2))
     dma("y", "down", 16, ["sv"], ["lown"], T.lists[me], T.sv[:, 0:4])
+    need("g", wr["lown"])
+    spread("aL", lambda d: (T.lists[me], T.lists[me]), others[4:], parts(near, 1, 1, 1))
 
-    for n in (128, 256, 512, 1024):
-        plus = 128.0 if n == 128 else b("bc%d" % (n // P))
-        copy(["xt", "bc1", "bc2", "bc4"], ["xt"], T.xt[:, n:2 * n], T.xt[:, 0:n], "a", plus)
+    for n in steps:
+        copy(["xt", "bc%d" % n], ["xt"], T.xt[:, n:2 * n], T.xt[:, 0:n], "a", b("bc%d" % n))
+        if n == 64:
+            line("cap", "m14", -16.0 * TAG, 15.0 * TAG)
         if n == 128:
             wr["xb"] = wr["xt"]
+            line("tag", "m14", -2.0 * TAG, 2.0 * TAG)
+        if n == 256:
+            copy(["tag", "e14"], ["tg0"], b("tg0"), b("e14"), "a", b("tag"))
     full = wr["xt"]
     tsc(["cod"], ["em"], b("em", 0, 32), T.src[0:32, 8:24], 0.0, A.is_lt, float(NO), A.mult)
-    sb("p16", "pi", 16, A.bitwise_and)
-    sb("p5", "pi", 32, A.bitwise_and)
-    fill("kk", b("kk"), 99.0)
-    wr["kd"] = wr["kk"]
-    fill("gli", b("gli"), 0)
-    tt(["em", "idb"], ["idn"], b("idn", 0, 32), b("em", 0, 32), b("idb", 0, 32), A.max)
-    sb("o4", "p16", 0.25, A.mult)
-    sb("c1", "p5", 4 * SI / 32.0, A.mult)
-    sb("c2", "p5", -8 * SI / 32.0, A.mult, 4.0 * SI, A.add)
-    sb("cap", "m14", -16.0 * TAG, A.mult, 15.0 * TAG, A.add)
     copy(["xb"], ["x1"], T.xt[:, NP:NP + 256], T.xt[:, 0:256], "v", float(NP))
     seed = wr["x1"]
-    sb("tag", "m14", -2.0 * TAG, A.mult, 2.0 * TAG, A.add)
-    sb("e14", "p15", float(AY), A.is_equal, float(TAG), A.mult)
-    copy(["tag", "e14"], ["tg0"], b("tg0"), b("e14"), "a", b("tag"))
+    tt(["em", "idb"], ["idn"], b("idn", 0, 32), b("em", 0, 32), b("idb", 0, 32), A.max)
+    copy([], ["x1"], T.xt[:, NP + 256:NP + 512], T.xt[:, NP:NP + 256], "a", 256.0)
     need("y", full + seed)
     for p in (0, 16, 48):
-        for h in range(2):
-            dma("y", "dem", 96, ["idn"], ["xe"], T.xt[p:p + 1, OB + 128 * h:OB + 128 * h + 128], T.idn[0:16, 8 * h:8 * h + 8])
+        dma("y", "dem", 48, ["idn"], ["xe"], T.xt[p:p + 1, OB:OB + P], T.idn[0:16, :])
 
-    iota("jm.0", T.jm[:, 0:16], [[1, 16]], 0, 0)
-    iota("jm.1", T.jm[:, 16:80], [[0, N], [1, N]], 0, 0)
-    iota("jm", T.jm[:, 80:144], [[1, N], [0, N]], 0, 0)
     cuts = [k for k in range(N - 1) if k in (0, 4) or others[k] != others[k - 1] + 1] + [N - 1]
     kkeys = ["kk", "kd"]
     for k0, k1 in zip(cuts[:-1], cuts[1:]):
@@ -294,9 +320,7 @@ def rank_program(g, core, T, topo):
         iota("kd%d" % k0, T.kk[:, 32 + lc(k0):32 + lc(k0) + 3 * (k1 - k0)], [[1, k1 - k0], [0, 3]], others[k0], 0)
         iota("kk%d" % k0, T.kk[:, lc(k0):lc(k0) + 3 * (k1 - k0)], [[0, k1 - k0], [16, 3]], 0, 0)
         kkeys += ["kd%d" % k0, "kk%d" % k0]
-    for r1, base in ((32, OB - 128), (16, OB)):
-        iota("gli", b("gli", 0, r1), [[128, 2], [1, 8]], base, 8, False)
-    need("g", wr["gli"])
+    iota("jm", T.jm[:, 80:144], [[1, N], [0, N]], 0, 0)
     iota("pf.z", T.pf[:, IT:SI], [[0, SI - IT]], 0, 0)
     iota("lo", b("lo", 0, 32), [[0, SI // 16], [1, 16]], 1, 0)
     iota("tab.z", T.tab[:, NO:NO + 16], [[0, 16]], IT // 2 + 4, 0)
@@ -307,7 +331,9 @@ def rank_program(g, core, T, topo):
 
     tsc(["dl", "o4"], ["dl"], b("dl"), b("dl"), b("o4"), A.mult)
     tsc(["cap", "c1"], ["v1"], T.v1[:, 0:V], T.v1[:, 0:V], b("c1"), A.add, b("cap"), A.min)
-    fill("cv.z", T.cv[:, 4 * IT:4 * NI], 0.0)
+    sb("p3", "pi", 3, A.bitwise_and)
+    sb("row", "pl", 16.0, A.mult, float(OB), A.add)
+    sb("p6", "pi", 64.0, A.is_ge, 4.0, A.mult)
     tt(["dl", "v1"], ["v1"], T.v1[:, 0:V], T.v1[:, 0:V], b("dl"), A.add)
     for nm in ("of1", "ofq", "ofz"):
         copy(["dd"], [nm], b(nm, 64, 128), b("dd", 64, 128, 0, POOL[nm][2]))
@@ -321,11 +347,27 @@ def rank_program(g, core, T, topo):
     tt(["rk", "r1"], ["r2"], b("r2", 0, 32), b("rk", 0, 32, 20, 24), b("r1", 0, 32), A.add)
     tt(["s14", "s34"], ["sv.v"], T.sv[0:32, 4:8], b("s1", 0, 32, 4, 8), b("s3", 0, 32, 4, 8), A.add)
     copy(["v1", "c2"], ["v1"], T.v1[:, 4 * V:8 * V], T.v1[:, 0:4 * V], "v", b("c2"))
+    tsc(["p5", "p6"], ["a4"], b("a4"), b("p5"), 0.25, A.mult, b("p6"), A.add)
     copy(["sv.v"], ["gl.v"], T.go[0:32, 16:20], T.sv[0:32, 4:8])
     copy(["r2"], ["ow.2"], T.go[0:32, 36:40], b("r2", 0, 32))
+    copy(["jm.0", "row"], ["gl.c"], T.go[:, 0:16], T.jm[:, 0:16], "v", b("row"))
     op("v", g.vector.quantize_mx, ["cv.z", "cv.c"], ["qo"], b("qo"), b("qos"), b("cv"))
+    gk = ["gl.c", "gl.v", "ow.c", "ow.2"]
 
-    arrive("aL", "lfar", [2] * 7)
+    def onto(r0):
+        copy(gk[0:4], ["go%d" % r0], T.go[r0:r0 + 32, 16:40], T.go[0:32, 16:40])
+
+    flip(kkeys, ["kt"], b("kt"), b("kk"))
+    onto(32)
+    onto(64)
+    dcol = T.kt[:, 32:33]
+    tsc(["jm", "kt"], ["ne"], b("ne"), T.jm[:, 0:80], dcol, A.not_equal, BIG, A.mult)
+    tsc(["jm", "kt"], ["n1"], b("n1"), T.jm[:, 80:144], dcol, A.not_equal)
+    onto(96)
+    tsc(["ne"], ["n2"], b("n2"), b("ne", 0, 128, 16, 80), 2 * TAG - 0.5, A.add)
+    gk += ["go32", "go64", "go96"]
+
+    arrive("aL", "lfar", [2, 2, 2, 2, 1, 1, 1])
     lk = ["lfar", "lown"]
     for r in range(4):
         dma("ya"[r % 2], "df1", 64, lk, ["f1f"], T.f1f[0:64, 4 * r:4 * r + 4], T.lists[r:N:4, 64:96, :])
@@ -335,11 +377,10 @@ def rank_program(g, core, T, topo):
         dma("ya"[h % 2], "dfan", 64, lk, ["xt"], T.xt[p:p + 1, 0:NP], T.lists[:, 0:64, :])
     for h in range(2):
         p, w = 16 * h + AD, slice(96 + 16 * h, 112 + 16 * h)
-        dma("y", "dv1", 96, lk, ["v1"], T.v1[p:p + 1, :], T.lists[:, w, :])
+        dma("a", "dv1", 96, lk, ["v1"], T.v1[p:p + 1, :], T.lists[:, w, :])
         for a in range(2):
             dma("y", "dv1", 96, lk, ["v1"], T.v1[32 + p:33 + p, HC * a:HC * a + HC], T.lists[4 - 4 * a:8 - 4 * a, w, :])
-    for n in (256, 512):
-        copy([], ["x1"], T.xt[:, NP + n:NP + 2 * n], T.xt[:, NP:NP + n], "a", float(n))
+    copy([], ["x1"], T.xt[:, NP + 512:NP + 1024], T.xt[:, NP:NP + 512], "a", 512.0)
     need("y", wr["v1"])
     load_w("y", 0)
     load_w("y", 1)
@@ -349,34 +390,27 @@ def rank_program(g, core, T, topo):
     copy(["f1f"], ["og"], b("of1", 0, 64, 0, 16), b("f1f", 0, 64))
     for a in range(2):
         copy(["f1f"], ["of1%d" % a], b("of1", 32 * a, 32 * a + 32, 16, 32), b("f1f", 32 - 32 * a, 64 - 32 * a))
-    copy(X[0:2] + ["of1", "og", "tg0"], ["g0"], b("g0"), T.xt[:, 0:NP].indirect(T.of1[:, 0:16]), "a", b("tg0"))
+
+    def step(keys, table, of, gm, tag):
+        for h in range(2):
+            copy(keys + [tag], [gm + "av"[h]], b(gm, 0, 128, 128 * h, 128 * h + 128), table.indirect(b(of, 0, 128, 8 * h, 8 * h + 8)),
+                 "av"[h], b(tag))
+
+    step(X[0:2] + ["of1", "og"], T.xt[:, 0:NP], "of1", "g0", "tg0")
     copy(["x1"], ["x2"], T.xt[:, NP + 1024:2 * NP], T.xt[:, NP:NP + 1024], "a", 1024.0)
-    flip(kkeys, ["kt"], b("kt"), b("kk"))
-    copy(["gli"], ["gl.c"], T.go[0:32, 0:16], b("gli", 0, 32))
-    sb("p3", "pi", 3, A.bitwise_and)
-    sb("p6", "pi", 64.0, A.is_ge, 4.0, A.mult)
-    dcol = T.kt[:, 32:33]
-    tsc(["jm", "kt"], ["ne"], b("ne"), T.jm[:, 0:80], dcol, A.not_equal, BIG, A.mult)
-    tsc(["jm", "kt"], ["n1"], b("n1"), T.jm[:, 80:144], dcol, A.not_equal)
-    flip(["g0"], ["tr"], T.tr[0:64, :], T.g0[0:64, :])
-    tsc(["ne"], ["n2"], b("n2"), b("ne", 0, 128, 16, 80), 2 * TAG - 0.5, A.add)
-    copy(["tr"], ["ofq0"], b("ofq", 0, 64), T.tr[0:64, AD:HC:16])
-    copy(["of1", "og", "of10", "of11", "v1"], X[0:2], T.xt[:, 0:NP].indirect(b("of1")), b("v1"))
-    copy(X + ["ofq", "ofq0", "tag"], ["g1"], b("g1"), b("xt").indirect(b("ofq")), "a", b("tag"))
-    tsc(["tr"], ["d2"], b("d2", 0, 64), T.tr[0:64, AD:HC:16], float(NP), A.is_ge, float(NP), A.mult)
-    gk = ["gl.c", "gl.v", "ow.c", "ow.2"]
-    for r0, r1 in quads[1:]:
-        copy(gk, ["go%d" % r0], T.go[r0:r1, :], T.go[0:32, :])
-    gk += ["go32", "go64", "go96"]
-    tt(["tr", "d2"], ["t3"], b("t3", 0, 64), T.tr[0:64, AD:HC:16], b("d2", 0, 64), A.add)
     tt(["n1", "n2"], ["thr.2"], T.thr[:, 16:80], b("n1"), b("n2"), A.mult)
+    flip(["g0a", "g0v"], ["tr"], T.tr[0:64, :], T.g0[0:64, :])
+    copy(["of1", "og", "of10", "of11", "v1"], X[0:2], T.xt[:, 0:NP].indirect(b("of1")), b("v1"))
+    copy(["tr"], ["ofq0"], b("ofq", 0, 64), T.tr[0:64, AD:HC:16])
+    tsc(["tr"], ["d2"], b("d2", 0, 64), T.tr[0:64, AD:HC:16], float(NP), A.is_ge, float(NP), A.mult)
+    step(X + ["ofq", "ofq0"], b("xt"), "ofq", "g1", "tag")
+    tt(["tr", "d2"], ["t3"], b("t3", 0, 64), T.tr[0:64, AD:HC:16], b("d2", 0, 64), A.add)
+    copy(["g1a", "g1v"], ["g0a", "g0v"], T.g0[64:128, :], T.g1[0:64, :], "a", 4.0 * TAG)
+    flip(["g1a", "g1v"], ["tr1"], T.tr1[0:64, :], T.g1[0:64, :])
     copy(["t3"], ["of2a"], b("of2", 0, 64), b("t3", 0, 64))
-    copy(["g1"], ["g0"], T.g0[64:128, :], T.g1[0:64, :], "a", 4.0 * TAG)
-    flip(["g1"], ["tr1"], T.tr1[0:64, :], T.g1[0:64, :])
-    tsc(["p5", "p6"], ["a4"], b("a4"), b("p5"), 0.25, A.mult, b("p6"), A.add)
     copy(["tr1"], ["of2b"], b("of2", 64, 128), T.tr1[0:64, AD:HC:16])
     copy(["tr1"], ["ofz0"], b("ofz", 0, 64, 0, 16), T.tr1[0:64, AD:HC:16])
-    copy(["of2a", "of2b", "g0"], X, b("xt").indirect(b("of2")), b("g0"))
+    copy(["of2a", "of2b", "g0a", "g0v"], X, b("xt").indirect(b("of2")), b("g0"))
     copy(["ne"], ["thr.c"], T.thr[:, 0:16], b("ne", 0, 128, 0, 16), "a", TAG - 0.5)
     copy(["thr.c", "thr.2"] + gk, ["th"], b("th"), b("thr").indirect(T.go[:, 20:40]), "a")
     copy(["kt", "a4"], ["u0"], b("u0"), T.kt[:, 0:1], "a", b("a4"))
@@ -408,17 +442,19 @@ def rank_program(g, core, T, topo):
     for c in range(2):
         op("a", g.scalar.activation, pk, ["ja%d" % c, "cnt%d" % c], T.ja[:, NC * c:NC * c + NC], T.pf[:, 0:NC], F.Sign,
            bias=b("uu", 0, 128, c, c + 1), scale=-1.0, accum_out=T.cnt[:, c:c + 1])
+    g3k = ["g2", "g2.u", "g3.0", "g3.1", "g3.2", "g3.3"]
+    tt(g3k, ["g4a"], b("g4", 0, 128, 0, 64), T.g2[:, 0:64], b("g3", 0, 128, 0, 64), A.max)
     for c in range(2):
         tsc(pk, ["jv%d" % c], T.jv[:, NC * c:NC * c + NC], T.pf[:, 0:NC], b("uu", 0, 128, 2 + c, 3 + c), A.is_lt, 2.0, A.mult)
     for c in range(2):
         w = slice(NC * c, NC * c + NC)
         op("v", g.vector.tensor_tensor_scan, ["jv%d" % c], ["jh%d" % c], T.jh[:, w], T.jv[:, w], T.jv[:, w], 0.0, A.add, A.max)
-    tt(["g2", "g2.u", "g3.0", "g3.1", "g3.2", "g3.3"], ["g4"], b("g4"), T.g2[:, 0:128], b("g3"), A.max)
+    tt(g3k, ["g4"], b("g4", 0, 128, 64, 128), T.g2[:, 64:128], b("g3", 0, 128, 64, 128), A.max)
     copy(["jh0", "jh1"], ["cnt2"], T.cnt[0:64, 2:4], T.jh[0:64, NC - 1:2 * NC:NC])
     copy(["jh0", "jh1"], ["cnt6"], T.cnt[0:64, 6:8], T.jh[64:128, NC - 1:2 * NC:NC])
     ck = ["cnt0", "cnt1", "cnt2", "cnt6"]
     copy(ck[0:2], ["cnt4"], T.cnt[0:64, 4:6], T.cnt[64:128, 0:2])
-    flip(["g4"], ["tr2"], b("tr2"), b("g4"))
+    flip(["g4a", "g4"], ["tr2"], b("tr2"), b("g4"))
     copy(ck + ["cnt4"], ["cnt8"], T.cnt[0:32, 8:16], T.cnt[32:64, 0:8])
     copy(ck + ["cnt4"], ["cnt16"], T.cnt[0:32, 16:24], T.cnt[0:32, 0:8])
     copy(ck + ["cnt4"], ["cnt24"], T.cnt[0:32, 24:32], T.cnt[32:64, 0:8])
@@ -445,32 +481,46 @@ def rank_program(g, core, T, topo):
     def codes(d):
         return [raw(x) for x in piece("sn", "fw", d)]
 
+    for p in range(0, 128, 16):
+        dma("yyaa"[p // 32], "dtab", 128, ["pffar", "pfown"], tabs, T.tab[p:p + 1, 0:NO], T.pfi[:])
     pick(0, 2, "v")
     tsc(["p4", "odd"], ["ofw"], b("ofw"), b("p4"), b("odd"), A.add)
     pick(2, 4, "v")
     for k0, k1 in ((0, 2), (2, 4), (4, N - 1)):
         pick(k0, k1, "a")
-    copy(["ofw", "g4"], X, b("xt").indirect(b("ofw")), b("g4"))
+    copy(["ofw", "g4a", "g4"], X, b("xt").indirect(b("ofw")), b("g4"))
     pick(4, N - 1, "v")
     need("g", wr["sn0"])
-    g.remote_dma_fused([write(helper(me), near, "aR", raw(T.sn[:, 0:2 * E]), raw(b("rlc")))], local_sem=T.sem.lsent)
-    sent[0] += len(near)
-    need("g", wr["sn2"])
-    spread("aC", codes, others[2:4], parts(far, 4, 4))
+
+    way, via = ways(me), {"h": helper(me), "o": beyond(me)}
+    for call in CALLS[way]:
+        need("g", wr["sn2"] if call[-1] >= 2 else [])
+        ts = []
+        for k in call:
+            a, n = dealt(me, k)
+            mask = (near if way[k] == "h" else far)[a:a + n]
+            sent[0] += n
+            if way[k] == "d":
+                ts.append(write(cores[others[k]], mask, "aC", *codes(others[k])))
+            else:
+                w = slice(E * k, E * k + E)
+                ts.append(write(via[way[k]], mask, "aR%d" % way[0:k].count(way[k]), raw(T.sn[:, w]), raw(T.rlc[:, w])))
+        g.remote_dma_fused(ts, local_sem=T.sem.lsent)
     need("g", wr["sns4"])
     spread("aS", lambda d: piece("sns", "fws", d), others, parts(far, 2, 2, 2, 2) + parts(near, 4, 2, 2))
-    need("g", wr["sn4"] + [("iss", 1)])
-    spread("aC", codes, others[4:], parts(near, 2, 2, 4))
-    arrive("aC", "fw.far", [4, 4, 4, 4, 2, 2, 4])
+    need("g", wr["sn4"])
+    late = [k for k in range(4) if not any(k in call for call in CALLS[way])]
+    spread("aC", codes, [others[k] for k in late] + others[4:], [far for k in late] + parts(near, 2, 2, 4))
+    mine = [(s, at(me, s), ways(s)[at(me, s)]) for s in others[0:4]]
+    wr["fw.far"] = [("aC", sum(dealt(s, k)[1] if w == "d" else len(far) // ways(s).count(w) for s, k, w in mine) +
+                     sum([2, 2, 4][at(me, s) - 4] for s in others[4:]))]
     arrive("aS", "fws.far", [2, 2, 2, 2, 4, 2, 2])
-    for p in range(0, 128, 16):
-        dma("y", "dtab", 128, ["pffar", "pfown"], tabs, T.tab[p:p + 1, 0:NO], T.pfi[:])
-    g.sync.sem_inc(T.sem.iss, 1)
 
-    copy(X[0:2] + gk, ["x3"], b("x3"), T.xt[:, 0:NP].indirect(T.go[:, 0:16]), "a")
-    pack(0, 2)
-    flip(["x3"], ["x3t"], b("x3t"), b("x3"))
-    pack(2, 3)
+    for e, c0, c1 in (("a", 0, 12), ("v", 12, 16)):
+        copy(X[0:2] + gk, ["x3" + e], b("x3", 0, 128, 16 * c0, 16 * c1), T.xt[:, 0:NP].indirect(T.go[:, c0:c1]), e)
+    pack(0, 1)
+    flip(["x3a", "x3v"], ["x3t"], b("x3t"), b("x3"))
+    pack(1, 2)
     lo_, hi_ = T.x3t[0:32, 16:P:32], T.x3t[32:64, 16:P:32]
     tt(["x3t"], ["hk"], b("hk", 0, 64), T.x3t[0:64, 0:P:16], T.x3t[64:128, 0:P:16], A.max)
     tt(["x3t"], ["idi0"], b("idi", 0, 32), lo_, hi_, A.min)
@@ -480,36 +530,43 @@ def rank_program(g, core, T, topo):
         w = slice(hk + 3 - t, hk + 16, 2)
         tt(["hk"], ["idi%d" % t], b("idi", 32 * t, 32 * t + 32), T.tf[0:32, w], T.tf[32:64, w], A.max)
     tsc(["idi%d" % t for t in range(R)], ["idj"], b("idj"), b("idi"), TAG - 1, A.bitwise_and)
-    pack(3, 4)
+    pack(2, 3)
     for h in range(2):
         copy(["idj"], ["idu%d" % h], T.idu[:, h:16:2], b("idj"))
-    copy(tabs + ["tab.z", "idu0", "idu1"], ["gs"], b("gs"), b("tab").indirect(b("idu")), "a")
-    pack(4, 8)
-    flip(["gs"], ["gt"], b("gt"), b("gs"))
+    pack(3, 4)
+    for h in range(2):
+        copy(tabs + ["tab.z", "idu0", "idu1"], ["gs%d" % h], b("gs", 0, 128, 128 * h, 128 * h + 128),
+             b("tab").indirect(T.idu[:, 8 * h:8 * h + 8]), "av"[h])
+    pack(4, 5)
+    flip(["gs0", "gs1"], ["gt"], b("gt"), b("gs"))
+    pack(5, 6)
     for t, (r0, r1) in enumerate(quads):
         tt(["gt"], ["ga%d" % t], b("ga", 0, 32, 16 * t, 16 * t + 16), T.gt[r0:r1, 0:P:16], T.gt[r0:r1, 1:P:16], A.add)
+    pack(6, 7)
     for r0, r1 in quads:
         tsc(["ga%d" % t for t in range(R)], ["so%d" % r0], T.so[r0:r1, :], b("ga", 0, 32), -1.0, A.add)
+    pack(7, 8)
 
     def products(t):
         pk, ps, of = "pk%d" % t, "ps%d" % t, T.so[:, 16 * t:16 * t + 16]
         sk = ["so%d" % r0 for r0, r1 in quads]
         copy(["fw.own", "fw.far"] + sk, [pk], b(pk).bitcast(dt.uint32), b("fw").bitcast(dt.uint32).indirect(of))
         copy(["fw.own", "fws.far"] + sk, [ps], b(ps), b("fws").indirect(of), "a")
-        for i in range(O * t, O * t + O):
-            w = slice(128 * i, 128 * i + 128)
-            op("p", g.tensor.matmul_mx, ["wq%d" % i, pk, ps], ["acc%d" % i], T.acc[:, 512 * i:512 * i + P],
-               T.wq[:, w], T.wqs[:, w], b(pk), b(ps), True, True)
+        for i, c0, c1, bank in PARTS:
+            if i // O == t:
+                w = slice(128 * i, 128 * i + 128)
+                op("p", g.tensor.matmul_mx, ["wq%d" % i, pk, ps], ["acc%d" % bank], T.acc[:, 512 * bank:512 * bank + c1 - c0],
+                   T.wq[:, w], T.wqs[:, w], b(pk, 0, 128, c0, c1), b(ps, 0, 128, c0, c1), True, True)
 
-    def out(i, e):
-        w = slice(P * i, P * i + P)
-        copy(["acc%d" % i], ["ys%d" % i], T.ys[:, w], T.acc[:, 512 * i:512 * i + P], e)
-        if i + 1 in STORES:
-            i0 = STORES[STORES.index(i + 1) - 1]
-            w = slice(P * i0, P * i + P)
-            dma("y", "dy", NS, ["ys%d" % k for k in range(i0, i + 1)], ["y%d" % i], T.y[:, w], T.ys[:, w])
+    def out(k, e):
+        tile, c0, c1, bank = PARTS[k]
+        copy(["acc%d" % bank], ["ys%d" % k], T.ys[:, P * tile + c0:P * tile + c1], T.acc[:, 512 * bank:512 * bank + c1 - c0], e)
+        if k in STORES:
+            i0, i1 = STORES[k]
+            w = slice(P * i0, P * i1)
+            dma("y", "dy", NS, ["ys%d" % j for j in range(len(PARTS)) if i0 <= PARTS[j][0] < i1], ["y%d" % k], T.y[:, w], T.ys[:, w])
 
-    NS = 16 * (len(STORES) - 1)
+    NS = 16 * len(STORES)
     left = [0]
     for t in range(R):
         products(t)

from concourse.bass import DstId, RemoteDMATransfer
from concourse.mybir import dt, AluOpType as A, ActivationFunctionType as F, AxisListType as AX

N, P, V, R, O = 8, 256, 64, 4, 2
CH = N * V
HC = CH // 2
NP = N * P
AD, AY = 15, 14
E = 48
IT = P + V
NI = IT + 16
NC = IT
SI = 384
NO = N * SI
TAG = 4096
LC = 25
MC = 26
WW = NI + (N - 1) * E
RE = 4
BIG = 1.0e9
SIM = 64
CALLS = {"hdhd": [[0, 1], [2, 3]], "ohdd": [[0, 1], [2, 3]], "ohhd": [[0, 1], [2, 3]]}
WAYS = ["hdhd", "ohdd", "ohhd"]
PARTS = [(i, 0, P, i) for i in range(R * O - 1)] + [(R * O - 1, 0, P // 2, R * O - 1), (R * O - 1, P // 2, P, 0)]
LEAVE = ["", "v", "v", "avavava"]
STORES = {0: (0, 1), 2: (1, 3), 4: (3, 5), 5: (5, 6), 6: (6, 7), 8: (7, 8)}

SCRATCH = {"lists": ("dram", [8, 128, 4], "float32"), "pfo": ("dram", [9, 128, 3], "bfloat16"), "pfi": ("dram", [8, 128, 3], "bfloat16"),
           "acc": ("psum", [128, 4096], "float32")}
POOL = {}


def _sb(dtype, **cols):
    for k in cols:
        SCRATCH[k] = ("sbuf", [128, cols[k]], dtype)
        POOL[k] = (k, 0, cols[k])


def _pool(buf, dtype, **cols):
    a = 0
    for k in cols:
        POOL[k] = (buf, a, cols[k])
        a += cols[k]
    SCRATCH[buf] = ("sbuf", [128, a], dtype)


_sb("int32", src=28, pi=1, dd=32)
_sb("float32", ydf=64, yid=64, x3=P, x3t=P, sv=8, k4=4, jm=144, ne=80, n1=64, n2=64, g0=HC, g1=HC, g2=CH, g3=128, g4=128, tr=HC, tr1=HC,
    tr2=128, f1f=16, v1=CH, xt=3 * NP, th=IT, thr=80, kk=64, kt=64, cnt=32, ct=32, idb=16, idn=16, ga=64, ys=2048)
_sb("uint16", of1=32, ofq=16, of2=16, ofz=32, ofw=8, go=40, pm=MC, idu=16, so=64)
_sb("bfloat16", cv=4 * NI, wt=4096, m2q=IT, mh=IT, mk=NC, pf=SI, ja=2 * NC, jv=2 * NC, tab=NO + 16, lo=SI, gs=P, gt=P)
_sb("float16", jh=2 * NC)
_sb("float8_e4m3fn_x4", wq=1024, qo=NI, sn=16 * LC, rlc=4 * E, fw=WW, pk0=P, pk1=P, pk2=P, pk3=P)
_sb("uint8", wqs=1024, qos=NI, sns=16 * LC, rls=4 * E, fws=WW, ps0=P, ps1=P, ps2=P, ps3=P)
_pool("tf", "float32", s1=8, s3=8, m14=1, bc64=1, bc128=1, bc256=1, bc512=1, bc1024=1, tag=1, tag3=1, tg0=1, e14=1, cap=1, odd=1, row=1, o4=1, c1=1, c2=1, dl=64, bi=1, bi2=1, a4=1, u0=1, u1=4, uu=4, p6=1,
      d2=16, t3=16, em=16, hk=16, m3=8, c3=8, b4=8, p4=8)
_pool("ti", "int32", b1=8, b2=8, b3=8, p15=1, pl=1, p16=1, p3=1, p5=1, rk=24, r1=4, r2=4, idi=8, idj=8)
SEMAPHORES = ["vv", "aa", "pp", "gq", "lsent", "aL", "aM", "aC", "aS", "aR0", "aR1", "dsrc", "dcod", "dcv", "dw0", "dw1", "dfw", "down",
              "dfan", "df1", "dv1", "dem", "dlo", "dpf", "dtab", "dy"]


def rank_program(g, core, T, topo):
    me = T.rank_of(core)
    cores = T.cores

    def rest(r):
        on = [d for d in range(N) if topo.chip(cores[d]) == topo.chip(cores[r])]
        off = [d for d in range(N) if d not in on]
        k = on.index(r)
        return off[k:] + off[0:k] + on[0:k] + on[k + 1:]

    def at(s, d):
        return rest(d).index(s)

    def helper(s):
        mine = topo.cores_of(cores[s])
        free = [c for c in mine if c not in cores and topo.die(c) != topo.die(cores[s])]
        return free[[c for c in mine if c in cores].index(cores[s])]

    def parts(engines, *sizes):
        return [engines[sum(sizes[0:k]):sum(sizes[0:k + 1])] for k in range(len(sizes))]

    def raw(x):
        return x.bitcast(dt.uint8)

    def write(to, mask, sem, src, dst):
        rid, pid = topo.addr(to)[0:2]
        return RemoteDMATransfer(dst_ids=[DstId(rid=rid, pnc=pid)], dma_engine_mask=sum(1 << x for x in mask), remote_sem=T.sem[sem],
                                 src=src, dst=dst)

    def beyond(s):
        to = cores[rest(s)[0]]
        there = [c for c in range(SIM) if topo.mates(topo.chip(c), topo.chip(to)) and topo.die(c) == topo.die(cores[s]) and topo.may_write(c, to)]
        able = [c for c in topo.cores_of(cores[s]) if c in cores and topo.may_write(c, there[0])]
        return there[able.index(cores[s])] if cores[s] in able else None

    def ways(s):
        return WAYS[0] if beyond(s) is None else WAYS[1 + s % 2]

    def dealt(s, k):
        w = ways(s)
        like = [j for call in CALLS[w] if k in call for j in call if (w[j] == "h") == (w[k] == "h")] or [k]
        return 8 // len(like) * like.index(k), 8 // len(like)

    if me is None:
        for s in range(N):
            for way, via in (("h", helper(s)), ("o", beyond(s))):
                ks = [k for k in range(4) if ways(s)[k] == way]
                if via == core and ks:
                    far = topo.engines(core, cores[rest(s)[0]])
                    for j, k in enumerate(ks):
                        c = NI + E * at(s, rest(s)[k])
                        g.wait_ge(T.sem["aR%d" % j], dealt(s, k)[1])
                        g.remote_dma_fused([write(cores[rest(s)[k]], far[j::len(ks)], "aC", raw(T.rlc[:, E * k:E * k + E]), raw(T.fw[:, c:c + E]))],
                                           local_sem=T.sem.lsent)
                    g.wait_ge(T.sem.lsent, len(far))
        return
    others = rest(me)
    OB = P * me
    q = {"v": g.vector, "a": g.scalar, "p": g.tensor, "g": g, "y": g.sync}
    csem = {"v": "vv", "a": "aa", "p": "pp", "g": "gq"}
    cnt = {"v": 0, "a": 0, "p": 0, "g": 0}
    known, wr, rd, pre = {}, {}, {}, {}

    def b(name, r0=0, r1=128, c0=0, c1=None):
        buf, a, w = POOL[name]
        return T[buf][r0:r1, a + c0:a + (w if c1 is None else c1)]

    def need(e, toks):
        best = {}
        for s, n in toks:
            best[s] = max(best.get(s, 0), n)
        for s in sorted(best):
            if known.get((e, s), 0) < best[s]:
                q[e].wait_ge(T.sem[s], best[s])
                known[(e, s)] = best[s]

    def op(e, fn, reads, writes, *args, **kw):
        toks = []
        for k in reads:
            toks += wr.get(k, [])
        for k in writes:
            toks += wr.get(k, []) + rd.get(k, [])
        need(e, toks)
        cnt[e] += 1
        fn(*args, **kw).then_inc(T.sem[csem[e]], 1)
        tok = (csem[e], cnt[e])
        for k in reads:
            rd.setdefault(k, []).append(tok)
        for k in writes:
            wr[k], rd[k] = [tok], []

    def dma(e, sem, total, reads, writes, out, in_):
        tok, toks = (sem, total), []
        for k in writes:
            if wr.get(k) != [tok]:
                pre[(sem, k)] = wr.get(k, []) + rd.get(k, [])
                wr[k], rd[k] = [tok], []
            toks += pre[(sem, k)]
        for k in reads:
            toks += wr.get(k, [])
        need(e, toks)
        q[e].dma_start(out, in_).then_inc(T.sem[sem], 16)
        for k in reads:
            rd.setdefault(k, []).append(tok)

    def copy(reads, writes, out, in_, e="v", plus=None):
        if e == "v" and plus is None:
            op("v", g.vector.tensor_copy, reads, writes, out, in_)
        elif e == "v":
            op("v", g.vector.tensor_scalar, reads, writes, out, in_, plus, None, A.add)
        elif plus is None:
            op("a", g.scalar.activation, reads, writes, out, in_, F.Copy)
        else:
            op("a", g.scalar.activation, reads, writes, out, in_, F.Identity, bias=plus)

    def tsc(reads, writes, out, in0, s1, op0, s2=None, op1=None):
        if op1 is None:
            op("v", g.vector.tensor_scalar, reads, writes, out, in0, s1, None, op0)
        else:
            op("v", g.vector.tensor_scalar, reads, writes, out, in0, s1, s2, op0, op1)

    def tt(reads, writes, out, in0, in1, o):
        op("v", g.vector.tensor_tensor, reads, writes, out, in0, in1, o)

    def tb(out, in0, in1, o):
        tt([in0, in1], [out], b(out), b(in0), b(in1), o)

    def sb(out, in0, s1, op0, s2=None, op1=None):
        tsc([in0], [out], b(out), b(in0), s1, op0, s2, op1)

    def line(out, in0, scale, bias):
        op("a", g.scalar.activation, [in0], [out], b(out), b(in0), F.Identity, bias=bias, scale=scale)

    def flip(reads, writes, out, in_):
        op("v", g.vector.transpose, reads, writes, out, in_)

    def fill(key, ap, c):
        op("v", g.vector.memset, [], [key], ap, c)

    def iota(key, out, pattern, base, mult, f=True):
        kw = {"allow_small_or_imprecise_dtypes": True} if f else {}
        op("g", g.iota, [], [key], out, pattern, base, mult, **kw)

    far = topo.engines(core, cores[others[0]])
    near = [x for x in topo.engines(core, cores[others[-1]]) if x not in far]
    sent = [0]

    def spread(sem, piece, to, masks):
        sent[0] += sum(len(m) for m in masks)
        g.remote_dma_fused([write(cores[d], m, sem, *piece(d)) for d, m in zip(to, masks)], local_sem=T.sem.lsent)

    def arrive(sem, key, sizes):
        wr[key] = [(sem, sum(sizes[at(me, s)] for s in others))]

    def lc(k):
        return 3 * k + (4 if k >= 4 else 0)

    def load_w(e, h):
        dma(e, "dw%d" % h, 16, [], ["wt%d" % h], T.wt[:, 2048 * h:2048 * h + 2048], T.w[:, 2048 * h:2048 * h + 2048])

    def pack(i0, i1):
        a, c = 128 * i0, 128 * i1
        op("v", g.vector.quantize_mx, ["wt0", "wt1"], ["wq%d" % i for i in range(i0, i1)], T.wq[:, a:c], T.wqs[:, a:c],
           T.wt[:, 4 * a:4 * c])

    quads = [(32 * a, 32 * a + 32) for a in range(4)]

    ns = 16 * 14
    dma("y", "dsrc", ns, [], ["src"], T.src[0:64, 0:4], T.alt[:, :])
    for c in range(4):
        dma("yaaa"[c], "dsrc", ns, [], ["src"], T.src[64:80, c:c + 1], T.f1[4 * c:4 * c + 4, :])
    dma("y", "dsrc", ns, [], ["src"], T.src[96:112, 0:4], T.f2[:, :])
    for c in range(4):
        x = c + 1 - 2 * (c % 2)
        dma("a", "dsrc", ns, [], ["src"], T.src[80:96, c:c + 1], T.f1[4 * x:4 * x + 4, :])
        dma("y", "dsrc", ns, [], ["src"], T.src[112 + 4 * c:116 + 4 * c, 0:4], T.f2[4 * x:4 * x + 4, :])
    for h in range(2):
        dma("y", "dcod", 96, [], ["cod"], T.src[16 * h:16 * h + 16, 8:24], T.alt[:, :])
        dma("y", "dcod", 96, [], ["cod"], T.src[16 * h:16 * h + 16, 4:8], T.f1[:, :])
        dma("y", "dcod", 96, [], ["cod"], T.src[16 * h:16 * h + 16, 24:28], T.f2[:, :])
    dma("y", "dcv", 32, [], ["cv.c"], T.cv[:, 0:4 * P], T.c[:, :])
    dma("y", "dcv", 32, [], ["cv.c"], T.cv[:, 4 * P:4 * IT], T.v[:, :])

    iota("pi", b("pi"), [[1, 1]], 0, 1, False)
    iota("ydf", b("ydf"), [[15, 4], [-15, 16]], 0, 0)
    iota("yid", b("yid"), [[1, 4], [16, 16]], 0, 0)
    iota("k4", b("k4"), [[1, 4]], NP + OB, 4)
    fill("xt", T.xt[64:128, 0:64], -float(TAG))
    fill("kk", b("kk"), 99.0)
    wr["kd"] = wr["kk"]
    fill("cv.z", T.cv[:, 4 * IT:4 * NI], 0.0)
    sb("p15", "pi", 0x4F, A.bitwise_and)
    sb("pl", "pi", 15, A.bitwise_and)
    sb("p16", "pi", 16, A.bitwise_and)
    sb("p5", "pi", 32, A.bitwise_and)
    sb("m14", "p15", float(AY), A.is_ge)
    sb("o4", "p16", 0.25, A.mult)
    sb("e14", "p15", float(AY), A.is_equal, float(TAG), A.mult)
    tsc(["m14"], ["ydf"], b("ydf", 0, 64), b("ydf", 0, 64), b("m14", 0, 64), A.mult)
    sb("c1", "p5", 4 * SI / 32.0, A.mult)
    sb("c2", "p5", -8 * SI / 32.0, A.mult, 4.0 * SI, A.add)
    tt(["ydf", "yid"], ["xt"], T.xt[0:64, 0:64], b("ydf", 0, 64), b("yid", 0, 64), A.add)
    steps = (64, 128, 256, 512, 1024)
    for n in steps:
        more = n // 16 if n < P else n // P * SI
        line("bc%d" % n, "m14", float(n - more), float(more))
    iota("idb", b("idb", 0, 32), [[16, 16]], SI * me, 1)
    iota("v1", T.v1[:, 0:V], [[1, 16], [16, 4]], TAG + P, 0)
    iota("dl", b("dl"), [[0, 2], [-2, 2], [0, 16]], 1, 0)
    iota("dd", b("dd"), [[16, 32]], 0, 1, False)
    iota("jm.0", T.jm[:, 0:16], [[1, 16]], 0, 0)
    iota("jm.1", T.jm[:, 16:80], [[0, N], [1, N]], 0, 0)

    def bits(key, r1, c0):
        x, k = T.src[0:r1, c0:c0 + 4], str(c0)
        tsc([key], ["b1" + k], b("b1", 0, r1, c0, c0 + 4), x, 0xF00, A.bitwise_and)
        tsc([key], ["b2" + k], b("b2", 0, r1, c0, c0 + 4), x, 4, A.arith_shift_right, 15, A.bitwise_and)
        tsc([key], ["b3" + k], b("b3", 0, r1, c0, c0 + 4), x, 15, A.bitwise_and)

    def sums(r1, c0):
        k = str(c0)
        tt(["b1" + k, "b2" + k], ["s1" + k], b("s1", 0, r1, c0, c0 + 4), b("b1", 0, r1, c0, c0 + 4), b("b2", 0, r1, c0, c0 + 4), A.add)
        tsc(["b3" + k], ["s3" + k], b("s3", 0, r1, c0, c0 + 4), b("b3", 0, r1, c0, c0 + 4), 16.0, A.mult)

    bits("src", 128, 0)
    sums(128, 0)
    for j in range(4):
        tsc(["s10", "s30", "k4"], ["sv"] if j == 3 else [], T.sv[:, j:j + 1], b("s1", 0, 128, j, j + 1), b("s3", 0, 128, j, j + 1), A.add,
            T.k4[:, j:j + 1], A.min)
    need("g", wr["sv"])
    spread("aL", lambda d: (T.sv[:, 0:4], T.lists[me]), others[0:4], parts(far, 2, 2, 2, 2))
    dma("y", "down", 16, ["sv"], ["lown"], T.lists[me], T.sv[:, 0:4])
    need("g", wr["lown"])
    spread("aL", lambda d: (T.lists[me], T.lists[me]), others[4:], parts(near, 1, 1, 1))

    for n in steps:
        copy(["xt", "bc%d" % n], ["xt"], T.xt[:, n:2 * n], T.xt[:, 0:n], "a", b("bc%d" % n))
        if n == 64:
            line("cap", "m14", -16.0 * TAG, 15.0 * TAG)
        if n == 128:
            wr["xb"] = wr["xt"]
            line("tag", "m14", -2.0 * TAG, 2.0 * TAG)
        if n == 256:
            copy(["tag", "e14"], ["tg0"], b("tg0"), b("e14"), "a", b("tag"))
    full = wr["xt"]
    tsc(["cod"], ["em"], b("em", 0, 32), T.src[0:32, 8:24], 0.0, A.is_lt, float(NO), A.mult)
    copy(["xb"], ["x1"], T.xt[:, NP:NP + 256], T.xt[:, 0:256], "v", float(NP))
    seed = wr["x1"]
    tt(["em", "idb"], ["idn"], b("idn", 0, 32), b("em", 0, 32), b("idb", 0, 32), A.max)
    copy([], ["x1"], T.xt[:, NP + 256:NP + 512], T.xt[:, NP:NP + 256], "a", 256.0)
    need("y", full + seed)
    for p in (0, 16, 48):
        dma("y", "dem", 48, ["idn"], ["xe"], T.xt[p:p + 1, OB:OB + P], T.idn[0:16, :])

    cuts = [k for k in range(N - 1) if k in (0, 4) or others[k] != others[k - 1] + 1] + [N - 1]
    kkeys = ["kk", "kd"]
    for k0, k1 in zip(cuts[:-1], cuts[1:]):
        wr["kd%d" % k0], wr["kk%d" % k0] = wr["kd"], wr["kk"]
        iota("kd%d" % k0, T.kk[:, 32 + lc(k0):32 + lc(k0) + 3 * (k1 - k0)], [[1, k1 - k0], [0, 3]], others[k0], 0)
        iota("kk%d" % k0, T.kk[:, lc(k0):lc(k0) + 3 * (k1 - k0)], [[0, k1 - k0], [16, 3]], 0, 0)
        kkeys += ["kd%d" % k0, "kk%d" % k0]
    iota("jm", T.jm[:, 80:144], [[1, N], [0, N]], 0, 0)
    iota("pf.z", T.pf[:, IT:SI], [[0, SI - IT]], 0, 0)
    iota("lo", b("lo", 0, 32), [[0, SI // 16], [1, 16]], 1, 0)
    iota("tab.z", T.tab[:, NO:NO + 16], [[0, 16]], IT // 2 + 4, 0)
    iota("tab%d" % me, T.tab[:, SI * me:SI * me + IT], [[16, IT // 16], [0, 16]], 0, 0)
    for s in others:
        iota("tab%d" % s, T.tab[:, SI * s:SI * s + IT], [[0, IT]], NI + E * at(s, me), 0)
    tabs = ["tab%d" % s for s in range(N)]

    tsc(["dl", "o4"], ["dl"], b("dl"), b("dl"), b("o4"), A.mult)
    tsc(["cap", "c1"], ["v1"], T.v1[:, 0:V], T.v1[:, 0:V], b("c1"), A.add, b("cap"), A.min)
    sb("p3", "pi", 3, A.bitwise_and)
    sb("row", "pl", 16.0, A.mult, float(OB), A.add)
    sb("p6", "pi", 64.0, A.is_ge, 4.0, A.mult)
    tt(["dl", "v1"], ["v1"], T.v1[:, 0:V], T.v1[:, 0:V], b("dl"), A.add)
    for nm in ("of1", "ofq", "ofz"):
        copy(["dd"], [nm], b(nm, 64, 128), b("dd", 64, 128, 0, POOL[nm][2]))
    tsc(["cod"], ["rk"], b("rk", 0, 32), T.src[0:32, 4:28], 8, A.arith_shift_right, 15, A.bitwise_and)
    bits("cod", 32, 4)
    copy(["v1"], ["v1"], T.v1[:, V:2 * V], T.v1[:, 0:V], "v", float(SI))
    sums(32, 4)
    tsc(["rk"], ["r1"], b("r1", 0, 32), b("rk", 0, 32, 0, 4), float(N), A.mult, 16.0, A.add)
    copy(["rk"], ["ow.c"], T.go[0:32, 20:36], b("rk", 0, 32, 4, 20))
    copy(["v1"], ["v1"], T.v1[:, 2 * V:4 * V], T.v1[:, 0:2 * V], "v", float(2 * SI))
    tt(["rk", "r1"], ["r2"], b("r2", 0, 32), b("rk", 0, 32, 20, 24), b("r1", 0, 32), A.add)
    tt(["s14", "s34"], ["sv.v"], T.sv[0:32, 4:8], b("s1", 0, 32, 4, 8), b("s3", 0, 32, 4, 8), A.add)
    copy(["v1", "c2"], ["v1"], T.v1[:, 4 * V:8 * V], T.v1[:, 0:4 * V], "v", b("c2"))
    tsc(["p5", "p6"], ["a4"], b("a4"), b("p5"), 0.25, A.mult, b("p6"), A.add)
    copy(["sv.v"], ["gl.v"], T.go[0:32, 16:20], T.sv[0:32, 4:8])
    copy(["r2"], ["ow.2"], T.go[0:32, 36:40], b("r2", 0, 32))
    copy(["jm.0", "row"], ["gl.c"], T.go[:, 0:16], T.jm[:, 0:16], "v", b("row"))
    op("v", g.vector.quantize_mx, ["cv.z", "cv.c"], ["qo"], b("qo"), b("qos"), b("cv"))
    gk = ["gl.c", "gl.v", "ow.c", "ow.2"]

    def onto(r0):
        copy(gk[0:4], ["go%d" % r0], T.go[r0:r0 + 32, 16:40], T.go[0:32, 16:40])

    flip(kkeys, ["kt"], b("kt"), b("kk"))
    onto(32)
    onto(64)
    dcol = T.kt[:, 32:33]
    tsc(["jm", "kt"], ["ne"], b("ne"), T.jm[:, 0:80], dcol, A.not_equal, BIG, A.mult)
    tsc(["jm", "kt"], ["n1"], b("n1"), T.jm[:, 80:144], dcol, A.not_equal)
    onto(96)
    tsc(["ne"], ["n2"], b("n2"), b("ne", 0, 128, 16, 80), 2 * TAG - 0.5, A.add)
    gk += ["go32", "go64", "go96"]

    arrive("aL", "lfar", [2, 2, 2, 2, 1, 1, 1])
    lk = ["lfar", "lown"]
    for r in range(4):
        dma("ya"[r % 2], "df1", 64, lk, ["f1f"], T.f1f[0:64, 4 * r:4 * r + 4], T.lists[r:N:4, 64:96, :])
    for h in range(4):
        p = 16 * h + AD
        need("ya"[h % 2], seed)
        dma("ya"[h % 2], "dfan", 64, lk, ["xt"], T.xt[p:p + 1, 0:NP], T.lists[:, 0:64, :])
    for h in range(2):
        p, w = 16 * h + AD, slice(96 + 16 * h, 112 + 16 * h)
        dma("a", "dv1", 96, lk, ["v1"], T.v1[p:p + 1, :], T.lists[:, w, :])
        for a in range(2):
            dma("y", "dv1", 96, lk, ["v1"], T.v1[32 + p:33 + p, HC * a:HC * a + HC], T.lists[4 - 4 * a:8 - 4 * a, w, :])
    copy([], ["x1"], T.xt[:, NP + 512:NP + 1024], T.xt[:, NP:NP + 512], "a", 512.0)
    need("y", wr["v1"])
    load_w("y", 0)
    load_w("y", 1)
    dma("y", "dlo", 16, ["lo"], ["pfown"], T.pfi[me], b("lo", 0, 1))

    X = ["xt", "xe", "x1", "x2"]
    copy(["f1f"], ["og"], b("of1", 0, 64, 0, 16), b("f1f", 0, 64))
    for a in range(2):
        copy(["f1f"], ["of1%d" % a], b("of1", 32 * a, 32 * a + 32, 16, 32), b("f1f", 32 - 32 * a, 64 - 32 * a))

    def step(keys, table, of, gm, tag):
        for h in range(2):
            copy(keys + [tag], [gm + "av"[h]], b(gm, 0, 128, 128 * h, 128 * h + 128), table.indirect(b(of, 0, 128, 8 * h, 8 * h + 8)),
                 "av"[h], b(tag))

    step(X[0:2] + ["of1", "og"], T.xt[:, 0:NP], "of1", "g0", "tg0")
    copy(["x1"], ["x2"], T.xt[:, NP + 1024:2 * NP], T.xt[:, NP:NP + 1024], "a", 1024.0)
    tt(["n1", "n2"], ["thr.2"], T.thr[:, 16:80], b("n1"), b("n2"), A.mult)
    flip(["g0a", "g0v"], ["tr"], T.tr[0:64, :], T.g0[0:64, :])
    copy(["of1", "og", "of10", "of11", "v1"], X[0:2], T.xt[:, 0:NP].indirect(b("of1")), b("v1"))
    copy(["tr"], ["ofq0"], b("ofq", 0, 64), T.tr[0:64, AD:HC:16])
    tsc(["tr"], ["d2"], b("d2", 0, 64), T.tr[0:64, AD:HC:16], float(NP), A.is_ge, float(NP), A.mult)
    step(X + ["ofq", "ofq0"], b("xt"), "ofq", "g1", "tag")
    tt(["tr", "d2"], ["t3"], b("t3", 0, 64), T.tr[0:64, AD:HC:16], b("d2", 0, 64), A.add)
    copy(["g1a", "g1v"], ["g0a", "g0v"], T.g0[64:128, :], T.g1[0:64, :], "a", 4.0 * TAG)
    flip(["g1a", "g1v"], ["tr1"], T.tr1[0:64, :], T.g1[0:64, :])
    copy(["t3"], ["of2a"], b("of2", 0, 64), b("t3", 0, 64))
    copy(["tr1"], ["of2b"], b("of2", 64, 128), T.tr1[0:64, AD:HC:16])
    copy(["tr1"], ["ofz0"], b("ofz", 0, 64, 0, 16), T.tr1[0:64, AD:HC:16])
    copy(["of2a", "of2b", "g0a", "g0v"], X, b("xt").indirect(b("of2")), b("g0"))
    copy(["ne"], ["thr.c"], T.thr[:, 0:16], b("ne", 0, 128, 0, 16), "a", TAG - 0.5)
    copy(["thr.c", "thr.2"] + gk, ["th"], b("th"), b("thr").indirect(T.go[:, 20:40]), "a")
    copy(["kt", "a4"], ["u0"], b("u0"), T.kt[:, 0:1], "a", b("a4"))
    op("a", g.scalar.activation, ["tag"], ["tag3"], b("tag3"), b("tag"), F.Identity, scale=4.0)
    op("a", g.scalar.activation, ["o4"], ["odd"], b("odd"), b("o4"), F.Identity, scale=NP / 4.0)
    copy(["jm", "u0"], ["u1"], b("u1"), T.jm[:, 0:4], "a", b("u0"))
    copy(["u1"], ["uu"], b("uu"), b("u1"), "a", 0.5)
    dma("y", "dfw", 32, ["qo"], ["fw.own"], T.fw[:, 0:NI].bitcast(dt.uint8), b("qo").bitcast(dt.uint8))
    dma("y", "dfw", 32, ["qo"], ["fw.own"], T.fws[:, 0:NI], b("qos"))

    for a in range(2):
        copy(["tr1"], ["ofz%d" % (a + 1)], b("ofz", 32 * a, 32 * a + 32, 16, 32), T.tr1[32 - 32 * a:64 - 32 * a, AD:HC:16])
    tt(X[0:2] + gk + ["th"], ["m2q"], b("m2q"), T.xt[:, 0:NP].indirect(T.go[:, 0:20]), b("th"), A.is_gt)
    copy(X + ["ofz", "ofz0", "ofz1", "ofz2", "tag3"], ["g2"], b("g2"), b("xt").indirect(b("ofz")), "a", b("tag3"))
    sb("bi", "p3", 2.0, A.is_lt, float(NC), A.mult)
    tt(["m2q"], ["mh"], b("mh", 0, 64), b("m2q", 0, 64), b("m2q", 64, 128), A.max)
    tt(["mh"], ["mk"], b("mk", 0, 32, 0, IT), b("mh", 0, 32), b("mh", 32, 64), A.max)
    for r0, r1 in quads:
        op("v", g.vector.tensor_tensor_scan, ["mk", "mk.z"], ["pf%d" % r0], T.pf[r0:r1, 0:NC], b("mk", 0, 32), b("mk", 0, 32), 0.0, A.add, A.max)
    dma("y", "dpf", 16, ["pf0", "pf.z"], ["pfo"], T.pfo[:], T.pf[0:LC:3, :])
    need("g", wr["pfo"])
    spread("aM", lambda d: (T.pfo[(lc(at(d, me)) + 2) // 3], T.pfi[me]), others, parts(far, 2, 2, 2, 2) + parts(near, 2, 2, 4))
    arrive("aM", "pffar", [2, 2, 2, 2, 2, 2, 4])
    copy(["g2"], ["g2.u"], T.g2[64:128, 0:128], T.g2[0:64, 128:256], "a")
    for a in range(4):
        o = 32 - 32 * (a % 2)
        copy(["g2"], ["g3.%d" % a], T.g3[32 * a:32 * a + 32, :], T.g2[o:o + 32, 256 + 128 * (a // 2):384 + 128 * (a // 2)], "a")
    pk = ["pf0", "pf32", "pf64", "pf96", "uu"]
    for c in range(2):
        op("a", g.scalar.activation, pk, ["ja%d" % c, "cnt%d" % c], T.ja[:, NC * c:NC * c + NC], T.pf[:, 0:NC], F.Sign,
           bias=b("uu", 0, 128, c, c + 1), scale=-1.0, accum_out=T.cnt[:, c:c + 1])
    g3k = ["g2", "g2.u", "g3.0", "g3.1", "g3.2", "g3.3"]
    tt(g3k, ["g4a"], b("g4", 0, 128, 0, 64), T.g2[:, 0:64], b("g3", 0, 128, 0, 64), A.max)
    for c in range(2):
        tsc(pk, ["jv%d" % c], T.jv[:, NC * c:NC * c + NC], T.pf[:, 0:NC], b("uu", 0, 128, 2 + c, 3 + c), A.is_lt, 2.0, A.mult)
    for c in range(2):
        w = slice(NC * c, NC * c + NC)
        op("v", g.vector.tensor_tensor_scan, ["jv%d" % c], ["jh%d" % c], T.jh[:, w], T.jv[:, w], T.jv[:, w], 0.0, A.add, A.max)
    tt(g3k, ["g4"], b("g4", 0, 128, 64, 128), T.g2[:, 64:128], b("g3", 0, 128, 64, 128), A.max)
    copy(["jh0", "jh1"], ["cnt2"], T.cnt[0:64, 2:4], T.jh[0:64, NC - 1:2 * NC:NC])
    copy(["jh0", "jh1"], ["cnt6"], T.cnt[0:64, 6:8], T.jh[64:128, NC - 1:2 * NC:NC])
    ck = ["cnt0", "cnt1", "cnt2", "cnt6"]
    copy(ck[0:2], ["cnt4"], T.cnt[0:64, 4:6], T.cnt[64:128, 0:2])
    flip(["g4a", "g4"], ["tr2"], b("tr2"), b("g4"))
    copy(ck + ["cnt4"], ["cnt8"], T.cnt[0:32, 8:16], T.cnt[32:64, 0:8])
    copy(ck + ["cnt4"], ["cnt16"], T.cnt[0:32, 16:24], T.cnt[0:32, 0:8])
    copy(ck + ["cnt4"], ["cnt24"], T.cnt[0:32, 24:32], T.cnt[32:64, 0:8])
    tsc(["tr2"], ["m3"], b("m3"), T.tr2[:, AY:128:16], float(TAG), A.is_ge, BIG, A.mult)
    tsc(["tr2"], ["c3"], b("c3"), T.tr2[:, AY:128:16], -float(TAG), A.add)
    flip(ck + ["cnt4", "cnt8", "cnt16", "cnt24"], ["ct"], T.ct[0:32, :], T.cnt[0:32, :])
    tt(["tr2", "m3"], ["b4"], b("b4"), T.tr2[:, AD:128:16], b("m3"), A.subtract)
    pm = ["pm%d" % r0 for r0, r1 in quads]
    for r0, r1 in quads:
        tsc(["ct", "bi"], ["pm%d" % r0], T.pm[r0:r1, :], T.ct[0:32, 0:MC], b("bi", 0, 32), A.add, 0.5, A.mult)
    tb("p4", "b4", "c3", A.max)

    def piece(src, dst, d):
        a, c = 16 * lc(at(d, me)), NI + E * at(me, d)
        return T[src][:, a:a + E], T[dst][:, c:c + E]

    def pick(k0, k1, e):
        of, w = T.pm[:, lc(k0):lc(k1 - 1) + 3], slice(16 * lc(k0), 16 * lc(k1 - 1) + E)
        if e == "v":
            copy(["qo"] + pm, ["sn%d" % k0], T.sn[:, w].bitcast(dt.uint32), b("qo").bitcast(dt.uint32).indirect(of))
        else:
            copy(["qo"] + pm, ["sns%d" % k0], T.sns[:, w], b("qos").indirect(of), "a")

    def codes(d):
        return [raw(x) for x in piece("sn", "fw", d)]

    for p in range(0, 128, 16):
        dma("yyaa"[p // 32], "dtab", 128, ["pffar", "pfown"], tabs, T.tab[p:p + 1, 0:NO], T.pfi[:])
    pick(0, 2, "v")
    tsc(["p4", "odd"], ["ofw"], b("ofw"), b("p4"), b("odd"), A.add)
    pick(2, 4, "v")
    for k0, k1 in ((0, 2), (2, 4), (4, N - 1)):
        pick(k0, k1, "a")
    copy(["ofw", "g4a", "g4"], X, b("xt").indirect(b("ofw")), b("g4"))
    pick(4, N - 1, "v")
    need("g", wr["sn0"])

    way, via = ways(me), {"h": helper(me), "o": beyond(me)}
    for call in CALLS[way]:
        need("g", wr["sn2"] if call[-1] >= 2 else [])
        ts = []
        for k in call:
            a, n = dealt(me, k)
            mask = (near if way[k] == "h" else far)[a:a + n]
            sent[0] += n
            if way[k] == "d":
                ts.append(write(cores[others[k]], mask, "aC", *codes(others[k])))
            else:
                w = slice(E * k, E * k + E)
                ts.append(write(via[way[k]], mask, "aR%d" % way[0:k].count(way[k]), raw(T.sn[:, w]), raw(T.rlc[:, w])))
        g.remote_dma_fused(ts, local_sem=T.sem.lsent)
    need("g", wr["sns4"])
    spread("aS", lambda d: piece("sns", "fws", d), others, parts(far, 2, 2, 2, 2) + parts(near, 4, 2, 2))
    need("g", wr["sn4"])
    late = [k for k in range(4) if not any(k in call for call in CALLS[way])]
    spread("aC", codes, [others[k] for k in late] + others[4:], [far for k in late] + parts(near, 2, 2, 4))
    mine = [(s, at(me, s), ways(s)[at(me, s)]) for s in others[0:4]]
    wr["fw.far"] = [("aC", sum(dealt(s, k)[1] if w == "d" else len(far) // ways(s).count(w) for s, k, w in mine) +
                     sum([2, 2, 4][at(me, s) - 4] for s in others[4:]))]
    arrive("aS", "fws.far", [2, 2, 2, 2, 4, 2, 2])

    for e, c0, c1 in (("a", 0, 12), ("v", 12, 16)):
        copy(X[0:2] + gk, ["x3" + e], b("x3", 0, 128, 16 * c0, 16 * c1), T.xt[:, 0:NP].indirect(T.go[:, c0:c1]), e)
    pack(0, 1)
    flip(["x3a", "x3v"], ["x3t"], b("x3t"), b("x3"))
    pack(1, 2)
    lo_, hi_ = T.x3t[0:32, 16:P:32], T.x3t[32:64, 16:P:32]
    tt(["x3t"], ["hk"], b("hk", 0, 64), T.x3t[0:64, 0:P:16], T.x3t[64:128, 0:P:16], A.max)
    tt(["x3t"], ["idi0"], b("idi", 0, 32), lo_, hi_, A.min)
    tt(["x3t"], ["idi1"], b("idi", 32, 64), lo_, hi_, A.max)
    hk = POOL["hk"][1]
    for t in (2, 3):
        w = slice(hk + 3 - t, hk + 16, 2)
        tt(["hk"], ["idi%d" % t], b("idi", 32 * t, 32 * t + 32), T.tf[0:32, w], T.tf[32:64, w], A.max)
    tsc(["idi%d" % t for t in range(R)], ["idj"], b("idj"), b("idi"), TAG - 1, A.bitwise_and)
    pack(2, 3)
    for h in range(2):
        copy(["idj"], ["idu%d" % h], T.idu[:, h:16:2], b("idj"))
    pack(3, 4)
    for h in range(2):
        copy(tabs + ["tab.z", "idu0", "idu1"], ["gs%d" % h], b("gs", 0, 128, 128 * h, 128 * h + 128),
             b("tab").indirect(T.idu[:, 8 * h:8 * h + 8]), "av"[h])
    pack(4, 5)
    flip(["gs0", "gs1"], ["gt"], b("gt"), b("gs"))
    pack(5, 6)
    for t, (r0, r1) in enumerate(quads):
        tt(["gt"], ["ga%d" % t], b("ga", 0, 32, 16 * t, 16 * t + 16), T.gt[r0:r1, 0:P:16], T.gt[r0:r1, 1:P:16], A.add)
    pack(6, 7)
    for r0, r1 in quads:
        tsc(["ga%d" % t for t in range(R)], ["so%d" % r0], T.so[r0:r1, :], b("ga", 0, 32), -1.0, A.add)
    pack(7, 8)

    def products(t):
        pk, ps, of = "pk%d" % t, "ps%d" % t, T.so[:, 16 * t:16 * t + 16]
        sk = ["so%d" % r0 for r0, r1 in quads]
        copy(["fw.own", "fw.far"] + sk, [pk], b(pk).bitcast(dt.uint32), b("fw").bitcast(dt.uint32).indirect(of))
        copy(["fw.own", "fws.far"] + sk, [ps], b(ps), b("fws").indirect(of), "a")
        for i, c0, c1, bank in PARTS:
            if i // O == t:
                w = slice(128 * i, 128 * i + 128)
                op("p", g.tensor.matmul_mx, ["wq%d" % i, pk, ps], ["acc%d" % bank], T.acc[:, 512 * bank:512 * bank + c1 - c0],
                   T.wq[:, w], T.wqs[:, w], b(pk, 0, 128, c0, c1), b(ps, 0, 128, c0, c1), True, True)

    def out(k, e):
        tile, c0, c1, bank = PARTS[k]
        copy(["acc%d" % bank], ["ys%d" % k], T.ys[:, P * tile + c0:P * tile + c1], T.acc[:, 512 * bank:512 * bank + c1 - c0], e)
        if k in STORES:
            i0, i1 = STORES[k]
            w = slice(P * i0, P * i1)
            dma("y", "dy", NS, ["ys%d" % j for j in range(len(PARTS)) if i0 <= PARTS[j][0] < i1], ["y%d" % k], T.y[:, w], T.ys[:, w])

    NS = 16 * len(STORES)
    left = [0]
    for t in range(R):
        products(t)
        for e in LEAVE[t]:
            out(left[0], e)
            left[0] += 1
    need("y", [("dy", NS)])
    need("g", [("lsent", sent[0])])
